import numpy as np, ml_dtypes
CORES = [2,3,42,43,82,83,122,123]
N = 8
BF = ml_dtypes.bfloat16
C, I, P, T, ST = 4096, 128, 1024, 4, 3
SX, SP = 32, 8
def parts(rng):
    return rng.integers(0, 256, (N, 8, C, 16)), rng.integers(0, 4096, (N, 8, I, 16)), rng.integers(0, 4096, (N, 8, P, 16)), rng.integers(1, 256, (N, 8, 16))
def turn(a):
    return np.ascontiguousarray(np.swapaxes(a, 2, 3)).reshape(N, 128, -1)
def pack(x, w, p, t):
    return {"xt": turn(x).astype(np.float32).astype(BF), "wd": turn(w).astype(np.int32), "pd": turn(p).astype(np.int32), "wt": np.reshape(t, (N, 128, 1)).astype(np.int32)}
def place(a, b, s):
    return ((a * b >> 5) + 37 * a + b + s) & (C - 1)
def setup_inputs(rng):
    x, w, p, t = parts(rng)
    return pack(x, w, p, t)
def setup_inputs_spread(rng):
    x, w, p, t = parts(rng)
    s = rng.choice(np.array([0.0, 0.25, 0.5, 1.0]), (N, 8, 1, 1))
    x = (x * np.exp2(-8 * s * rng.random((N, 8, C, 1)))).astype(np.int64)
    w = np.where(rng.random((N, 8, I, 1)) < 0.5, np.exp2(12 * rng.random(w.shape)).astype(np.int64) - 1, w)
    p = np.where(rng.random((N, 8, P, 1)) < 0.5, np.exp2(12 * rng.random(p.shape)).astype(np.int64) - 1, p)
    t = np.minimum(np.exp2(8 * rng.random(t.shape)).astype(np.int64), 255)
    return pack(x, np.minimum(w, 4095), np.minimum(p, 4095), t)
def setup_inputs_ends(rng):
    x, w, p, t = parts(rng); m = np.arange(16); s = np.arange(32)
    x = np.where(x < 128, 0, 255); x = np.where(rng.random(x.shape) < 0.1, np.abs(x - 1), x)
    x[:, :, (s - 1) & (C - 1)] = 0; x[:, :, (s + 37 * 4095) & (C - 1)] = 255
    w = np.where(rng.random((N, 8, I, 1)) < 0.75, 4095 * rng.integers(0, 2, w.shape), w)
    kind = rng.integers(0, 4, (N, 8, P, 1))
    p = np.where(kind == 0, 0, np.where(kind == 1, 4095, np.where(kind == 2, 4095 * rng.integers(0, 2, p.shape), p)))
    v = rng.integers(64, 2000, (N, 8))
    w[:, :, I - 1] = 0; w[:, :, I - 1, 14] = v; w[:, :, I - 1, 15] = 4095
    w[:, :, I - 2] = 4095; w[:, :, I - 2, 0] = 0; w[:, :, I - 2, 1] = v
    w[:, :, 0] = 0; w[:, :, 0, 15] = 4095; w[:, :, 1] = 4095 * (m % 2)
    p[:, :, 0] = 4095; p[:, 1::2, 0, 15] = 0
    t = np.where(t < 128, 1, 255); t[:, 0] = 1; t[:, 7] = 255
    return pack(x, w, p, t)
def setup_inputs_corners(rng):
    x, w, p, t = parts(rng); m = np.arange(16)
    kw = rng.integers(0, 6, (N, 8, I, 1)); z = rng.integers(0, 16, (N, 8, I, 1)); one = w[..., :1]
    w = np.where(kw == 0, one, np.where(kw == 1, w[..., m % 2], np.where(kw == 2, (one & 1023) + 1024 * (w & 3), np.where(kw == 3, np.where(m == z, w[..., 1:2], one), np.where(kw == 4, w[..., m % 8], w)))))
    kp = rng.integers(0, 4, (N, 8, P, 1))
    p = np.where(kp == 0, p[..., :1], np.where(kp == 1, p[..., m % 4], np.where(kp == 2, 4095 * (p & 1), p)))
    p[:, 1::2, ::SP] = w[:, 1::2]
    x[:, 0::4] = x[:, 0::4] & 1; x[:, 1::4] = x[:, 1::4][:, :, (np.arange(C) >> 2) & 7]; x[:, 2::4] = 255 * (x[:, 2::4] & 1)
    t[:, 0] = 1; t[:, 1] = 255; t[:, 2] = np.where(m == 15, 255, 1); t[:, 3] = np.where(m == 0, 1, 255)
    return pack(x, w, p, t)
def setup_inputs_crowd(rng):
    x, w, p, t = parts(rng); g1 = int(rng.integers(0, 8))
    for q in (0, 1, N - 1):
        for g in range(8):
            but = (g == g1) if q == 1 else (q > 1 and rng.random() < 0.5)
            base = rng.integers(0, 256, 16); x[q, g] = base
            if but:
                a = w[q, g]; b = np.roll(a, -1, axis=1)
                n = np.bincount(np.concatenate([place(a, b, 0).ravel(), place(b, a, 0).ravel()]), minlength=C)
                x[q, g, int(rng.choice(np.flatnonzero(n == 1)))] = 255 - base
    al = np.argsort(rng.random((8, 4096)), axis=1)[:, :4]
    a = np.take_along_axis(al, rng.integers(0, 4, (8, I)), 1)[:, :, None]; b = (a + rng.integers(1, C // 4, (8, I, 1))) & 4095
    w[2] = np.where(np.arange(16) == rng.integers(0, 16, (8, I, 1)), b, a)
    p[2, :, :, :4] = al[:, None, :]; p[2] = np.take_along_axis(p[2], np.argsort(rng.random((8, P, 16)), axis=2), 2)
    return pack(x, w, p, t)
def setup_inputs_brink(rng):
    x, w, p, t = parts(rng); m = np.arange(16)
    for q in range(N):
        for g in range(8):
            s = 1 + rng.permutation(36)
            cut = np.zeros(36, np.int64); cut[8:12] = 1
            if g % 2 == 0:
                cut[12:] = rng.integers(2, 256, 24); cut[35] = 255
            else:
                cut[12:24] = 2040; cut[24:] = 2041
            o = np.argsort(rng.random((36, 16)), axis=1)
            far = 255 - np.clip(cut[:, None] - 255 * o, 0, 255)
            lo = (255 - far) * rng.integers(0, 2, (36, 16)); up = rng.random((36, 16)) < 0.5
            x[q, g, s] = np.where(up, lo + far, lo); x[q, g, 37 * s] = np.where(up, lo, lo + far)
            p[q, g] = s[rng.integers(0, np.where(rng.random((P, 1)) < 0.5, 24, 36), (P, 16))]
            z1 = rng.integers(1, 7, (I, 1)); z2 = z1 + 2 + rng.integers(0, 8, (I, 1))
            v = np.where(m == z1, s[rng.integers(8, 12, (I, 1))], np.where(m == z2, s[rng.integers(0, 8, (I, 1))], 0))
            w[q, g] = np.where(rng.random((I, 1)) < 0.75, v, w[q, g])
    return pack(x, w, p, t)
def check_inputs(d):
    bad = []
    for k, lo, hi in (("xt", 0, 255), ("wd", 0, 4095), ("pd", 0, 4095), ("wt", 1, 255)):
        a = np.asarray(d[k]).astype(np.float64)
        if not (np.all(a >= lo) and np.all(a <= hi) and np.all(a == np.floor(a))): bad.append("range of " + k)
    return bad
def reference(xt, wd, pd, wt):
    x = np.ascontiguousarray(np.swapaxes(xt.astype(np.float32).astype(np.int32).reshape(N, 8, 16, C), 2, 3))
    w = np.ascontiguousarray(np.swapaxes(wd.astype(np.int64).reshape(N, 8, 16, I), 2, 3))
    p = np.ascontiguousarray(np.swapaxes(pd.astype(np.int64).reshape(N, 8, 16, P), 2, 3))
    wts = wt.astype(np.int64).reshape(N, 8, 1, 16)
    gi = np.arange(8)[:, None]; ti = np.arange(I)[None, :]; g3 = np.arange(8)[:, None, None]
    A = np.zeros(N, np.int64)
    for t in range(T):
        A2 = np.zeros(N, np.int64)
        for r in range(N):
            q = (r + ST * t) % N
            v = w[r].copy(); v1 = np.roll(v, -1, axis=2)
            f = x[q][g3, place(v, v1, A[q])]; h = x[q][g3, place(v1, v, A[q])]
            e = np.add.reduce(np.abs(f - h), axis=3)
            k = np.argmax(e, axis=2); kn = (k + 1) & 15
            c = np.where(e[gi, ti, (k - 1) & 15] >= e[gi, ti, kn], k, kn)
            u = np.add.reduce(wts[q] * f[gi, ti, k], axis=2)
            b = p[q][gi, u & (P - 1)]
            before = v[gi, ti, (c - 1) & 15][:, :, None]; after = v[gi, ti, (c + 1) & 15][:, :, None]
            y = x[q][g3, place(before, b, A[q])]; z = x[q][g3, place(b, after, A[q])]
            E = np.add.reduce(np.abs(y - z), axis=3)
            j = np.argmin(E, axis=2)
            good = 2 * E[gi, ti, j] < e[gi, ti, k]
            mend = v.copy(); mend[gi, ti, c] = b[gi, ti, j]
            swap = v.copy(); swap[gi, ti, k] = v[gi, ti, kn]; swap[gi, ti, kn] = v[gi, ti, k]
            new = np.where(good[:, :, None], mend, swap)
            gg, ii = np.nonzero(good)
            p[q, gg, SP * ii + (u[gg, ii] & (SP - 1))] = new[gg, ii]
            x[q, gi, SX * ti + (u & (SX - 1))] = (y[gi, ti, j] + z[gi, ti, j]) >> 1
            w[r] = new; A2[q] = (8 * I - len(gg)) & 31
        A = A2
    return {"yw": turn(w).astype(np.float32), "yp": turn(p).astype(np.float32), "yx": turn(x).astype(np.float32).astype(BF)}

@@ -1,0 +1,535 @@
+import numpy as np
+from concourse.mybir import AluOpType, AxisListType, ActivationFunctionType
+
+Op = AluOpType
+AF = ActivationFunctionType
+NV, STEP, H = 4, 3, 2
+GAM = 1.6
+CH1 = [[16] * 4, [16] * 4]
+CH2 = [[32] * 2, [16] * 4]
+TRIES = 3000
+SEED = 1
+BIG = float(2 ** 24)
+LAND = "la lb lc ld le".split()
+EXT = {"xt": [128, 4096], "wd": [128, 128], "pd": [128, 1024], "wt": [128, 1],
+       "yw": [128, 128], "yp": [128, 1024], "yx": [128, 4096]}
+SCRATCH = {}
+PK = {}
+
+
+def bufs(where, dtype, shape, names, pack=None, halves=False):
+    for n in names.split():
+        for m in ([n + "0", n + "1"] if halves else [n]):
+            if pack is None:
+                SCRATCH[m] = (where, shape, dtype)
+            else:
+                o = SCRATCH[pack][1][1] if pack in SCRATCH else 0
+                PK[m] = (pack, o, shape[1])
+                SCRATCH[pack] = (where, [128, o + (shape[1] + 15) // 16 * 16], dtype)
+
+
+bufs("sbuf", "bfloat16", [128, 4096], "rec")
+bufs("sbuf", "float32", [128, 2048], "stock")
+bufs("sbuf", "int32", [128, 1024], "pdi")
+bufs("sbuf", "int32", [128, 128], "wdi")
+bufs("sbuf", "int32", [128, 1], "wti")
+bufs("sbuf", "bfloat16", [128, 2048], "K1 K2 KU")
+bufs("sbuf", "bfloat16", [128, 1024], "ohJ")
+bufs("sbuf", "bfloat16", [128, 64], "Tg Tx")
+bufs("sbuf", "float16", [128, 4, 16], "CK1 CK2")
+bufs("sbuf", "float32", [128, 4, 16], "CKc")
+bufs("sbuf", "int32", [128, 4, 16], "CKi CKj")
+bufs("sbuf", "int32", [128, 128], "cD cM cK cT1 cT2 cT3 tabi tabj", "PI")
+bufs("sbuf", "int32", [128, 64], "oji ojk", "PI")
+bufs("sbuf", "int32", [128, 8], "RC Gi Ga", "PI")
+bufs("sbuf", "float32", [128, 1], "wcol Gs A32", "PF")
+bufs("sbuf", "float32", [128, 128], "ISh I32", "PF")
+bufs("sbuf", "float32", [128, 64], "SM2", "PF")
+bufs("sbuf", "float16", [128, 128], "BO mI nI mS mP tA tB I3 I2 S3 S2 BO3 BO2 onh", "PH")
+bufs("sbuf", "float16", [128, 256], "CA", "PH")
+bufs("sbuf", "bfloat16", [128, 128], "BOm on16 tabe", "PB")
+bufs("sbuf", "float16", [128, 64], "la lb lc ld le snd", halves=True)
+bufs("sbuf", "float16", [128, 64], "bj", "PH", True)
+bufs("sbuf", "float16", [128, 128], "pr", "PH", True)
+bufs("sbuf", "float32", [128, 64], "M B dl Y", "PF", True)
+bufs("sbuf", "float32", [128, 128], "X", "PF", True)
+bufs("sbuf", "float32", [128, 4], "tf", "PF", True)
+bufs("sbuf", "float32", [128, 64], "yo", halves=True)
+bufs("sbuf", "int32", [128, 128], "Xi Xs", "PI", True)
+bufs("sbuf", "int32", [128, 64], "hd Ms m2", "PI", True)
+bufs("sbuf", "int32", [128, 16], "cc c2 ui uq sb rs FI", "PI", True)
+bufs("sbuf", "uint16", [128, 128], "lu", "PU", True)
+bufs("sbuf", "uint16", [128, 16], "cu uu FU", "PU", True)
+bufs("sbuf", "bfloat16", [128, 128], "mk", "PB", True)
+bufs("sbuf", "bfloat16", [128, 64], "mx gp nr fk", "PB", True)
+bufs("sbuf", "bfloat16", [128, 4], "ng", "PB", True)
+bufs("sbuf", "bfloat16", [128, 4, 256], "ab", halves=True)
+bufs("sbuf", "bfloat16", [128, 1024], "f e y d", halves=True)
+bufs("sbuf", "float32", [128, 4, 16], "pv cb", halves=True)
+bufs("sbuf", "float32", [128, 512], "po", halves=True)
+bufs("psum", "float32", [128, 512], "pA pW", halves=True)
+bufs("psum", "float32", [128, 4, 128], "pE", halves=True)
+A_ = slice(None)
+
+
+def c(a, b, st=1):
+    return slice(a, b, st)
+
+
+def shift(name, s):
+    o, w = PK[name][1:]
+    a, b, st = s.indices(w)
+    return slice(o + a, o + b, st)
+
+
+def r(name, *ix, ind=None):
+    if ind is not None:
+        ind = (PK[ind[0]][0], shift(ind[0], ind[1]))
+    if name in PK:
+        return ("ref", PK[name][0], (shift(name, ix[0] if ix else A_),), ind)
+    return ("ref", name, ix, ind)
+
+
+def isref(x):
+    return isinstance(x, tuple) and len(x) == 4 and x[0] == "ref"
+
+
+def span(name, ix):
+    shape = (SCRATCH[name][1] if name in SCRATCH else EXT[name])[1:]
+    lo = hi = 0
+    stride = 1
+    for k in range(len(shape) - 1, -1, -1):
+        s = ix[k] if k < len(ix) else A_
+        if isinstance(s, int):
+            a = b = s
+        else:
+            a, b, st = s.indices(shape[k])
+            b = a + (b - 1 - a) // st * st
+        lo += a * stride
+        hi += b * stride
+        stride *= shape[k]
+    return lo, hi + 1
+
+
+def ap(T, ref):
+    x = T[ref[1]][(A_,) + tuple(ref[2])]
+    return x if ref[3] is None else x.indirect(T[ref[3][0]][:, ref[3][1]])
+
+
+NODES = []
+ACC = {}
+HALF = [""]
+
+
+def add(eng, dur, calls, kind="comp", tag="", extra=(), pre=()):
+    n = len(NODES)
+    preds = set(pre)
+    touch = list(extra)
+    for m, kw in calls:
+        for k, v in kw.items():
+            if isref(v):
+                touch.append((v[1],) + span(v[1], v[2]) + (k == "out",))
+                if v[3] is not None:
+                    touch.append((v[3][0],) + span(v[3][0], (v[3][1],)) + (False,))
+    for name, lo, hi, w in touch:
+        psum = name in SCRATCH and SCRATCH[name][0] == "psum"
+        keep = []
+        for q in ACC.setdefault(name, []):
+            m, me, a, b, mw = q
+            if m != n and psum and me != eng:
+                preds.add(m)
+                keep.append(q)
+                continue
+            if m != n and a < hi and lo < b and (w or mw):
+                preds.add(m)
+                if w and lo <= a and b <= hi:
+                    continue
+            keep.append(q)
+        keep.append((n, eng, lo, hi, w))
+        ACC[name] = keep
+    NODES.append({"eng": eng, "dur": dur, "calls": calls, "kind": kind, "tag": tag, "preds": sorted(preds), "key": tag + HALF[0]})
+    return n
+
+
+def V(n, meth, tag="", **kw):
+    return add("V", 25 + 1.0 * max(n, 64), [(meth, kw)], tag=tag)
+
+
+def S(n, calls, tag=""):
+    return add("S", sum(35 + 1.0 * max(k, 64) for k in n), [("activation", kw) for kw in calls], tag=tag)
+
+
+def SG(out, win, lst, n, tag):
+    return add("S", 70 + GAM * n, [("activation", dict(out=out, in_=r(win[0], *win[1:], ind=lst), func=AF.Copy))], tag=tag)
+
+
+def P(calls, tag="", slow=0):
+    return add("P", 60 + 40 * len(calls) + slow, [("matmul", kw) for kw in calls], tag=tag)
+
+
+def I(out, pattern, base, cm, n, **kw):
+    return add("G", 130 + 1.7 * n, [("iota", dict(out=out, pattern=pattern, base=base, channel_multiplier=cm, **kw))], tag="set")
+
+
+def mm(out, lhsT, rhs, start=True, stop=True):
+    return dict(out=out, lhsT=lhsT, rhs=rhs, start=start, stop=stop)
+
+
+def ts(out, in0, s1, op0, s2=None, op1=None, n=64, tag="set"):
+    kw = {} if op1 is None else {"op1": op1}
+    return V(n, "tensor_scalar", tag, out=out, in0=in0, scalar1=s1, scalar2=s2, op0=op0, **kw)
+
+
+def tt(out, a, b, op, n=64, tag="set"):
+    return V(n, "tensor_tensor", tag, out=out, in0=a, in1=b, op=op)
+
+
+def cp(out, in_, n=64, tag="set"):
+    return V(n, "tensor_copy", tag, out=out, in_=in_)
+
+
+def ms(out, v, n=64):
+    return V(n, "memset", "set", out=out, value=v)
+
+
+def scan(out, data1, tag):
+    return V(64, "tensor_tensor_scan", tag, out=out, data0=r("SM2"), data1=data1, initial=BIG, op0=Op.add, op1=Op.min)
+
+
+def dma(q, out, in_, dur, tag):
+    return add(q, dur, [("dma_start", dict(out=out, in_=in_))], kind="dma", tag=tag)
+
+
+def sums(out, K, src, first):
+    return [mm(out, r("mI"), r(first), True, False)] + [
+        mm(out, r(K, c(128 * k, 128 * k + 128)), r(src, A_, c(16 * k, 16 * k + 16)), False, k == 15) for k in range(16)]
+
+
+def gathers(h, a, b, ta, tb, chunks):
+    o = 0
+    for w in chunks:
+        k, e = c(16 * o, 16 * o + 16 * w), o + w
+        SG(r(a + h, k), ("rec",), ("lu" + h, c(o, e)), 16 * w, ta)
+        V(16 * w * GAM, "tensor_tensor", tb, out=r(b + h, k), in0=r("rec", ind=("lu" + h, c(64 + o, 64 + e))), in1=r(a + h, k), op=Op.subtract)
+        S([16 * w], [dict(out=r("ab" + h, c(o // 16, e // 16), A_), in_=r(b + h, k), func=AF.Abs)], "ab" + tb)
+        o = e
+
+
+def build():
+    AND, SAR, SLR = Op.bitwise_and, Op.arith_shift_right, Op.logical_shift_right
+    dma("Y", r("wdi"), r("wd"), 2000, "load")
+    dma("S", r("wti"), r("wt"), 2000, "load")
+    dma("Y", r("rec", c(0, 2048)), r("xt", c(0, 2048)), 4500, "load")
+    dma("S", r("rec", c(2048, 4096)), r("xt", c(2048, 4096)), 4500, "load")
+    dma("Y", r("pdi"), r("pd"), 4500, "load")
+    I(r("cD"), [[1, 128]], 0, -1, 128)
+    I(r("cM"), [[1, 128]], 0, 0, 128)
+    I(r("cK"), [[0, 128]], 0, 1, 128)
+    ts(r("cT3"), r("cD"), 15, AND, n=128)
+    ts(r("cT1"), r("cM"), 4, SLR, n=128)
+    ts(r("cT2"), r("cK"), 4, SLR, n=128)
+    tt(r("BO"), r("cT1"), r("cT2"), Op.is_equal, n=256)
+    ts(r("mI"), r("cD"), 0, Op.is_equal, n=128)
+    ts(r("tA"), r("cT3"), 15, Op.is_equal, n=128)
+    tt(r("mS"), r("tA"), r("BO"), Op.mult, n=256)
+    for o, i, k in (("I3", "mI", 3232.0), ("I2", "mI", 2080.0), ("S3", "mS", 3232.0), ("S2", "mS", 2080.0), ("nI", "mI", -1.0),
+                    ("BO3", "BO", 3232.0), ("BO2", "BO", 2080.0), ("BOm", "BO", -4096.0)):
+        ts(r(o), r(i), k, Op.mult)
+    for h in "01":
+        ts(r("la" + h), r("wdi", c(64 * int(h), 64 * int(h) + 64)), -2048.0, Op.add)
+    ms(r("K1"), 0.0, 1024)
+    for g in range(8):
+        cp(r("K1", c(16 * g, 16 * g + 1936, 129)), r("BOm", c(16 * g, 16 * g + 16)))
+    ts(r("wcol"), r("wti"), -1.0 / 2048, Op.mult)
+    ts(r("KU"), r("K1"), r("wcol"), Op.mult, n=1024)
+    S([2048], [dict(out=r("K2"), in_=r("K1"), func=AF.Copy, scale=-1.0)], "set")
+    cp(r("I32"), r("mI"), n=128)
+    ts(r("tB"), r("cT3"), 1, Op.is_equal, n=128)
+    tt(r("mP"), r("tB"), r("BO"), Op.mult, n=256)
+    tt(r("ISh"), r("mI"), r("mP"), Op.subtract, n=256)
+    ms(r("on16"), 1.0)
+    ms(r("onh"), 1.0)
+    ms(r("CA", c(0, 64)), 2080.0)
+    ms(r("CA", c(64, 128)), 3232.0)
+    ms(r("CA", c(128, 256)), 0.0)
+    I(r("CKi"), [[0, 4], [1, 16]], 0, 16, 64)
+    I(r("CKc"), [[256, 4], [0, 16]], 0, 0, 64, allow_small_or_imprecise_dtypes=True)
+    ts(r("CKj"), r("CKi"), 255, AND)
+    tt(r("CK2"), r("CKj"), r("CKc"), Op.add, n=128)
+    ts(r("CK1"), r("CK2"), 2.0, Op.mult)
+    ts(r("RC", c(0, 4)), r("CK2", A_, 0), 2.0, Op.mult)
+    ts(r("RC", c(4, 8)), r("CK2", A_, 0), 1.0, Op.mult)
+    ms(r("SM2"), 0.0)
+    ms(r("SM2", c(0, 64, 16)), BIG)
+    I(r("tabi", c(0, 96)), [[1, 3], [1, 16], [1, 2]], -1, -1, 96)
+    I(r("tabi", c(96, 128)), [[1, 16], [0, 2]], 0, -1, 32)
+    ts(r("tabj"), r("tabi"), 15, AND, n=128)
+    ts(r("tabe"), r("tabj"), 0, Op.is_equal, n=128)
+    ms(r("Tg"), 0.0)
+    ms(r("Tx"), 0.0)
+    for o, a, x in (("Tg", 32, 0), ("Tx", 96, 1)):
+        S([64], [dict(out=r(o, c(x, 64, 2)), in_=r("tabe", c(a, a + 32)), func=AF.Copy)], "set")
+    I(r("oji"), [[0, 4], [1, 16]], 0, -1, 64)
+    ts(r("ojk"), r("oji"), 15, AND)
+    ts(r("ohJ", c(0, 64)), r("ojk"), 0, Op.is_equal)
+    for k in (64, 128, 256, 512):
+        S([k], [dict(out=r("ohJ", c(k, 2 * k)), in_=r("ohJ", c(0, k)), func=AF.Copy)], "set")
+    for h in (0, 1):
+        ts(r("stock", c(1024 * h, 1024 * h + 1024, 2)), r("pdi", c(512 * h, 512 * h + 512)), -2048.0, Op.add, n=512)
+        S([512], [dict(out=r("stock", c(1024 * h + 1, 1024 * h + 1024, 2)), in_=r("stock", c(1024 * h, 1024 * h + 1024, 2)), func=AF.Copy)], "set")
+
+    for t in range(NV):
+        for hh in range(H):
+            h = str(hh)
+            HALF[0] = h
+            al = r(LAND[t] + h)
+            pA, pW, pE = "pA" + h, "pW" + h, "pE" + h
+            c4, c8 = c(0, 4), c(4, 8)
+            last = c(15, 64, 16)
+            late = t > 0 and hh == 0
+            L = [mm(r(pA, c(0, 64)), r("mS"), al)]
+            if t > 0 and not late:
+                L.append(mm(r(pA, c(64, 192)), r("mI"), r("CA", c(128, 256)), True, False))
+            s = len(L) == 1
+            L += [mm(r(pA, c(64, 128)), r("I3"), al, s, False), mm(r(pA, c(64, 128)), r("S2"), al, False, s),
+                  mm(r(pA, c(128, 192)), r("I2"), al, s, False), mm(r(pA, c(128, 192)), r("S3"), al, False, True)]
+            P(L, "lists")
+            tt(r("M" + h), al, r(pA, c(0, 64)), Op.mult, tag="l")
+            xo = "X" if late else "Xi"
+            tt(r(xo + h, c(0, 64)), r("M" + h), r(pA, c(64, 128)), Op.add, tag="l")
+            tt(r(xo + h, c(64, 128)), r("M" + h), r(pA, c(128, 192)), Op.add, tag="l")
+            if late:
+                ts(r("Xi" + h), r("X" + h), r("A32"), Op.add, n=128, tag="l2")
+            ts(r("Xs" + h), r("Xi" + h), 5, SAR, 4095, AND, n=128, tag="l2")
+            cp(r("lu" + h), r("Xs" + h), n=128, tag="l2")
+            P([mm(r(pA, c(192, 256)), r("mI"), al), mm(r(pA, c(256, 320)), r("mI"), al),
+               mm(r(pA, c(320, 384)), r("mS"), al, True, False), mm(r(pA, c(320, 384)), r("nI"), al, False, True)], "keep")
+            gathers(h, "f", "e", "gf", "gd", CH1[hh])
+            P(sums(r(pE, A_, c(0, 16)), "K1", "ab" + h, "CK1"), "key1")
+            S([60, 4, 4], [dict(out=r("pv" + h, A_, c(1, 16)), in_=r(pE, A_, c(0, 15)), func=AF.Copy),
+                           dict(out=r("pv" + h, A_, 0), in_=r(pE, A_, 15), func=AF.Copy, bias=-32.0),
+                           dict(out=r(pE, A_, 16), in_=r(pE, A_, 0), func=AF.Copy, bias=32.0)], "ring")
+            tt(r("cb" + h), r("pv" + h), r(pE, A_, c(1, 17)), Op.is_gt, tag="a")
+            tt(r(pW, c(384, 448)), r("cb" + h), r(pE, A_, c(0, 16)), Op.add, tag="a")
+            scan(r("Ms" + h), r(pW, c(384, 448)), "a")
+            ts(r("cc" + h, c8), r("Ms" + h, last), 1, SAR, 1023, AND, tag="a")
+            ts(r("cc" + h, c4), r("Ms" + h, last), 31, AND, tag="a")
+            cp(r("cu" + h, c(0, 8)), r("cc" + h, c(0, 8)), tag="a2")
+            SG(r("fk" + h), ("f" + h,), ("cu" + h, c8), 64, "fk")
+            P([mm(r(pE, 0, c(64, 68)), r("KU", c(128 * k, 128 * k + 128)), r("fk" + h, c(k, 64, 16)), k == 0, k == 15) for k in range(16)], "u")
+            for k in (0, 64):
+                SG(r("mk" + h, c(k, k + 64)), ("tabe", c(k, k + 32)), ("cu" + h, c4), 64, "mask")
+            tt(r("pr" + h), r("mk" + h), r(pA, c(192, 320)), Op.mult, n=128, tag="a3")
+            P([mm(r(pW, c(0, 256)), r("mI"), r("CA"), True, False), mm(r(pW, c(0, 128)), r("BO"), r("pr" + h), False, False),
+               mm(r(pW, c(128, 192)), r("BO3"), r("pr" + h, c(0, 64)), False, False),
+               mm(r(pW, c(192, 256)), r("BO2"), r("pr" + h, c(64, 128)), False, True)], "wl", 100)
+            cp(r("ui" + h, c4), r(pE, 0, c(64, 68)), tag="o")
+            ts(r("uq" + h, c4), r("ui" + h, c4), 2046, AND, tag="o")
+            cp(r("uu" + h, c4), r("uq" + h, c4), tag="o")
+            SG(r("B" + h), ("stock",), ("uu" + h, c4), 64, "B")
+            tt(r("X" + h, c(0, 64)), r("B" + h), r(pW, c(0, 64)), Op.mult, tag="m")
+            tt(r("X" + h, c(64, 128)), r("B" + h), r(pW, c(64, 128)), Op.mult, tag="m")
+            tt(r("Xi" + h), r("X" + h), r(pW, c(128, 256)), Op.add, n=128, tag="m")
+            ts(r("Xs" + h), r("Xi" + h), 5, SAR, 4095, AND, n=128, tag="m")
+            cp(r("lu" + h), r("Xs" + h), n=128, tag="m")
+            gathers(h, "y", "d", "gy", "gz", CH2[hh])
+            P(sums(r(pW, c(448, 512)), "K2", "ab" + h, "CK2"), "key2")
+            ts(r("tf" + h), r("Ms" + h, last), -0.5, Op.mult, tag="pre")
+            ts(r("c2" + h, c4), r("cc" + h, c4), 2.0, Op.mult, tag="pre")
+            ts(r("rs" + h, c4), r("ui" + h, c4), 1, SAR, 31, AND, tag="pre")
+            ts(r("rs" + h, c8), r("ui" + h, c4), 14, AND, tag="pre")
+            tt(r("FI" + h, c8), r("rs" + h, c4), r("RC", c4), Op.add, tag="pre")
+            tt(r("sb" + h, c4), r("rs" + h, c8), r("RC", c8), Op.add, tag="pre")
+            scan(r("m2" + h), r(pW, c(448, 512)), "b")
+            tt(r("ng" + h), r("m2" + h, last), r("tf" + h), Op.is_ge, tag="b")
+            ts(r("FI" + h, c4), r("m2" + h, last), 1023, AND, tag="b")
+            tt(r("FI" + h, c(12, 16)), r("c2" + h, c4), r("ng" + h), Op.add, tag="b")
+            tt(r("FI" + h, c(8, 12)), r("sb" + h, c4), r("ng" + h), Op.add, tag="b")
+            cp(r("FU" + h), r("FI" + h), tag="b2")
+            SG(r("mx" + h), ("Tx",), ("FU" + h, c(12, 16)), 64, "mask2")
+            SG(r("gp" + h), ("Tg",), ("FU" + h, c(12, 16)), 64, "mask2")
+            V(150, "tensor_tensor", "w", out=r("bj" + h), in0=r("ohJ", ind=("FU" + h, c4)), in1=r("B" + h), op=Op.mult)
+            P([mm(r(pW, c(256, 320)), r("BO"), r("bj" + h), True, False), mm(r(pW, c(256, 320)), r("nI"), al, False, True)], "bj")
+            tt(r("dl" + h), r("mx" + h), r(pA, c(320, 384)), Op.mult, tag="w")
+            P([mm(r(pW, c(320, 384)), r("mI"), al, True, False), mm(r(pW, c(320, 384)), r("ISh"), r("dl" + h), False, True)], "R", 150)
+            tt(r("Y" + h), r("gp" + h), r(pW, c(256, 320)), Op.mult, tag="w")
+            tt(r("snd" + h), r("Y" + h), r(pW, c(320, 384)), Op.add, tag="w")
+            sn = add("G", 300, [("remote_dma", dict(to=LAND[t + 1] + h, in_=r("snd" + h)))], kind="send", tag="%d%d" % (t, hh))
+            add("R", 2300, [], kind="recv", tag="%d%d" % (t, hh), pre=[sn], extra=[(LAND[t + 1] + h, 0, 64, True)])
+            V(150, "tensor_scalar", "nr", out=r("hd" + h), in0=r("d" + h, ind=("FU" + h, c4)), scalar1=0.5, scalar2=-0.25, op0=Op.mult, op1=Op.add)
+            V(150, "tensor_tensor", "nr", out=r("nr" + h), in0=r("y" + h, ind=("FU" + h, c4)), in1=r("hd" + h), op=Op.add)
+        for hh in range(H):
+            h = HALF[0] = str(hh)
+            V(240, "tensor_copy", "sr", out=r("rec", c(2048 * hh, 2048 * hh + 2048), ind=("FU" + h, c(4, 8))), in_=r("nr" + h))
+        HALF[0] = ""
+        if t + 1 < NV:
+            pa = r("pE1", 0, c(116, 120))
+            P([mm(pa, r("on16"), r("ng0"), True, False), mm(pa, r("on16"), r("ng1"), False, True)], "A")
+            V(64, "tensor_reduce", "A", out=r("Gs"), in_=pa, axis=AxisListType.X, op=Op.add)
+            cp(r("Gi", c(0, 1)), r("Gs"), tag="A")
+            ts(r("Ga", c(0, 1)), r("Gi", c(0, 1)), 31, AND, tag="A")
+            ts(r("A32"), r("Ga", c(0, 1)), 32.0, Op.mult, tag="A")
+            ts(r("CA", c(128, 256)), r("onh"), r("A32"), Op.mult, n=128, tag="CA")
+        for hh in range(H):
+            h = HALF[0] = str(hh)
+            V(240, "tensor_copy", "ss", out=r("stock", c(1024 * hh, 1024 * hh + 1024), ind=("FU" + h, c(8, 12))), in_=r("snd" + h))
+    for hh in range(H):
+        h = HALF[0] = str(hh)
+        dma("Y", r("yx", c(2048 * hh, 2048 * hh + 2048)), r("rec", c(2048 * hh, 2048 * hh + 2048)), 3000, "store")
+        S([512], [dict(out=r("po" + h), in_=r("stock", c(1024 * hh, 1024 * hh + 1024, 2)), func=AF.Copy, bias=2048.0)], "po")
+        dma("Y", r("yp", c(512 * hh, 512 * hh + 512)), r("po" + h), 2500, "store")
+        ts(r("yo" + h), r("le" + h), 2048.0, Op.add, tag="yo")
+        dma("Y", r("yw", c(64 * hh, 64 * hh + 64)), r("yo" + h), 2000, "store")
+
+
+def ways():
+    n = len(NODES)
+    succ = [[] for _ in range(n)]
+    for i, x in enumerate(NODES):
+        for p in x["preds"]:
+            succ[p].append(i)
+    way = [0.0] * n
+    for i in range(n - 1, -1, -1):
+        way[i] = NODES[i]["dur"] + max([way[j] + 110.0 for j in succ[i]], default=0.0)
+    return succ, way
+
+
+def schedule(bonus, sw):
+    succ, way = sw
+    n = len(NODES)
+    prio = [way[i] + bonus.get(NODES[i]["key"], 0) for i in range(n)]
+    look = {q: bonus.get("look" + q, 0) for q in "VSPGYR"}
+    left = [len(x["preds"]) for x in NODES]
+    rt = [0.0] * n
+    ready = {}
+    for i in range(n):
+        if left[i] == 0:
+            ready.setdefault(NODES[i]["eng"], []).append(i)
+    free = {}
+    order = []
+    end = 0.0
+    while len(order) < n:
+        s, e = min((max(free.get(q, 0.0), min(rt[i] for i in L)), q) for q, L in ready.items() if L)
+        i = max((i for i in ready[e] if rt[i] <= s + look[e]), key=lambda k: (prio[k] - 10 * max(rt[k] - s, 0), -k))
+        s = max(s, rt[i])
+        ready[e].remove(i)
+        x = NODES[i]
+        free[e] = s + (100.0 if x["kind"] == "dma" else 0.0 if x["kind"] == "recv" else x["dur"])
+        x["t0"], x["t1"] = s, s + x["dur"]
+        end = max(end, x["t1"])
+        order.append(i)
+        for j in succ[i]:
+            left[j] -= 1
+            rt[j] = max(rt[j], x["t1"] + (60.0 if NODES[j]["eng"] == e else 110.0))
+            if left[j] == 0:
+                ready.setdefault(NODES[j]["eng"], []).append(j)
+    return order, end
+
+
+def search(tries, seed):
+    rnd = np.random.RandomState(seed)
+    sw = ways()
+    keys = sorted({x["key"] for x in NODES})
+    B = {q: 1500 for q in keys if q.endswith("0") and q[0] != "s"}
+    B.update({"A": 6000, "sr0": 5000, "sr1": 5000, "ss0": -9000, "ss1": -9000, "set": -3000, "lookS": 50, "lookV": 100})
+    best, end = schedule(B, sw)
+    steps = (-8000, -4000, -2000, -1000, -500, 500, 1000, 2000, 4000, 8000)
+    for _ in range(tries):
+        C = dict(B)
+        for _ in range((1, 1, 2, 3, 6)[rnd.randint(5)]):
+            k = rnd.randint(len(keys) + 6)
+            if k >= len(keys):
+                C["look" + "VSP"[k % 3]] = (0, 50, 100, 200, 300, 500)[rnd.randint(6)]
+            else:
+                C[keys[k]] = steps[rnd.randint(10)] + (C.get(keys[k], 0) if rnd.randint(2) else 0)
+        o, v = schedule(C, sw)
+        if v <= end:
+            best, end, B = o, v, C
+    return schedule(B, sw)[0]
+
+
+def plan(order):
+    cnt, know, comp, out, final = {}, {}, {}, [], {}
+    for i in order:
+        x = NODES[i]
+        e, kind = x["eng"], x["kind"]
+        K = know.setdefault(e, {})
+        waits = []
+        need = {}
+        for p in (x["preds"] if kind != "recv" else []):
+            sm, v = NODES[p]["tok"]
+            if need.get(sm, (0, 0))[0] < v:
+                need[sm] = (v, p)
+        for sm, (v, p) in sorted(need.items(), key=lambda z: -NODES[z[1][1]]["t1"]):
+            if K.get(sm, 0) < v:
+                waits.append((sm, v))
+                for a, b in NODES[p]["clk"].items():
+                    K[a] = max(K.get(a, 0), b)
+        clk = dict(K) if kind != "recv" else {}
+        if kind == "comp":
+            sm = "s" + e
+            v = cnt[sm] = cnt.get(sm, 0) + (1 if x["calls"][0][0] == "matmul" else len(x["calls"]))
+            for a, b in comp.get(e, {}).items():
+                clk[a] = max(clk.get(a, 0), b)
+            comp[e] = clk
+        elif kind == "dma":
+            sm, v = "d%d" % i, 16
+        else:
+            sm, v = ("l" if kind == "send" else "r") + x["tag"], 8
+        clk[sm] = v
+        x["tok"], x["clk"] = (sm, v), clk
+        final[sm] = v
+        out.append((i, waits))
+    return out, final, know["G"]
+
+
+build()
+PLAN, FINAL, KNOWG = plan(search(TRIES, SEED))
+SEMAPHORES = list(FINAL)
+
+
+def rank_program(g, core, T, topo):
+    rank = T.rank_of(core)
+    if rank is None:
+        return
+    n = len(T.cores)
+    Q = {"V": g.vector, "S": g.scalar, "P": g.tensor, "G": g, "Y": g.sync}
+    for i, waits in PLAN:
+        x = NODES[i]
+        if x["kind"] == "recv":
+            continue
+        q = Q[x["eng"]]
+        for sm, v in waits:
+            q.wait_ge(T.sem[sm], v)
+        if x["kind"] == "send":
+            t = int(x["tag"][0])
+            dst = T.cores[(rank + (STEP if t + 1 < NV else -STEP * (NV - 1))) % n]
+            kw = x["calls"][0][1]
+            rid, pid = topo.addr(dst)[:2]
+            g.remote_dma(out_ap=T[kw["to"]][:], in_ap=ap(T, kw["in_"]), remote_sem=T.sem["r" + x["tag"]], local_sem=T.sem["l" + x["tag"]],
+                         pid=pid, routing_id=rid, dma_engine_mask=sum(1 << e for e in topo.engines(core, dst)[:8]))
+            continue
+        k = len(x["calls"])
+        for m, kw in x["calls"]:
+            k -= 1
+            kw = {a: (ap(T, b) if isref(b) else b) for a, b in kw.items()}
+            if m == "memset":
+                ins = q.memset(kw["out"], kw["value"])
+            elif m == "dma_start":
+                ins = q.dma_start(kw["out"], kw["in_"])
+            elif m == "matmul":
+                ins = q.matmul(kw["out"], kw["lhsT"], kw["rhs"], kw["start"], kw["stop"])
+            elif m == "iota":
+                ins = q.iota(kw.pop("out"), **kw)
+            elif m == "activation":
+                ins = q.activation(**kw)
+            else:
+                ins = {"tensor_copy": q.tensor_copy, "tensor_tensor": q.tensor_tensor, "tensor_scalar": q.tensor_scalar,
+                       "tensor_reduce": q.tensor_reduce, "tensor_tensor_scan": q.tensor_tensor_scan}[m](**kw)
+            if x["kind"] == "dma":
+                ins.then_inc(T.sem[x["tok"][0]], 16)
+            elif m != "matmul" or k == 0:
+                ins.then_inc(T.sem[x["tok"][0]], 1)
+    for sm in SEMAPHORES:
+        if KNOWG.get(sm, 0) < FINAL[sm]:
+            g.wait_ge(T.sem[sm], FINAL[sm])

@@ -1,13 +1,13 @@
 import numpy as np
-from concourse.mybir import AluOpType, AxisListType, ActivationFunctionType
+from concourse.mybir import AluOpType, ActivationFunctionType
 
 Op = AluOpType
 AF = ActivationFunctionType
 NV, STEP, H = 4, 3, 2
-GAM = 1.6
-CH1 = [[16] * 4, [16] * 4]
-CH2 = [[32] * 2, [16] * 4]
-TRIES = 3000
+CH = {1: ([16, 16, 16, 16], [16, 16, 16, 8, 8], [16, 16, 16, 8, 8]),
+      3: ([16, 16, 16, 16], [16, 16, 16, 8, 8], [16, 16, 16, 8, 8])}
+EARLY = 8
+TRIES = 1500
 SEED = 1
 BIG = float(2 ** 24)
 LAND = "la lb lc ld le".split()
@@ -28,47 +28,51 @@ def bufs(where, dtype, shape, names, pack=None, halves=False):
                 SCRATCH[pack] = (where, [128, o + (shape[1] + 15) // 16 * 16], dtype)
 
 
-bufs("sbuf", "bfloat16", [128, 4096], "rec")
+bufs("sbuf", "bfloat16", [128, 4096 + 32], "rec")
+bufs("sbuf", "bfloat16", [128, 2048], "rec2")
 bufs("sbuf", "float32", [128, 2048], "stock")
 bufs("sbuf", "int32", [128, 1024], "pdi")
 bufs("sbuf", "int32", [128, 128], "wdi")
 bufs("sbuf", "int32", [128, 1], "wti")
-bufs("sbuf", "bfloat16", [128, 2048], "K1 K2 KU")
+bufs("sbuf", "bfloat16", [128, 144], "Z1 Z2 ZU", "PB")
 bufs("sbuf", "bfloat16", [128, 1024], "ohJ")
-bufs("sbuf", "bfloat16", [128, 64], "Tg Tx")
-bufs("sbuf", "float16", [128, 4, 16], "CK1 CK2")
-bufs("sbuf", "float32", [128, 4, 16], "CKc")
+bufs("sbuf", "bfloat16", [128, 256], "tab")
+bufs("sbuf", "float16", [128, 4, 16], "CK1 CK2 CKU")
+bufs("sbuf", "float32", [128, 4, 16], "CKa CKb CKc")
 bufs("sbuf", "int32", [128, 4, 16], "CKi CKj")
-bufs("sbuf", "int32", [128, 128], "cD cM cK cT1 cT2 cT3 tabi tabj", "PI")
-bufs("sbuf", "int32", [128, 64], "oji ojk", "PI")
-bufs("sbuf", "int32", [128, 8], "RC Gi Ga", "PI")
-bufs("sbuf", "float32", [128, 1], "wcol Gs A32", "PF")
+bufs("sbuf", "int32", [128, 128], "cD cM cK cT1 cT2 cT3", "PI")
+bufs("sbuf", "int32", [128, 256], "tabi tabj", "PI")
+bufs("sbuf", "int32", [128, 16], "oji ojk", "PI")
+bufs("sbuf", "int32", [128, 8], "RC r31 r7 SI", "PI")
+bufs("sbuf", "uint16", [128, 8], "SU", "PU")
+bufs("sbuf", "float32", [128, 1], "wcol Acol", "PF")
+bufs("sbuf", "bfloat16", [128, 1], "nq", "PB")
 bufs("sbuf", "float32", [128, 128], "ISh I32", "PF")
-bufs("sbuf", "float32", [128, 64], "SM2", "PF")
-bufs("sbuf", "float16", [128, 128], "BO mI nI mS mP tA tB I3 I2 S3 S2 BO3 BO2 onh", "PH")
+bufs("sbuf", "float32", [128, 64], "SMa SMi", "PF")
+bufs("sbuf", "float16", [128, 128], "BO mI nI mS mP tA tB I3 I2 S3 S2 mF mG SmI BO3 BO2 onh n2I I5 nI5", "PH")
 bufs("sbuf", "float16", [128, 256], "CA", "PH")
-bufs("sbuf", "bfloat16", [128, 128], "BOm on16 tabe", "PB")
-bufs("sbuf", "float16", [128, 64], "la lb lc ld le snd", halves=True)
+bufs("sbuf", "float16", [128, 64], "C2k", "PH")
+bufs("sbuf", "float16", [128, 8], "RS ng c48", "PH")
+bufs("sbuf", "float16", [128, 64], "la lb lc ld snd", halves=True)
+bufs("sbuf", "float32", [128, 64], "le nw", halves=True)
 bufs("sbuf", "float16", [128, 64], "bj", "PH", True)
 bufs("sbuf", "float16", [128, 128], "pr", "PH", True)
-bufs("sbuf", "float32", [128, 64], "M B dl Y", "PF", True)
+bufs("sbuf", "float32", [128, 64], "M B dl Y Rs hd ne", "PF", True)
 bufs("sbuf", "float32", [128, 128], "X", "PF", True)
-bufs("sbuf", "float32", [128, 4], "tf", "PF", True)
-bufs("sbuf", "float32", [128, 64], "yo", halves=True)
-bufs("sbuf", "int32", [128, 128], "Xi Xs", "PI", True)
-bufs("sbuf", "int32", [128, 64], "hd Ms m2", "PI", True)
-bufs("sbuf", "int32", [128, 16], "cc c2 ui uq sb rs FI", "PI", True)
+bufs("sbuf", "int32", [128, 128], "Xi Xs MU", "PI", True)
+bufs("sbuf", "int32", [128, 64], "nr m2", "PI", True)
+bufs("sbuf", "int32", [128, 2, 8], "cc")
+bufs("sbuf", "int32", [128, 2, 12], "FI")
 bufs("sbuf", "uint16", [128, 128], "lu", "PU", True)
-bufs("sbuf", "uint16", [128, 16], "cu uu FU", "PU", True)
-bufs("sbuf", "bfloat16", [128, 128], "mk", "PB", True)
-bufs("sbuf", "bfloat16", [128, 64], "mx gp nr fk", "PB", True)
-bufs("sbuf", "bfloat16", [128, 4], "ng", "PB", True)
-bufs("sbuf", "bfloat16", [128, 4, 256], "ab", halves=True)
-bufs("sbuf", "bfloat16", [128, 1024], "f e y d", halves=True)
-bufs("sbuf", "float32", [128, 4, 16], "pv cb", halves=True)
-bufs("sbuf", "float32", [128, 512], "po", halves=True)
+bufs("sbuf", "uint16", [128, 16], "cu FU", "PU", True)
+bufs("sbuf", "bfloat16", [128, 64], "mx gp", "PB", True)
+bufs("sbuf", "bfloat16", [128, 4, 256], "ab f", halves=True)
+bufs("sbuf", "bfloat16", [128, 1024], "e y d", halves=True)
+bufs("sbuf", "float32", [128, 4, 16], "pv", halves=True)
+bufs("sbuf", "float16", [128, 4, 16], "cb", halves=True)
 bufs("psum", "float32", [128, 512], "pA pW", halves=True)
 bufs("psum", "float32", [128, 4, 128], "pE", halves=True)
+bufs("psum", "float32", [128, 512], "pC pS")
 A_ = slice(None)
 
 
@@ -97,18 +101,15 @@ def isref(x):
 def span(name, ix):
     shape = (SCRATCH[name][1] if name in SCRATCH else EXT[name])[1:]
     lo = hi = 0
-    stride = 1
+    stride = n = 1
     for k in range(len(shape) - 1, -1, -1):
         s = ix[k] if k < len(ix) else A_
-        if isinstance(s, int):
-            a = b = s
-        else:
-            a, b, st = s.indices(shape[k])
-            b = a + (b - 1 - a) // st * st
-        lo += a * stride
-        hi += b * stride
+        q = [s] if isinstance(s, int) else range(*s.indices(shape[k]))
+        lo += min(q[0], q[-1]) * stride
+        hi += max(q[0], q[-1]) * stride
         stride *= shape[k]
-    return lo, hi + 1
+        n *= len(q)
+    return lo, hi + 1, n
 
 
 def ap(T, ref):
@@ -118,26 +119,56 @@ def ap(T, ref):
 
 NODES = []
 ACC = {}
+BANK = {}
 HALF = [""]
+MODELS = [(1.04, 1.56, 3.8, 25, 0.55, 2300, 60, 110), (0.9, 1.4, 3.0, 40, 0.8, 2500, 100, 150)]
 
 
-def add(eng, dur, calls, kind="comp", tag="", extra=(), pre=()):
+def cost(eng, calls, model):
+    cy, gam, sc, fix, pe = model[:5]
+    t = 0.0
+    for m, kw in calls:
+        refs = [v for v in kw.values() if isref(v)]
+        n = max(span(v[1], v[2])[2] for v in refs if v[3] is None)
+        dts = [SCRATCH[v[1]][2] for v in refs if span(v[1], v[2])[2] > 1]
+        if m == "matmul":
+            t += max(64, span(kw["rhs"][1], kw["rhs"][2])[2]) * pe * (4 if SCRATCH[kw["rhs"][1]][2] == "float32" else 1)
+        elif eng == "G":
+            t += 150 + 2 * cy * n
+        elif kw["out"][3] is not None:
+            t += 50 + sc * cy * n
+        elif any(v[3] is not None for v in refs):
+            t += (50 if eng == "V" else 65) + gam * cy * n
+        else:
+            if m == "tensor_tensor" and SCRATCH[kw["in0"][1]][0] == SCRATCH[kw["in1"][1]][0]:
+                n *= 2
+            elif eng == "V" and m != "tensor_tensor" and all(d in ("bfloat16", "float16", "uint16") for d in dts):
+                n /= 2
+            t += fix + cy * max(n, 64)
+    return t + (40 if eng == "P" else 0)
+
+
+def add(eng, calls, kind="comp", tag="", dur=None, extra=(), pre=()):
     n = len(NODES)
-    preds = set(pre)
+    preds, after = set(pre), set()
     touch = list(extra)
     for m, kw in calls:
         for k, v in kw.items():
             if isref(v):
-                touch.append((v[1],) + span(v[1], v[2]) + (k == "out",))
+                touch.append((v[1],) + span(v[1], v[2])[:2] + (k == "out",))
                 if v[3] is not None:
-                    touch.append((v[3][0],) + span(v[3][0], (v[3][1],)) + (False,))
+                    touch.append((v[3][0],) + span(v[3][0], (v[3][1],))[:2] + (False,))
     for name, lo, hi, w in touch:
         psum = name in SCRATCH and SCRATCH[name][0] == "psum"
+        if psum and eng == "P":
+            after.add(BANK.get(name, n))
+            BANK[name] = n
         keep = []
         for q in ACC.setdefault(name, []):
             m, me, a, b, mw = q
-            if m != n and psum and me != eng:
-                preds.add(m)
+            if m != n and psum and (me != eng or eng == "P"):
+                if me != eng:
+                    preds.add(m)
                 keep.append(q)
                 continue
             if m != n and a < hi and lo < b and (w or mw):
@@ -146,260 +177,295 @@ def add(eng, dur, calls, kind="comp", tag="", extra=(), pre=()):
                     continue
             keep.append(q)
         keep.append((n, eng, lo, hi, w))
-        ACC[name] = keep
-    NODES.append({"eng": eng, "dur": dur, "calls": calls, "kind": kind, "tag": tag, "preds": sorted(preds), "key": tag + HALF[0]})
+        ACC[name] = keep[-40:] if psum else keep
+    durs = [cost(eng, calls, M) if dur is None else M[5] if kind == "recv" else dur for M in MODELS]
+    NODES.append({"eng": eng, "dur": durs, "calls": calls, "kind": kind, "tag": tag, "preds": sorted(preds),
+                  "after": sorted(after - preds - {n}), "key": tag + HALF[0]})
     return n
 
 
-def V(n, meth, tag="", **kw):
-    return add("V", 25 + 1.0 * max(n, 64), [(meth, kw)], tag=tag)
+def V(meth, tag, **kw):
+    return add("V", [(meth, kw)], tag=tag)
 
 
-def S(n, calls, tag=""):
-    return add("S", sum(35 + 1.0 * max(k, 64) for k in n), [("activation", kw) for kw in calls], tag=tag)
+def S(out, in_, tag, func=AF.Copy, **kw):
+    return add("S", [("activation", dict(out=out, in_=in_, func=func, **kw))], tag=tag)
 
 
-def SG(out, win, lst, n, tag):
-    return add("S", 70 + GAM * n, [("activation", dict(out=out, in_=r(win[0], *win[1:], ind=lst), func=AF.Copy))], tag=tag)
+def P(calls, tag):
+    return add("P", [("matmul", kw) for kw in calls], tag=tag)
 
 
-def P(calls, tag="", slow=0):
-    return add("P", 60 + 40 * len(calls) + slow, [("matmul", kw) for kw in calls], tag=tag)
+def I(out, pattern, base, cm, **kw):
+    return add("G", [("iota", dict(out=out, pattern=pattern, base=base, channel_multiplier=cm, **kw))], tag="set")
 
 
-def I(out, pattern, base, cm, n, **kw):
-    return add("G", 130 + 1.7 * n, [("iota", dict(out=out, pattern=pattern, base=base, channel_multiplier=cm, **kw))], tag="set")
+def gcopy(out, in_, n):
+    return add("G", [("affine_select", dict(out=out, in_=in_, pattern=[[0, n]], compare_op=Op.is_gt, fill=0.0, base=1,
+                                            channel_multiplier=0))], tag="gset")
 
 
 def mm(out, lhsT, rhs, start=True, stop=True):
     return dict(out=out, lhsT=lhsT, rhs=rhs, start=start, stop=stop)
 
 
-def ts(out, in0, s1, op0, s2=None, op1=None, n=64, tag="set"):
+def ts(out, in0, s1, op0, s2=None, op1=None, tag="set"):
     kw = {} if op1 is None else {"op1": op1}
-    return V(n, "tensor_scalar", tag, out=out, in0=in0, scalar1=s1, scalar2=s2, op0=op0, **kw)
+    return V("tensor_scalar", tag, out=out, in0=in0, scalar1=s1, scalar2=s2, op0=op0, **kw)
 
 
-def tt(out, a, b, op, n=64, tag="set"):
-    return V(n, "tensor_tensor", tag, out=out, in0=a, in1=b, op=op)
+def tt(out, a, b, op, tag="set"):
+    return V("tensor_tensor", tag, out=out, in0=a, in1=b, op=op)
 
 
-def cp(out, in_, n=64, tag="set"):
-    return V(n, "tensor_copy", tag, out=out, in_=in_)
+def cp(out, in_, tag="set"):
+    return V("tensor_copy", tag, out=out, in_=in_)
 
 
-def ms(out, v, n=64):
-    return V(n, "memset", "set", out=out, value=v)
+def ms(out, v):
+    return V("memset", "set", out=out, value=v)
 
 
-def scan(out, data1, tag):
-    return V(64, "tensor_tensor_scan", tag, out=out, data0=r("SM2"), data1=data1, initial=BIG, op0=Op.add, op1=Op.min)
+def scan(out, data0, data1, op0, op1, tag):
+    return V("tensor_tensor_scan", tag, out=out, data0=data0, data1=data1, initial=0.0, op0=op0, op1=op1)
 
 
-def dma(q, out, in_, dur, tag):
-    return add(q, dur, [("dma_start", dict(out=out, in_=in_))], kind="dma", tag=tag)
+def dma(q, out, in_, dur, tag, pre=()):
+    return add(q, [("dma_start", dict(out=out, in_=in_))], kind="dma", tag=tag, dur=dur, pre=pre)
 
 
-def sums(out, K, src, first):
-    return [mm(out, r("mI"), r(first), True, False)] + [
-        mm(out, r(K, c(128 * k, 128 * k + 128)), r(src, A_, c(16 * k, 16 * k + 16)), False, k == 15) for k in range(16)]
+def sums(out, Z, src, ks, start, stop):
+    return [mm(out, r(Z, c(15 - k, 143 - k)), r(src, A_, c(16 * k, 16 * k + 16)), start and k == ks[0], stop and k == ks[-1]) for k in ks]
 
 
-def gathers(h, a, b, ta, tb, chunks):
-    o = 0
-    for w in chunks:
-        k, e = c(16 * o, 16 * o + 16 * w), o + w
-        SG(r(a + h, k), ("rec",), ("lu" + h, c(o, e)), 16 * w, ta)
-        V(16 * w * GAM, "tensor_tensor", tb, out=r(b + h, k), in0=r("rec", ind=("lu" + h, c(64 + o, 64 + e))), in1=r(a + h, k), op=Op.subtract)
-        S([16 * w], [dict(out=r("ab" + h, c(o // 16, e // 16), A_), in_=r(b + h, k), func=AF.Abs)], "ab" + tb)
-        o = e
+def piece(name, o, e):
+    if len(SCRATCH[name][1]) == 2:
+        return r(name, c(16 * o, 16 * e))
+    if e - o > 16:
+        return r(name, c(o // 16, e // 16), A_)
+    return r(name, o // 16, c(o % 16 * 16, ((e - 1) % 16 + 1) * 16))
+
+
+def cuts(w):
+    return [(sum(w[:k]), sum(w[:k + 1])) for k in range(len(w))]
+
+
+def gathers(h, a, b, win, stage):
+    s = str(stage)
+    for o, e in cuts(CH[stage][0]):
+        S(piece(a + h, o, e), r("rec", win, ind=("lu" + h, c(o, e))), "ga" + s)
+    for o, e in cuts(CH[stage][1]):
+        tt(piece(b + h, o, e), r("rec", win, ind=("lu" + h, c(64 + o, 64 + e))), piece(a + h, o, e), Op.subtract, "gb" + s)
+    for o, e in cuts(CH[stage][2]):
+        S(piece("ab" + h, o, e), piece(b + h, o, e), "ab" + s, AF.Abs)
 
 
 def build():
     AND, SAR, SLR = Op.bitwise_and, Op.arith_shift_right, Op.logical_shift_right
     dma("Y", r("wdi"), r("wd"), 2000, "load")
     dma("S", r("wti"), r("wt"), 2000, "load")
-    dma("Y", r("rec", c(0, 2048)), r("xt", c(0, 2048)), 4500, "load")
-    dma("S", r("rec", c(2048, 4096)), r("xt", c(2048, 4096)), 4500, "load")
-    dma("Y", r("pdi"), r("pd"), 4500, "load")
-    I(r("cD"), [[1, 128]], 0, -1, 128)
-    I(r("cM"), [[1, 128]], 0, 0, 128)
-    I(r("cK"), [[0, 128]], 0, 1, 128)
-    ts(r("cT3"), r("cD"), 15, AND, n=128)
-    ts(r("cT1"), r("cM"), 4, SLR, n=128)
-    ts(r("cT2"), r("cK"), 4, SLR, n=128)
-    tt(r("BO"), r("cT1"), r("cT2"), Op.is_equal, n=256)
-    ts(r("mI"), r("cD"), 0, Op.is_equal, n=128)
-    ts(r("tA"), r("cT3"), 15, Op.is_equal, n=128)
-    tt(r("mS"), r("tA"), r("BO"), Op.mult, n=256)
+    dma("Y", r("rec", c(0, 2048)), r("xt", c(0, 2048)), 4300, "load")
+    dma("S", r("rec", c(2048, 4096)), r("xt", c(2048, 4096)), 4300, "load")
+    dma("Y", r("pdi"), r("pd"), 5800, "loadp")
+    I(r("cD"), [[1, 128]], 0, -1)
+    I(r("cM"), [[1, 128]], 0, 0)
+    I(r("cK"), [[0, 128]], 0, 1)
+    ts(r("cT3"), r("cD"), 15, AND)
+    ts(r("cT1"), r("cM"), 4, SLR)
+    ts(r("cT2"), r("cK"), 4, SLR)
+    tt(r("BO"), r("cT1"), r("cT2"), Op.is_equal)
+    ts(r("mI"), r("cD"), 0, Op.is_equal)
+    ts(r("tA"), r("cT3"), 15, Op.is_equal)
+    tt(r("mS"), r("tA"), r("BO"), Op.mult)
     for o, i, k in (("I3", "mI", 3232.0), ("I2", "mI", 2080.0), ("S3", "mS", 3232.0), ("S2", "mS", 2080.0), ("nI", "mI", -1.0),
-                    ("BO3", "BO", 3232.0), ("BO2", "BO", 2080.0), ("BOm", "BO", -4096.0)):
+                    ("BO3", "BO", 3232.0), ("BO2", "BO", 2080.0), ("n2I", "mI", -2.0), ("I5", "mI", 512.0), ("nI5", "mI", -512.0),
+                    ("I32", "mI", 1.0)):
         ts(r(o), r(i), k, Op.mult)
+    tt(r("mF"), r("I3"), r("S2"), Op.add)
+    tt(r("mG"), r("I2"), r("S3"), Op.add)
+    tt(r("SmI"), r("mS"), r("mI"), Op.subtract)
     for h in "01":
         ts(r("la" + h), r("wdi", c(64 * int(h), 64 * int(h) + 64)), -2048.0, Op.add)
-    ms(r("K1"), 0.0, 1024)
-    for g in range(8):
-        cp(r("K1", c(16 * g, 16 * g + 1936, 129)), r("BOm", c(16 * g, 16 * g + 16)))
-    ts(r("wcol"), r("wti"), -1.0 / 2048, Op.mult)
-    ts(r("KU"), r("K1"), r("wcol"), Op.mult, n=1024)
-    S([2048], [dict(out=r("K2"), in_=r("K1"), func=AF.Copy, scale=-1.0)], "set")
-    cp(r("I32"), r("mI"), n=128)
-    ts(r("tB"), r("cT3"), 1, Op.is_equal, n=128)
-    tt(r("mP"), r("tB"), r("BO"), Op.mult, n=256)
-    tt(r("ISh"), r("mI"), r("mP"), Op.subtract, n=256)
-    ms(r("on16"), 1.0)
+    ms(r("Z1"), 0.0)
+    ts(r("Z1", c(15, 143, 16)), r("BO", c(0, 128, 16)), 2048.0, Op.mult)
+    ts(r("Z2"), r("Z1"), 2.0, Op.mult)
+    ts(r("wcol"), r("wti"), 1.0 / 2048, Op.mult)
+    ts(r("ZU"), r("Z1"), r("wcol"), Op.mult)
+    ts(r("tB"), r("cT3"), 1, Op.is_equal)
+    tt(r("mP"), r("tB"), r("BO"), Op.mult)
+    tt(r("ISh"), r("mI"), r("mP"), Op.subtract)
     ms(r("onh"), 1.0)
+    ms(r("c48"), 48.0)
+    ms(r("C2k"), 2048.0)
     ms(r("CA", c(0, 64)), 2080.0)
     ms(r("CA", c(64, 128)), 3232.0)
     ms(r("CA", c(128, 256)), 0.0)
-    I(r("CKi"), [[0, 4], [1, 16]], 0, 16, 64)
-    I(r("CKc"), [[256, 4], [0, 16]], 0, 0, 64, allow_small_or_imprecise_dtypes=True)
+    I(r("CKi"), [[0, 4], [1, 16]], 0, 16)
+    for o, pat, base in (("CKc", [[256, 4], [0, 16]], 1024), ("CKa", [[0, 4], [-4, 16]], 62), ("CKb", [[0, 4], [-2048, 16]], 15 * 2048)):
+        I(r(o), pat, base, 0, allow_small_or_imprecise_dtypes=True)
     ts(r("CKj"), r("CKi"), 255, AND)
-    tt(r("CK2"), r("CKj"), r("CKc"), Op.add, n=128)
-    ts(r("CK1"), r("CK2"), 2.0, Op.mult)
-    ts(r("RC", c(0, 4)), r("CK2", A_, 0), 2.0, Op.mult)
-    ts(r("RC", c(4, 8)), r("CK2", A_, 0), 1.0, Op.mult)
-    ms(r("SM2"), 0.0)
-    ms(r("SM2", c(0, 64, 16)), BIG)
-    I(r("tabi", c(0, 96)), [[1, 3], [1, 16], [1, 2]], -1, -1, 96)
-    I(r("tabi", c(96, 128)), [[1, 16], [0, 2]], 0, -1, 32)
-    ts(r("tabj"), r("tabi"), 15, AND, n=128)
-    ts(r("tabe"), r("tabj"), 0, Op.is_equal, n=128)
-    ms(r("Tg"), 0.0)
-    ms(r("Tx"), 0.0)
-    for o, a, x in (("Tg", 32, 0), ("Tx", 96, 1)):
-        S([64], [dict(out=r(o, c(x, 64, 2)), in_=r("tabe", c(a, a + 32)), func=AF.Copy)], "set")
-    I(r("oji"), [[0, 4], [1, 16]], 0, -1, 64)
+    tt(r("CK2"), r("CKj"), r("CKc"), Op.add)
+    cp(r("CK1"), r("CKa"))
+    cp(r("CKU"), r("CKb"))
+    for hh in range(H):
+        ts(r("RC", c(4 * hh, 4 * hh + 4)), r("CK2", A_, 0), -1024.0, Op.add, 2.0, Op.mult)
+        ts(r("RS", c(4 * hh, 4 * hh + 4)), r("CK2", A_, 0), 0.5, Op.mult, -512.0 * hh, Op.add)
+    for o, v in (("SMa", -BIG), ("SMi", BIG)):
+        ms(r(o), 0.0)
+        ms(r(o, c(0, 64, 16)), v)
+    for q, (pat, base) in enumerate((([[1, 16], [1, 2], [0, 2]], 1), ([[1, 16], [1, 2], [0, 2]], 15), ([[1, 16], [1, 2], [256, 2]], 0),
+                                     ([[1, 16], [0, 2], [-256, 2]], 257))):
+        I(r("tabi", c(64 * q, 64 * q + 64)), pat, base, 1)
+    ts(r("tabj"), r("tabi"), 0x10F, AND)
+    ts(r("tab"), r("tabj"), 0, Op.is_equal)
+    I(r("oji"), [[1, 16]], 0, -1)
     ts(r("ojk"), r("oji"), 15, AND)
-    ts(r("ohJ", c(0, 64)), r("ojk"), 0, Op.is_equal)
-    for k in (64, 128, 256, 512):
-        S([k], [dict(out=r("ohJ", c(k, 2 * k)), in_=r("ohJ", c(0, k)), func=AF.Copy)], "set")
+    ts(r("ohJ", c(0, 16)), r("ojk"), 0, Op.is_equal)
     for h in (0, 1):
-        ts(r("stock", c(1024 * h, 1024 * h + 1024, 2)), r("pdi", c(512 * h, 512 * h + 512)), -2048.0, Op.add, n=512)
-        S([512], [dict(out=r("stock", c(1024 * h + 1, 1024 * h + 1024, 2)), in_=r("stock", c(1024 * h, 1024 * h + 1024, 2)), func=AF.Copy)], "set")
+        gcopy(r("stock", c(512 + 512 * h, 1024 + 512 * h)), r("pdi", c(512 * h, 512 * h + 512)), 512)
+    for k in (16, 32, 64, 128, 256, 512):
+        gcopy(r("ohJ", c(k, 2 * k)), r("ohJ", c(0, k)), k)
 
+    c4, c8, c12 = c(0, 4), c(4, 8), c(8, 12)
+    last = c(15, 64, 16)
     for t in range(NV):
+        end = t + 1 == NV
+        win = c(0, 4096 + 32 * (t > 0))
+
+        def offsets(h, tag):
+            ts(r("Xs" + h), r("Xi" + h), 5, SAR, 4095, AND, tag)
+            if t == 0:
+                cp(r("lu" + h), r("Xs" + h), tag + "u")
+            else:
+                ts(r("lu" + h), r("Xs" + h), r("Acol"), Op.add, tag=tag + "u")
+
+        if end:
+            HALF[0] = ""
+            dma("Y", r("rec2"), r("rec", c(0, 2048)), 3000, "rec2")
         for hh in range(H):
-            h = str(hh)
-            HALF[0] = h
+            h = HALF[0] = str(hh)
             al = r(LAND[t] + h)
             pA, pW, pE = "pA" + h, "pW" + h, "pE" + h
-            c4, c8 = c(0, 4), c(4, 8)
-            last = c(15, 64, 16)
-            late = t > 0 and hh == 0
-            L = [mm(r(pA, c(0, 64)), r("mS"), al)]
-            if t > 0 and not late:
-                L.append(mm(r(pA, c(64, 192)), r("mI"), r("CA", c(128, 256)), True, False))
-            s = len(L) == 1
-            L += [mm(r(pA, c(64, 128)), r("I3"), al, s, False), mm(r(pA, c(64, 128)), r("S2"), al, False, s),
-                  mm(r(pA, c(128, 192)), r("I2"), al, s, False), mm(r(pA, c(128, 192)), r("S3"), al, False, True)]
-            P(L, "lists")
-            tt(r("M" + h), al, r(pA, c(0, 64)), Op.mult, tag="l")
-            xo = "X" if late else "Xi"
-            tt(r(xo + h, c(0, 64)), r("M" + h), r(pA, c(64, 128)), Op.add, tag="l")
-            tt(r(xo + h, c(64, 128)), r("M" + h), r(pA, c(128, 192)), Op.add, tag="l")
-            if late:
-                ts(r("Xi" + h), r("X" + h), r("A32"), Op.add, n=128, tag="l2")
-            ts(r("Xs" + h), r("Xi" + h), 5, SAR, 4095, AND, n=128, tag="l2")
-            cp(r("lu" + h), r("Xs" + h), n=128, tag="l2")
-            P([mm(r(pA, c(192, 256)), r("mI"), al), mm(r(pA, c(256, 320)), r("mI"), al),
-               mm(r(pA, c(320, 384)), r("mS"), al, True, False), mm(r(pA, c(320, 384)), r("nI"), al, False, True)], "keep")
-            gathers(h, "f", "e", "gf", "gd", CH1[hh])
-            P(sums(r(pE, A_, c(0, 16)), "K1", "ab" + h, "CK1"), "key1")
-            S([60, 4, 4], [dict(out=r("pv" + h, A_, c(1, 16)), in_=r(pE, A_, c(0, 15)), func=AF.Copy),
-                           dict(out=r("pv" + h, A_, 0), in_=r(pE, A_, 15), func=AF.Copy, bias=-32.0),
-                           dict(out=r(pE, A_, 16), in_=r(pE, A_, 0), func=AF.Copy, bias=32.0)], "ring")
-            tt(r("cb" + h), r("pv" + h), r(pE, A_, c(1, 17)), Op.is_gt, tag="a")
-            tt(r(pW, c(384, 448)), r("cb" + h), r(pE, A_, c(0, 16)), Op.add, tag="a")
-            scan(r("Ms" + h), r(pW, c(384, 448)), "a")
-            ts(r("cc" + h, c8), r("Ms" + h, last), 1, SAR, 1023, AND, tag="a")
-            ts(r("cc" + h, c4), r("Ms" + h, last), 31, AND, tag="a")
-            cp(r("cu" + h, c(0, 8)), r("cc" + h, c(0, 8)), tag="a2")
-            SG(r("fk" + h), ("f" + h,), ("cu" + h, c8), 64, "fk")
-            P([mm(r(pE, 0, c(64, 68)), r("KU", c(128 * k, 128 * k + 128)), r("fk" + h, c(k, 64, 16)), k == 0, k == 15) for k in range(16)], "u")
+            P([mm(r(pA, c(64 * k, 64 * k + 64)), r(m), al) for k, m in enumerate(("mS", "mF", "mG"))], "lists")
+            tt(r("M" + h), al, r(pA, c(0, 64)), Op.mult, "l")
+            tt(r("Xi" + h, c(0, 64)), r("M" + h), r(pA, c(64, 128)), Op.add, "l")
+            tt(r("Xi" + h, c(64, 128)), r("M" + h), r(pA, c(128, 192)), Op.add, "l")
+            offsets(h, "l2")
+            P([mm(r(pA, c(192, 256)), r("SmI"), al)], "keep")
+            gathers(h, "f", "e", win, 1)
+            pK, pU, E = r(pA, c(256, 320)), r(pA, c(320, 384)), r(pE, A_, c(0, 16))
+            P([mm(pU, r("I5"), r("CKU"), True, False)] + sums(pU, "ZU", "f" + h, range(16), False, True), "u")
+            P(sums(E, "Z1", "ab" + h, range(EARLY), True, False), "key1e")
+            P(sums(E, "Z1", "ab" + h, range(EARLY, 16), False, True), "key1")
+            S(r("pv" + h), E, "ring")
+            P([mm(pK, r("mI"), r("CK1"), True, False), mm(pK, r("I32"), r("pv" + h), False, False)], "k1")
+            tt(r("cb" + h, A_, c(1, 15)), r("pv" + h, A_, c(0, 14)), r(pE, A_, c(2, 16)), Op.is_lt, "a")
+            tt(r("cb" + h, A_, c(0, 16, 15)), r("pv" + h, A_, c(15, 13, -1)), r("pv" + h, A_, c(1, None, -1)), Op.is_lt, "a")
+            P([mm(pK, r("n2I"), r("cb" + h), False, True)], "k2")
+            scan(r("MU" + h, c(0, 64)), r("SMa"), pK, Op.add, Op.max, "a2")
+            tt(r("ne" + h), r("MU" + h, c(0, 64)), pK, Op.not_equal, "a2")
+            scan(r("MU" + h, c(64, 128)), r("ne" + h), pU, Op.mult, Op.max, "a2")
+            ts(r("cc", hh), r("MU" + h, c(15, 128, 16)), 1023, AND, tag="a2")
+            cp(r("cu" + h, c(0, 8)), r("cc", hh), "a2")
+            P([mm(r(pW, c(0, 256)), r("mI"), r("CA"), True, False)], "wc")
             for k in (0, 64):
-                SG(r("mk" + h, c(k, k + 64)), ("tabe", c(k, k + 32)), ("cu" + h, c4), 64, "mask")
-            tt(r("pr" + h), r("mk" + h), r(pA, c(192, 320)), Op.mult, n=128, tag="a3")
-            P([mm(r(pW, c(0, 256)), r("mI"), r("CA"), True, False), mm(r(pW, c(0, 128)), r("BO"), r("pr" + h), False, False),
+                tt(r("pr" + h, c(k, k + 64)), r("tab", c(k, k + 64), ind=("cu" + h, c4)), al, Op.mult, "a3")
+            P([mm(r(pW, c(0, 128)), r("BO"), r("pr" + h), False, False),
                mm(r(pW, c(128, 192)), r("BO3"), r("pr" + h, c(0, 64)), False, False),
-               mm(r(pW, c(192, 256)), r("BO2"), r("pr" + h, c(64, 128)), False, True)], "wl", 100)
-            cp(r("ui" + h, c4), r(pE, 0, c(64, 68)), tag="o")
-            ts(r("uq" + h, c4), r("ui" + h, c4), 2046, AND, tag="o")
-            cp(r("uu" + h, c4), r("uq" + h, c4), tag="o")
-            SG(r("B" + h), ("stock",), ("uu" + h, c4), 64, "B")
-            tt(r("X" + h, c(0, 64)), r("B" + h), r(pW, c(0, 64)), Op.mult, tag="m")
-            tt(r("X" + h, c(64, 128)), r("B" + h), r(pW, c(64, 128)), Op.mult, tag="m")
-            tt(r("Xi" + h), r("X" + h), r(pW, c(128, 256)), Op.add, n=128, tag="m")
-            ts(r("Xs" + h), r("Xi" + h), 5, SAR, 4095, AND, n=128, tag="m")
-            cp(r("lu" + h), r("Xs" + h), n=128, tag="m")
-            gathers(h, "y", "d", "gy", "gz", CH2[hh])
-            P(sums(r(pW, c(448, 512)), "K2", "ab" + h, "CK2"), "key2")
-            ts(r("tf" + h), r("Ms" + h, last), -0.5, Op.mult, tag="pre")
-            ts(r("c2" + h, c4), r("cc" + h, c4), 2.0, Op.mult, tag="pre")
-            ts(r("rs" + h, c4), r("ui" + h, c4), 1, SAR, 31, AND, tag="pre")
-            ts(r("rs" + h, c8), r("ui" + h, c4), 14, AND, tag="pre")
-            tt(r("FI" + h, c8), r("rs" + h, c4), r("RC", c4), Op.add, tag="pre")
-            tt(r("sb" + h, c4), r("rs" + h, c8), r("RC", c8), Op.add, tag="pre")
-            scan(r("m2" + h), r(pW, c(448, 512)), "b")
-            tt(r("ng" + h), r("m2" + h, last), r("tf" + h), Op.is_ge, tag="b")
-            ts(r("FI" + h, c4), r("m2" + h, last), 1023, AND, tag="b")
-            tt(r("FI" + h, c(12, 16)), r("c2" + h, c4), r("ng" + h), Op.add, tag="b")
-            tt(r("FI" + h, c(8, 12)), r("sb" + h, c4), r("ng" + h), Op.add, tag="b")
-            cp(r("FU" + h), r("FI" + h), tag="b2")
-            SG(r("mx" + h), ("Tx",), ("FU" + h, c(12, 16)), 64, "mask2")
-            SG(r("gp" + h), ("Tg",), ("FU" + h, c(12, 16)), 64, "mask2")
-            V(150, "tensor_tensor", "w", out=r("bj" + h), in0=r("ohJ", ind=("FU" + h, c4)), in1=r("B" + h), op=Op.mult)
-            P([mm(r(pW, c(256, 320)), r("BO"), r("bj" + h), True, False), mm(r(pW, c(256, 320)), r("nI"), al, False, True)], "bj")
-            tt(r("dl" + h), r("mx" + h), r(pA, c(320, 384)), Op.mult, tag="w")
-            P([mm(r(pW, c(320, 384)), r("mI"), al, True, False), mm(r(pW, c(320, 384)), r("ISh"), r("dl" + h), False, True)], "R", 150)
-            tt(r("Y" + h), r("gp" + h), r(pW, c(256, 320)), Op.mult, tag="w")
-            tt(r("snd" + h), r("Y" + h), r(pW, c(320, 384)), Op.add, tag="w")
-            sn = add("G", 300, [("remote_dma", dict(to=LAND[t + 1] + h, in_=r("snd" + h)))], kind="send", tag="%d%d" % (t, hh))
-            add("R", 2300, [], kind="recv", tag="%d%d" % (t, hh), pre=[sn], extra=[(LAND[t + 1] + h, 0, 64, True)])
-            V(150, "tensor_scalar", "nr", out=r("hd" + h), in0=r("d" + h, ind=("FU" + h, c4)), scalar1=0.5, scalar2=-0.25, op0=Op.mult, op1=Op.add)
-            V(150, "tensor_tensor", "nr", out=r("nr" + h), in0=r("y" + h, ind=("FU" + h, c4)), in1=r("hd" + h), op=Op.add)
-        for hh in range(H):
-            h = HALF[0] = str(hh)
-            V(240, "tensor_copy", "sr", out=r("rec", c(2048 * hh, 2048 * hh + 2048), ind=("FU" + h, c(4, 8))), in_=r("nr" + h))
+               mm(r(pW, c(192, 256)), r("BO2"), r("pr" + h, c(64, 128)), False, True)], "wl")
+            S(r("B" + h), r("stock", c(512, 1536), ind=("cu" + h, c8)), "B", bias=-2048.0)
+            tt(r("X" + h, c(0, 64)), r("B" + h), r(pW, c(0, 64)), Op.mult, "m")
+            tt(r("X" + h, c(64, 128)), r("B" + h), r(pW, c(64, 128)), Op.mult, "m")
+            tt(r("Xi" + h), r("X" + h), r(pW, c(128, 256)), Op.add, "m")
+            offsets(h, "m")
+            gathers(h, "y", "d", win, 3)
         HALF[0] = ""
-        if t + 1 < NV:
-            pa = r("pE1", 0, c(116, 120))
-            P([mm(pa, r("on16"), r("ng0"), True, False), mm(pa, r("on16"), r("ng1"), False, True)], "A")
-            V(64, "tensor_reduce", "A", out=r("Gs"), in_=pa, axis=AxisListType.X, op=Op.add)
-            cp(r("Gi", c(0, 1)), r("Gs"), tag="A")
-            ts(r("Ga", c(0, 1)), r("Gi", c(0, 1)), 31, AND, tag="A")
-            ts(r("A32"), r("Ga", c(0, 1)), 32.0, Op.mult, tag="A")
-            ts(r("CA", c(128, 256)), r("onh"), r("A32"), Op.mult, n=128, tag="CA")
+        ts(r("r31"), r("cc", A_, c8), 31, AND, tag="pre")
+        tt(r("FI", A_, c8), r("r31"), r("RC"), Op.add, "pre")
+        ts(r("r7"), r("cc", A_, c8), 7, AND, tag="pre")
+        if not end:
+            P([mm(r("pC", c(0, 1)), r("onh"), r("c48", c(0, 1)), True, False)], "A0")
         for hh in range(H):
             h = HALF[0] = str(hh)
-            V(240, "tensor_copy", "ss", out=r("stock", c(1024 * hh, 1024 * hh + 1024), ind=("FU" + h, c(8, 12))), in_=r("snd" + h))
+            al = r(LAND[t] + h)
+            pA, pW, pE = "pA" + h, "pW" + h, "pE" + h
+            k2, R, ng = r(pW, c(448, 512)), r(pE, A_, c(32, 48)), c(4 * hh, 4 * hh + 4)
+            P([mm(k2, r("mI"), r("CK2"), True, False)] + sums(k2, "Z2", "ab" + h, range(EARLY), False, False), "key2e")
+            P(sums(k2, "Z2", "ab" + h, range(EARLY, 16), False, True), "key2")
+            scan(r("m2" + h), r("SMi"), k2, Op.add, Op.min, "b")
+            tt(r("ng", ng), r("m2" + h, last), r("MU" + h, last), Op.is_ge, "b")
+            ts(r("FI", hh, c4), r("m2" + h, last), 1023, AND, tag="b")
+            tt(r("FI", hh, c12), r("cc", hh, c4), r("ng", ng), Op.add, "b")
+            cp(r("FU" + h, c(0, 12)), r("FI", hh), "b2")
+            if not end:
+                P([mm(r("pC", c(0, 1)), r("onh"), r("ng", c(k, k + 1)), False, k == 7) for k in range(4 * hh, 4 * hh + 4)], "A")
+            S(r("mx" + h), r("tab", c(192, 256), ind=("FU" + h, c12)), "mx")
+            S(r("gp" + h), r("tab", c(128, 192), ind=("FU" + h, c12)), "gp")
+            tt(r("bj" + h), r("ohJ", ind=("FU" + h, c4)), r("B" + h), Op.mult, "w")
+            P([mm(r(pW, c(256, 320)), r("nI"), al, True, False), mm(r(pW, c(256, 320)), r("BO"), r("bj" + h), False, True)], "bj")
+            tt(r("dl" + h), r("mx" + h), r(pA, c(192, 256)), Op.mult, "w")
+            P([mm(R, r("mI"), al, True, False)] + [mm(R, r("mI"), r("C2k"), False, False)] * end + [mm(R, r("ISh"), r("dl" + h), False, True)], "R")
+            tt(r("Y" + h), r("gp" + h), r(pW, c(256, 320)), Op.mult, "w")
+            new = r(("nw" if end else "snd") + h)
+            tt(new, r("Y" + h), R, Op.add, "w")
+            sn = add("G", [("remote_dma", dict(to=LAND[t + 1] + h, in_=new))], kind="send", tag="%d%d" % (t, hh), dur=300)
+            add("R", [], kind="recv", tag="%d%d" % (t, hh), dur=0, pre=[sn], extra=[(LAND[t + 1] + h, 0, 64, True)])
+            if not end:
+                S(r("Rs" + h), R, "Rs", bias=2048.0)
+            S(r("hd" + h), r("d" + h, ind=("FU" + h, c4)), "hd", scale=0.5, bias=-0.25)
+            tt(r("nr" + h), r("y" + h, ind=("FU" + h, c4)), r("hd" + h), Op.add, "nr")
+            w = r("rec2", ind=("FU" + h, c8)) if end and hh == 0 else r("rec", c(2048 * hh, 2048 * hh + 2048), ind=("FU" + h, c8))
+            cp(w, r("nr" + h), "sr")
+            if hh == 0 and not end:
+                S(r("rec", c(4096, 4128)), r("rec", c(0, 32)), "mirror")
+        HALF[0] = ""
+        if not end:
+            S(r("nq"), r("pC", c(0, 1)), "nq", scale=-1.0, bias=15.75)
+            S(r("Acol"), r("pC", c(0, 1)), "nq", AF.Identity, bias=r("nq"))
+        for hs in ([[0], [1]] if end else [[0, 1]]):
+            k = c(4 * hs[0], 4 * hs[-1] + 4)
+            HALF[0] = str(hs[0]) if end else ""
+            P([mm(r("pS", k), r("mI"), r("RS", k), True, False)] + [
+                mm(r("pS", c(4 * hh, 4 * hh + 4)), r("I5" if hh else "nI5"), r("ng", c(4 * hh, 4 * hh + 4)), False, hh == hs[-1]) for hh in hs], "sl")
+            tt(r("SI", k), r("r7", k), r("pS", k), Op.add, "sl")
+            cp(r("SU", k), r("SI", k), "sl")
+            for hh in hs:
+                h = HALF[0] = str(hh)
+                w = r("stock", c(1024 * hh, 1024 * hh + 1024), ind=("SU", c(4 * hh, 4 * hh + 4)))
+                if end:
+                    cp(w, r("nw" + h), "ss")
+                else:
+                    tt(w, r("Y" + h), r("Rs" + h), Op.add, "ss")
     for hh in range(H):
         h = HALF[0] = str(hh)
-        dma("Y", r("yx", c(2048 * hh, 2048 * hh + 2048)), r("rec", c(2048 * hh, 2048 * hh + 2048)), 3000, "store")
-        S([512], [dict(out=r("po" + h), in_=r("stock", c(1024 * hh, 1024 * hh + 1024, 2)), func=AF.Copy, bias=2048.0)], "po")
-        dma("Y", r("yp", c(512 * hh, 512 * hh + 512)), r("po" + h), 2500, "store")
-        ts(r("yo" + h), r("le" + h), 2048.0, Op.add, tag="yo")
-        dma("Y", r("yw", c(64 * hh, 64 * hh + 64)), r("yo" + h), 2000, "store")
+        dma("Y", r("yx", c(2048 * hh, 2048 * hh + 2048)), r("rec", c(2048, 4096)) if hh else r("rec2"), 3000, "store")
+        dma("Y", r("yp", c(512 * hh, 512 * hh + 512)), r("stock", c(512 + 512 * hh, 1024 + 512 * hh)), 2500, "store")
+        dma("Y", r("yw", c(64 * hh, 64 * hh + 64)), r("le" + h), 2000, "store")
 
 
 def ways():
     n = len(NODES)
     succ = [[] for _ in range(n)]
     for i, x in enumerate(NODES):
-        for p in x["preds"]:
+        for p in x["preds"] + x["after"]:
             succ[p].append(i)
     way = [0.0] * n
     for i in range(n - 1, -1, -1):
-        way[i] = NODES[i]["dur"] + max([way[j] + 110.0 for j in succ[i]], default=0.0)
+        way[i] = NODES[i]["dur"][0] + max([way[j] + 100.0 for j in succ[i]], default=0.0)
     return succ, way
+
+
+def busy(x, d):
+    return 100.0 if x["kind"] == "dma" else 0.0 if x["kind"] == "recv" else d
 
 
 def schedule(bonus, sw):
     succ, way = sw
     n = len(NODES)
+    w1, w2 = MODELS[0][6:]
     prio = [way[i] + bonus.get(NODES[i]["key"], 0) for i in range(n)]
     look = {q: bonus.get("look" + q, 0) for q in "VSPGYR"}
-    left = [len(x["preds"]) for x in NODES]
+    left = [len(x["preds"]) + len(x["after"]) for x in NODES]
     rt = [0.0] * n
     ready = {}
     for i in range(n):
@@ -414,25 +480,44 @@ def schedule(bonus, sw):
         s = max(s, rt[i])
         ready[e].remove(i)
         x = NODES[i]
-        free[e] = s + (100.0 if x["kind"] == "dma" else 0.0 if x["kind"] == "recv" else x["dur"])
-        x["t0"], x["t1"] = s, s + x["dur"]
+        free[e] = s + busy(x, x["dur"][0])
+        x["t0"], x["t1"] = s, s + x["dur"][0]
         end = max(end, x["t1"])
         order.append(i)
         for j in succ[i]:
             left[j] -= 1
-            rt[j] = max(rt[j], x["t1"] + (60.0 if NODES[j]["eng"] == e else 110.0))
+            rt[j] = max(rt[j], x["t1"] + (0.0 if i in NODES[j]["after"] else w1 if NODES[j]["eng"] == e else w2))
             if left[j] == 0:
                 ready.setdefault(NODES[j]["eng"], []).append(j)
     return order, end
+
+
+def replay(order, k):
+    w1, w2 = MODELS[k][6:]
+    free, t1 = {}, [0.0] * len(NODES)
+    for i in order:
+        x = NODES[i]
+        e, d = x["eng"], x["dur"][k]
+        s = free.get(e, 0.0)
+        for p in x["preds"]:
+            s = max(s, t1[p] + (w1 if NODES[p]["eng"] == e else w2))
+        t1[i] = s + d
+        free[e] = s + busy(x, d)
+    return max(t1)
 
 
 def search(tries, seed):
     rnd = np.random.RandomState(seed)
     sw = ways()
     keys = sorted({x["key"] for x in NODES})
+
+    def value(C):
+        o, v = schedule(C, sw)
+        return v + sum(replay(o, k) for k in range(1, len(MODELS)))
+
     B = {q: 1500 for q in keys if q.endswith("0") and q[0] != "s"}
-    B.update({"A": 6000, "sr0": 5000, "sr1": 5000, "ss0": -9000, "ss1": -9000, "set": -3000, "lookS": 50, "lookV": 100})
-    best, end = schedule(B, sw)
+    B.update({"ss0": -5000, "ss1": -5000, "set": -3000, "lookS": 50, "lookV": 100})
+    end = value(B)
     steps = (-8000, -4000, -2000, -1000, -500, 500, 1000, 2000, 4000, 8000)
     for _ in range(tries):
         C = dict(B)
@@ -442,9 +527,9 @@ def search(tries, seed):
                 C["look" + "VSP"[k % 3]] = (0, 50, 100, 200, 300, 500)[rnd.randint(6)]
             else:
                 C[keys[k]] = steps[rnd.randint(10)] + (C.get(keys[k], 0) if rnd.randint(2) else 0)
-        o, v = schedule(C, sw)
+        v = value(C)
         if v <= end:
-            best, end, B = o, v, C
+            end, B = v, C
     return schedule(B, sw)[0]
 
 
@@ -468,7 +553,7 @@ def plan(order):
         clk = dict(K) if kind != "recv" else {}
         if kind == "comp":
             sm = "s" + e
-            v = cnt[sm] = cnt.get(sm, 0) + (1 if x["calls"][0][0] == "matmul" else len(x["calls"]))
+            v = cnt[sm] = cnt.get(sm, 0) + 1
             for a, b in comp.get(e, {}).items():
                 clk[a] = max(clk.get(a, 0), b)
             comp[e] = clk
@@ -509,9 +594,7 @@ def rank_program(g, core, T, topo):
             g.remote_dma(out_ap=T[kw["to"]][:], in_ap=ap(T, kw["in_"]), remote_sem=T.sem["r" + x["tag"]], local_sem=T.sem["l" + x["tag"]],
                          pid=pid, routing_id=rid, dma_engine_mask=sum(1 << e for e in topo.engines(core, dst)[:8]))
             continue
-        k = len(x["calls"])
         for m, kw in x["calls"]:
-            k -= 1
             kw = {a: (ap(T, b) if isref(b) else b) for a, b in kw.items()}
             if m == "memset":
                 ins = q.memset(kw["out"], kw["value"])
@@ -521,15 +604,14 @@ def rank_program(g, core, T, topo):
                 ins = q.matmul(kw["out"], kw["lhsT"], kw["rhs"], kw["start"], kw["stop"])
             elif m == "iota":
                 ins = q.iota(kw.pop("out"), **kw)
+            elif m == "affine_select":
+                ins = q.affine_select(**kw)
             elif m == "activation":
                 ins = q.activation(**kw)
             else:
                 ins = {"tensor_copy": q.tensor_copy, "tensor_tensor": q.tensor_tensor, "tensor_scalar": q.tensor_scalar,
-                       "tensor_reduce": q.tensor_reduce, "tensor_tensor_scan": q.tensor_tensor_scan}[m](**kw)
-            if x["kind"] == "dma":
-                ins.then_inc(T.sem[x["tok"][0]], 16)
-            elif m != "matmul" or k == 0:
-                ins.then_inc(T.sem[x["tok"][0]], 1)
+                       "tensor_tensor_scan": q.tensor_tensor_scan}[m](**kw)
+        ins.then_inc(T.sem[x["tok"][0]], 16 if x["kind"] == "dma" else 1)
     for sm in SEMAPHORES:
         if KNOWG.get(sm, 0) < FINAL[sm]:
             g.wait_ge(T.sem[sm], FINAL[sm])

@@ -4,11 +4,25 @@ from concourse.mybir import AluOpType, ActivationFunctionType
 Op = AluOpType
 AF = ActivationFunctionType
 NV, STEP, H = 4, 3, 2
-CH = {1: ([16, 16, 16, 16], [16, 16, 16, 8, 8], [16, 16, 16, 8, 8]),
-      3: ([16, 16, 16, 16], [16, 16, 16, 8, 8], [16, 16, 16, 8, 8])}
-EARLY = 8
-TRIES = 1500
-SEED = 1
+CH = {q: ([16, 16, 16, 16], [16, 16, 16, 8, 8], [16, 16, 16, 8, 8]) for q in ("f0", "f1", "y0", "y1")}
+OWN = []
+SOLO = []
+SEL = dict(cb="V2", pr="S", nr="V", sp=1, own=["fa1", "ya0"], dl="V", fu="01", ch={q: ([12, 20, 20, 12],) * 3 for q in CH})
+RELU = []
+OPT = {"cb": "V2", "pr": "V", "nr": "V", "sp": 0}
+ORDER = {
+    "V": "ee0 ed0 ea0 eb0 ec0 M1 Xg1 Xf1 s11 u11 fa1 ea1 eb1 ec1 max0 cck0 ne0 cuk0 sel0 ccu0 ed1 cuu0 pr0 ee1 Xy0 Xz0 Xl0 s30 u30 ya0 da0 max1 cck1 ne1 cuk1 sel1 dc0 db0 ccu1 pr1 cuu1 dd0 de0 Xy1 Xz1 Xl1 s31 r31 u31 r7 rl min0 ng0 J0 co0 FU0 bj0 da1 dl0 Y0 db1 new0 dc1 dd1 de1 nr0 SI0 sr0 min1 ng1 J1 co1 FU1 bj1 dl1 nr1 Y1 +M0 new1 SU0 +Xg0 +Xf0 sr1 +s10 SI1 +u10 SU1 ss0 ss1",
+    "S": "fb0 fc0 |ed0 |eb0 |ea0 |ec0 |ee0 fb1 pv0 fc1 cb0 fd1 |ea1 |eb1 pb0 pa0 |ec1 B0 |ed1 |ee1 pv1 yd0 cb1 yc0 yb0 pa1 pb1 |da0 |dc0 |db0 B1 |dd0 |de0 ya1 yb1 mx0 gp0 yc1 yd1 |db1 |da1 |dc1 |dd1 |de1 hd0 rep0 Rs0 mx1 hd1 gp1 nq Acol Rs1 +fd0 +fa0",
+    "P": "lists1 U0 Ea0 Eb0 Ec1 Kc0 D0 keep1 Ra0 Ka0 Kb0 U1 W0 Kc1 Ea1 Eb1 Fc0 D1 Ka1 Kb1 W1 Fa0 Fb0 Sl0 Ba0 Bb0 A0 Fc1 Rb0 Fa1 Fb1 Ba1 A1 Ra1 Bb1 +lists0 Rb1 +Wc0 Sl1 +Ac +Wc1 +keep0 +Ec0",
+}
+ORDER = {
+    "V": "ea0 eb0 ec0 ed0 M1 Xf1 Xg1 s11 u11 fa1 cb0 cw0 ea1 max0 eb1 ne0 cck0 sel0 cuk0 ec1 ccu0 pr0 cuu0 ed1 Xz0 Xy0 Xl0 s30 u30 cb1 ya0 cw1 da0 max1 db0 ne1 cck1 sel1 cuk1 ccu1 dc0 cuu1 pr1 dd0 r31 Xy1 Xz1 r7 Xl1 s31 u31 min0 rl ng0 J0 co0 FU0 FV0 bj0 dl0 da1 Y0 new0 db1 dc1 dd1 nr0 sr0 min1 ng1 J1 co1 FU1 FV1 bj1 dl1 SI0 nr1 Y1 new1 sr1 SU0 +M0 SI1 +Xg0 +Xf0 +s10 +u10 SU1 ss0 ss1",
+    "S": "fd0 |ea0 |eb0 |ec0 |ed0 pv0 fb1 fc1 |ea1 fd1 |eb1 pb0 pa0 |ec1 B0 |ed1 pv1 dW0 yb0 yd0 |da0 yc0 |db0 pa1 pb1 B1 |dc0 |dd0 ya1 yb1 gp0 yc1 hd0 |da1 yd1 |db1 |dc1 |dd1 dW1 hd1 gp1 nq Acol Rs0 rep0 Rs1 +fa0 +fb0 +fc0",
+    "P": "E00 lists1 Ea0 E01 Eb0 Ec0 Ed0 Ub0 Kc0 Ka0 keep1 Kb0 U01 Ua1 Wc0 Ea1 Ub1 Kc1 W0 L0 Eb1 Ec1 Ed1 Ra0 Ka1 F00 Kb1 W1 L1 Fa0 Fb0 Fc0 Fd0 Sl0 F01 Ra1 Ba0 Bb0 Rb0 Fa1 A0 Fb1 Fc1 Fd1 Ba1 A1 Bb1 Rb1 +lists0 Sl1 +keep0 +Ac +Wc1 +U00 +Ua0",
+}
+OPT.update(SEL)
+OWN, RELU, SOLO = (SEL.get(k, []) for k in ("own", "relu", "solo"))
+CH.update(SEL.get("ch", {}))
 BIG = float(2 ** 24)
 LAND = "la lb lc ld le".split()
 EXT = {"xt": [128, 4096], "wd": [128, 128], "pd": [128, 1024], "wt": [128, 1],
@@ -34,28 +48,32 @@ bufs("sbuf", "float32", [128, 2048], "stock")
 bufs("sbuf", "int32", [128, 1024], "pdi")
 bufs("sbuf", "int32", [128, 128], "wdi")
 bufs("sbuf", "int32", [128, 1], "wti")
-bufs("sbuf", "bfloat16", [128, 144], "Z1 Z2 ZU", "PB")
+bufs("sbuf", "bfloat16", [128, 144], "Z1 Z2 ZU N1 N2", "PB")
 bufs("sbuf", "bfloat16", [128, 1024], "ohJ")
 bufs("sbuf", "bfloat16", [128, 256], "tab")
-bufs("sbuf", "float16", [128, 4, 16], "CK1 CK2 CKU")
-bufs("sbuf", "float32", [128, 4, 16], "CKa CKb CKc")
+bufs("sbuf", "float16", [128, 4, 16], "CK1 CK2 CKU C8k")
+bufs("sbuf", "float32", [128, 4, 16], "CKa CKb")
 bufs("sbuf", "int32", [128, 4, 16], "CKi CKj")
-bufs("sbuf", "int32", [128, 128], "cD cM cK cT1 cT2 cT3", "PI")
+bufs("sbuf", "int32", [128, 128], "cD cM cT1 cT3", "PI")
 bufs("sbuf", "int32", [128, 256], "tabi tabj", "PI")
 bufs("sbuf", "int32", [128, 16], "oji ojk", "PI")
-bufs("sbuf", "int32", [128, 8], "RC r31 r7 SI", "PI")
+bufs("sbuf", "int32", [128, 8], "r31 r7 SI", "PI")
+bufs("sbuf", "float32", [128, 8], "RC RD PD", "PF")
+bufs("sbuf", "int32", [128, 1], "q0 q1", "PI")
+bufs("sbuf", "float32", [128, 1], "g0 g1 f2", "PF")
+bufs("sbuf", "uint16", [128, 8], "PERM", "PU")
 bufs("sbuf", "uint16", [128, 8], "SU", "PU")
 bufs("sbuf", "float32", [128, 1], "wcol Acol", "PF")
 bufs("sbuf", "bfloat16", [128, 1], "nq", "PB")
-bufs("sbuf", "float32", [128, 128], "ISh I32", "PF")
+bufs("sbuf", "float32", [128, 128], "ISh", "PF")
 bufs("sbuf", "float32", [128, 64], "SMa SMi", "PF")
-bufs("sbuf", "float16", [128, 128], "BO mI nI mS mP tA tB I3 I2 S3 S2 mF mG SmI BO3 BO2 onh n2I I5 nI5", "PH")
-bufs("sbuf", "float16", [128, 256], "CA", "PH")
+bufs("sbuf", "float16", [128, 128], "BO mI nI mS tA I3 I2 mF mG SmI BO3 BO2 onh nB I5 nI5 I2k", "PH")
+bufs("sbuf", "float16", [128, 128], "CA", "PH")
 bufs("sbuf", "float16", [128, 64], "C2k", "PH")
 bufs("sbuf", "float16", [128, 8], "RS ng c48", "PH")
 bufs("sbuf", "float16", [128, 64], "la lb lc ld snd", halves=True)
 bufs("sbuf", "float32", [128, 64], "le nw", halves=True)
-bufs("sbuf", "float16", [128, 64], "bj", "PH", True)
+bufs("sbuf", "float16", [128, 64], "bj hq", "PH", True)
 bufs("sbuf", "float16", [128, 128], "pr", "PH", True)
 bufs("sbuf", "float32", [128, 64], "M B dl Y Rs hd ne", "PF", True)
 bufs("sbuf", "float32", [128, 128], "X", "PF", True)
@@ -65,14 +83,15 @@ bufs("sbuf", "int32", [128, 2, 8], "cc")
 bufs("sbuf", "int32", [128, 2, 12], "FI")
 bufs("sbuf", "uint16", [128, 128], "lu", "PU", True)
 bufs("sbuf", "uint16", [128, 16], "cu FU", "PU", True)
-bufs("sbuf", "bfloat16", [128, 64], "mx gp", "PB", True)
-bufs("sbuf", "bfloat16", [128, 4, 256], "ab f", halves=True)
-bufs("sbuf", "bfloat16", [128, 1024], "e y d", halves=True)
-bufs("sbuf", "float32", [128, 4, 16], "pv", halves=True)
+bufs("sbuf", "bfloat16", [128, 64], "mx gp hb yj", "PB", True)
+bufs("sbuf", "bfloat16", [128, 128], "mk", "PB", True)
+bufs("sbuf", "bfloat16", [128, 1024], "ab f e y d", halves=True)
+bufs("sbuf", "float16", [128, 4, 18], "pv", halves=True)
 bufs("sbuf", "float16", [128, 4, 16], "cb", halves=True)
 bufs("psum", "float32", [128, 512], "pA pW", halves=True)
 bufs("psum", "float32", [128, 4, 128], "pE", halves=True)
-bufs("psum", "float32", [128, 512], "pC pS")
+bufs("psum", "float32", [128, 512], "pC pD")
+bufs("sbuf", "bfloat16", [128, 128], "bI nbI", "PB")
 A_ = slice(None)
 
 
@@ -98,18 +117,19 @@ def isref(x):
     return isinstance(x, tuple) and len(x) == 4 and x[0] == "ref"
 
 
-def span(name, ix):
+def cols(name, ix):
     shape = (SCRATCH[name][1] if name in SCRATCH else EXT[name])[1:]
-    lo = hi = 0
-    stride = n = 1
+    x, stride = 1, 1
     for k in range(len(shape) - 1, -1, -1):
         s = ix[k] if k < len(ix) else A_
         q = [s] if isinstance(s, int) else range(*s.indices(shape[k]))
-        lo += min(q[0], q[-1]) * stride
-        hi += max(q[0], q[-1]) * stride
+        x = (((1 << len(q)) - 1) << q[0]) if stride == 1 and len(q) > 1 and q[1] == q[0] + 1 else sum(x << (j * stride) for j in q)
         stride *= shape[k]
-        n *= len(q)
-    return lo, hi + 1, n
+    return x
+
+
+def size(ref):
+    return bin(cols(ref[1], ref[2])).count("1")
 
 
 def ap(T, ref):
@@ -120,8 +140,8 @@ def ap(T, ref):
 NODES = []
 ACC = {}
 BANK = {}
-HALF = [""]
-MODELS = [(1.04, 1.56, 3.8, 25, 0.55, 2300, 60, 110), (0.9, 1.4, 3.0, 40, 0.8, 2500, 100, 150)]
+AT = {"visit": -1, "half": ""}
+MODELS = [(1.04, 1.56, 3.8, 25, 0.55, 2300, 60, 110)]
 
 
 def cost(eng, calls, model):
@@ -129,10 +149,10 @@ def cost(eng, calls, model):
     t = 0.0
     for m, kw in calls:
         refs = [v for v in kw.values() if isref(v)]
-        n = max(span(v[1], v[2])[2] for v in refs if v[3] is None)
-        dts = [SCRATCH[v[1]][2] for v in refs if span(v[1], v[2])[2] > 1]
+        n = max(size(v) for v in refs if v[3] is None)
+        dts = [SCRATCH[v[1]][2] for v in refs if size(v) > 1]
         if m == "matmul":
-            t += max(64, span(kw["rhs"][1], kw["rhs"][2])[2]) * pe * (4 if SCRATCH[kw["rhs"][1]][2] == "float32" else 1)
+            t += max(64, size(kw["rhs"])) * pe * (4 if SCRATCH[kw["rhs"][1]][2] == "float32" else 1)
         elif eng == "G":
             t += 150 + 2 * cy * n
         elif kw["out"][3] is not None:
@@ -148,61 +168,61 @@ def cost(eng, calls, model):
     return t + (40 if eng == "P" else 0)
 
 
-def add(eng, calls, kind="comp", tag="", dur=None, extra=(), pre=()):
+def add(eng, calls, tag, kind="comp", dur=None, extra=(), pre=()):
     n = len(NODES)
     preds, after = set(pre), set()
     touch = list(extra)
     for m, kw in calls:
         for k, v in kw.items():
             if isref(v):
-                touch.append((v[1],) + span(v[1], v[2])[:2] + (k == "out",))
+                touch.append((v[1], cols(v[1], v[2]), k == "out"))
                 if v[3] is not None:
-                    touch.append((v[3][0],) + span(v[3][0], (v[3][1],))[:2] + (False,))
-    for name, lo, hi, w in touch:
+                    touch.append((v[3][0], cols(v[3][0], (v[3][1],)), False))
+    for name, x, w in touch:
         psum = name in SCRATCH and SCRATCH[name][0] == "psum"
         if psum and eng == "P":
             after.add(BANK.get(name, n))
             BANK[name] = n
         keep = []
         for q in ACC.setdefault(name, []):
-            m, me, a, b, mw = q
+            m, me, a, mw = q
             if m != n and psum and (me != eng or eng == "P"):
                 if me != eng:
                     preds.add(m)
                 keep.append(q)
                 continue
-            if m != n and a < hi and lo < b and (w or mw):
+            if m != n and a & x and (w or mw):
                 preds.add(m)
-                if w and lo <= a and b <= hi:
+                if w and a & x == a:
                     continue
             keep.append(q)
-        keep.append((n, eng, lo, hi, w))
+        keep.append((n, eng, x, w))
         ACC[name] = keep[-40:] if psum else keep
     durs = [cost(eng, calls, M) if dur is None else M[5] if kind == "recv" else dur for M in MODELS]
-    NODES.append({"eng": eng, "dur": durs, "calls": calls, "kind": kind, "tag": tag, "preds": sorted(preds),
-                  "after": sorted(after - preds - {n}), "key": tag + HALF[0]})
+    NODES.append({"eng": eng, "dur": durs, "calls": calls, "kind": kind, "preds": sorted(preds), "after": sorted(after - preds - {n}),
+                  "key": tag + AT["half"], "visit": AT["visit"]})
     return n
 
 
 def V(meth, tag, **kw):
-    return add("V", [(meth, kw)], tag=tag)
+    return add("V", [(meth, kw)], tag)
 
 
 def S(out, in_, tag, func=AF.Copy, **kw):
-    return add("S", [("activation", dict(out=out, in_=in_, func=func, **kw))], tag=tag)
+    return add("S", [("activation", dict(out=out, in_=in_, func=func, **kw))], tag)
 
 
 def P(calls, tag):
-    return add("P", [("matmul", kw) for kw in calls], tag=tag)
+    return add("P", [("matmul", kw) for kw in calls], tag)
 
 
 def I(out, pattern, base, cm, **kw):
-    return add("G", [("iota", dict(out=out, pattern=pattern, base=base, channel_multiplier=cm, **kw))], tag="set")
+    return add("G", [("iota", dict(out=out, pattern=pattern, base=base, channel_multiplier=cm, **kw))], "set")
 
 
 def gcopy(out, in_, n):
     return add("G", [("affine_select", dict(out=out, in_=in_, pattern=[[0, n]], compare_op=Op.is_gt, fill=0.0, base=1,
-                                            channel_multiplier=0))], tag="gset")
+                                            channel_multiplier=0))], "set")
 
 
 def mm(out, lhsT, rhs, start=True, stop=True):
@@ -230,86 +250,110 @@ def scan(out, data0, data1, op0, op1, tag):
     return V("tensor_tensor_scan", tag, out=out, data0=data0, data1=data1, initial=0.0, op0=op0, op1=op1)
 
 
-def dma(q, out, in_, dur, tag, pre=()):
-    return add(q, [("dma_start", dict(out=out, in_=in_))], kind="dma", tag=tag, dur=dur, pre=pre)
+def dma(q, out, in_, dur, tag):
+    return add(q, [("dma_start", dict(out=out, in_=in_))], tag, kind="dma", dur=dur)
 
 
-def sums(out, Z, src, ks, start, stop):
-    return [mm(out, r(Z, c(15 - k, 143 - k)), r(src, A_, c(16 * k, 16 * k + 16)), start and k == ks[0], stop and k == ks[-1]) for k in ks]
+def sums(out, Z, src, o, e, stop):
+    return [mm(out, r(Z, c(15 - k, 143 - k)), r(src, c(64 * k, 64 * k + 64)), False, stop and k == 15) for k in range(o // 4, e // 4)]
 
 
 def piece(name, o, e):
-    if len(SCRATCH[name][1]) == 2:
-        return r(name, c(16 * o, 16 * e))
-    if e - o > 16:
-        return r(name, c(o // 16, e // 16), A_)
-    return r(name, o // 16, c(o % 16 * 16, ((e - 1) % 16 + 1) * 16))
+    return r(name, c(16 * o, 16 * e))
 
 
 def cuts(w):
-    return [(sum(w[:k]), sum(w[:k + 1])) for k in range(len(w))]
+    return [("abcdefgh"[k], sum(w[:k]), sum(w[:k + 1])) for k in range(len(w))]
 
 
-def gathers(h, a, b, win, stage):
-    s = str(stage)
-    for o, e in cuts(CH[stage][0]):
-        S(piece(a + h, o, e), r("rec", win, ind=("lu" + h, c(o, e))), "ga" + s)
-    for o, e in cuts(CH[stage][1]):
-        tt(piece(b + h, o, e), r("rec", win, ind=("lu" + h, c(64 + o, 64 + e))), piece(a + h, o, e), Op.subtract, "gb" + s)
-    for o, e in cuts(CH[stage][2]):
-        S(piece("ab" + h, o, e), piece(b + h, o, e), "ab" + s, AF.Abs)
+def gathers(h, a, b, win):
+    one, two, three = CH[a + h]
+    for k, o, e in cuts(one):
+        (cp if a + k + h in OWN else S)(piece(a + h, o, e), r("rec", win, ind=("lu" + h, c(o, e))), a + k)
+    for k, o, e in cuts(two):
+        if b + k + h in SOLO:
+            S(piece(b + h, o, e), r("rec", win, ind=("lu" + h, c(64 + o, 64 + e))), b + k)
+        else:
+            tt(piece(b + h, o, e), r("rec", win, ind=("lu" + h, c(64 + o, 64 + e))), piece(a + h, o, e), Op.subtract, b + k)
+    for k, o, e in cuts(three):
+        if b + k + h in SOLO:
+            D = r("pD", c(0, 16 * (e - o)))
+            P([mm(D, r("bI"), piece(b + h, o, e), True, False), mm(D, r("nbI"), piece(a + h, o, e), False, True)], "D" + k)
+            S(piece("ab" + h, o, e), D, "|" + b + k, AF.Abs)
+        elif b + k + h in RELU:
+            ts(piece("ab" + h, o, e), piece(b + h, o, e), 0.0, Op.max, 2.0, Op.mult, "|" + b + k)
+        else:
+            S(piece("ab" + h, o, e), piece(b + h, o, e), "|" + b + k, AF.Abs)
 
 
-def build():
-    AND, SAR, SLR = Op.bitwise_and, Op.arith_shift_right, Op.logical_shift_right
+def abs_sums(out, Z, N, h, a, b, tag):
+    for k, o, e in cuts(CH[a + h][2]):
+        if b + k + h in RELU:
+            P(sums(out, N, b + h, o, e, False), tag + "n" + k)
+    for k, o, e in cuts(CH[a + h][2]):
+        P(sums(out, Z, "ab" + h, o, e, e == 64), tag + k)
+
+
+AND, SAR, SLR = Op.bitwise_and, Op.arith_shift_right, Op.logical_shift_right
+c4, c8, c12 = c(0, 4), c(4, 8), c(8, 12)
+LAST = c(15, 64, 16)
+
+
+def setup():
     dma("Y", r("wdi"), r("wd"), 2000, "load")
     dma("S", r("wti"), r("wt"), 2000, "load")
     dma("Y", r("rec", c(0, 2048)), r("xt", c(0, 2048)), 4300, "load")
     dma("S", r("rec", c(2048, 4096)), r("xt", c(2048, 4096)), 4300, "load")
-    dma("Y", r("pdi"), r("pd"), 5800, "loadp")
+    dma("Y", r("pdi"), r("pd"), 5800, "load")
     I(r("cD"), [[1, 128]], 0, -1)
-    I(r("cM"), [[1, 128]], 0, 0)
-    I(r("cK"), [[0, 128]], 0, 1)
+    I(r("cM"), [[-16, 8], [0, 16]], 0, 1)
     ts(r("cT3"), r("cD"), 15, AND)
     ts(r("cT1"), r("cM"), 4, SLR)
-    ts(r("cT2"), r("cK"), 4, SLR)
-    tt(r("BO"), r("cT1"), r("cT2"), Op.is_equal)
+    ts(r("BO"), r("cT1"), 0, Op.is_equal)
     ts(r("mI"), r("cD"), 0, Op.is_equal)
     ts(r("tA"), r("cT3"), 15, Op.is_equal)
     tt(r("mS"), r("tA"), r("BO"), Op.mult)
-    for o, i, k in (("I3", "mI", 3232.0), ("I2", "mI", 2080.0), ("S3", "mS", 3232.0), ("S2", "mS", 2080.0), ("nI", "mI", -1.0),
-                    ("BO3", "BO", 3232.0), ("BO2", "BO", 2080.0), ("n2I", "mI", -2.0), ("I5", "mI", 512.0), ("nI5", "mI", -512.0),
-                    ("I32", "mI", 1.0)):
-        ts(r(o), r(i), k, Op.mult)
-    tt(r("mF"), r("I3"), r("S2"), Op.add)
-    tt(r("mG"), r("I2"), r("S3"), Op.add)
-    tt(r("SmI"), r("mS"), r("mI"), Op.subtract)
+    for o, i, k in (("I3", "mI", 3232.0), ("I2", "mI", 2080.0), ("nI", "mI", -1.0),
+                    ("BO3", "BO", 3232.0), ("BO2", "BO", 2080.0), ("nB", "mI", -1.0 if OPT["cb"] == "S" else -2.0),
+                    ("I5", "mI", 512.0), ("nI5", "mI", -512.0), ("I2k", "mI", 2048.0)) + (("bI", "mI", 1.0), ("nbI", "mI", -1.0)) * bool(SOLO):
+        S(r(o), r(i), "set", scale=k)
+    for k, (o, a, b, a2, b2) in enumerate((("mF", "I3", "mI", "I2", "mS"), ("mG", "I2", "mI", "I3", "mS"),
+                                           ("SmI", "nI", "mI", "mI", "mS"), ("ISh", "mI", "mI", "mS", "nI"))):
+        x = r(("pW0", "pW1")[k % 2], c(k // 2 * 128, k // 2 * 128 + 128))
+        P([mm(x, r(a), r(b), True, False), mm(x, r(a2), r(b2), False, True)], "set")
+        S(r(o), x, "set")
     for h in "01":
         ts(r("la" + h), r("wdi", c(64 * int(h), 64 * int(h) + 64)), -2048.0, Op.add)
     ms(r("Z1"), 0.0)
-    ts(r("Z1", c(15, 143, 16)), r("BO", c(0, 128, 16)), 2048.0, Op.mult)
-    ts(r("Z2"), r("Z1"), 2.0, Op.mult)
-    ts(r("wcol"), r("wti"), 1.0 / 2048, Op.mult)
-    ts(r("ZU"), r("Z1"), r("wcol"), Op.mult)
-    ts(r("tB"), r("cT3"), 1, Op.is_equal)
-    tt(r("mP"), r("tB"), r("BO"), Op.mult)
-    tt(r("ISh"), r("mI"), r("mP"), Op.subtract)
+    cp(r("Z1", c(15, 143, 16)), r("BO", c(0, 128, 16)))
+    for o, k in (("Z2", 4096.0),) + (("N1", -1.0), ("N2", -4096.0)) * bool(RELU):
+        S(r(o), r("Z1"), "set", scale=k)
+    cp(r("wcol"), r("wti"))
+    S(r("ZU"), r("Z1"), "set", scale=r("wcol"))
     ms(r("onh"), 1.0)
     ms(r("c48"), 48.0)
     ms(r("C2k"), 2048.0)
+    ms(r("C8k"), 8192.0)
     ms(r("CA", c(0, 64)), 2080.0)
     ms(r("CA", c(64, 128)), 3232.0)
-    ms(r("CA", c(128, 256)), 0.0)
-    I(r("CKi"), [[0, 4], [1, 16]], 0, 16)
-    for o, pat, base in (("CKc", [[256, 4], [0, 16]], 1024), ("CKa", [[0, 4], [-4, 16]], 62), ("CKb", [[0, 4], [-2048, 16]], 15 * 2048)):
+    I(r("CKi"), [[16, 4], [1, 16]], 0, 64)
+    for o, pat, base in (("PD", [[64, 2], [4, 4]], 0), ("CKa", [[0, 4], [-4, 16]], 61 if OPT["cb"] == "S" else 62),
+                         ("CKb", [[0, 4], [-2048, 16]], 15 * 2048), ("RD", [[0, 2], [512, 4]], 0)):
         I(r(o), pat, base, 0, allow_small_or_imprecise_dtypes=True)
-    ts(r("CKj"), r("CKi"), 255, AND)
-    tt(r("CK2"), r("CKj"), r("CKc"), Op.add)
-    cp(r("CK1"), r("CKa"))
-    cp(r("CKU"), r("CKb"))
+    p64 = r("CKi", 0, c(0, 1))
+    ts(r("q0"), p64, 192, AND)
+    ts(r("q1"), p64, 8, SAR, 3, AND)
+    ts(r("g0"), r("q0"), 0.25, Op.mult)
+    cp(r("g1"), r("q1"))
+    ts(r("PERM"), r("PD"), r("g0"), Op.add, r("g1"), Op.add)
+    ts(r("CKj"), r("CKi"), 1023, AND)
+    ts(r("CK2"), r("CKj"), 1024.0, Op.add)
+    ts(r("f2"), r("CKj", 0, c(0, 1)), 0.5, Op.mult)
+    S(r("CK1"), r("CKa"), "set")
+    S(r("CKU"), r("CKb"), "set")
+    S(r("RC"), r("RD"), "set", AF.Identity, bias=r("f2"))
     for hh in range(H):
-        ts(r("RC", c(4 * hh, 4 * hh + 4)), r("CK2", A_, 0), -1024.0, Op.add, 2.0, Op.mult)
-        ts(r("RS", c(4 * hh, 4 * hh + 4)), r("CK2", A_, 0), 0.5, Op.mult, -512.0 * hh, Op.add)
+        S(r("RS", c(4 * hh, 4 * hh + 4)), r("RC", c4), "set", scale=0.25, bias=512.0 - 512.0 * hh)
     for o, v in (("SMa", -BIG), ("SMi", BIG)):
         ms(r(o), 0.0)
         ms(r(o, c(0, 64, 16)), v)
@@ -326,211 +370,230 @@ def build():
     for k in (16, 32, 64, 128, 256, 512):
         gcopy(r("ohJ", c(k, 2 * k)), r("ohJ", c(0, k)), k)
 
-    c4, c8, c12 = c(0, 4), c(4, 8), c(8, 12)
-    last = c(15, 64, 16)
+
+def offsets(t, h, tag):
+    ts(r("Xs" + h), r("Xi" + h), 5, SAR, 4095, AND, "s" + tag)
+    if t == 0:
+        cp(r("lu" + h), r("Xs" + h, ind=("PERM", A_)), "u" + tag)
+    else:
+        ts(r("lu" + h), r("Xs" + h, ind=("PERM", A_)), r("Acol"), Op.add, tag="u" + tag)
+
+
+def front(t, hh):
+    h = AT["half"] = str(hh)
+    win = c(0, 4096 + 32 * (t > 0))
+    al = r(LAND[t] + h)
+    pA, pW, pE, pv, cb = "pA" + h, "pW" + h, "pE" + h, "pv" + h, "cb" + h
+    P([mm(r(pA, c(64 * k, 64 * k + 64)), r(m), al) for k, m in enumerate(("mS", "mF", "mG"))], "lists")
+    tt(r("M" + h), al, r(pA, c(0, 64)), Op.mult, "M")
+    tt(r("Xi" + h, c(0, 64)), r("M" + h), r(pA, c(64, 128)), Op.add, "Xf")
+    tt(r("Xi" + h, c(64, 128)), r("M" + h), r(pA, c(128, 192)), Op.add, "Xg")
+    offsets(t, h, "1")
+    P([mm(r(pA, c(192, 256)), r("SmI"), al)] + [mm(r(pA, c(k, k + 64)), r("mI"), al) for k in (384, 448) if OPT["pr"] == "S"], "keep")
+    gathers(h, "f", "e", win)
+    pK, pU, E = r(pA, c(256, 320)), r(pA, c(320, 384)), r(pE, A_, c(0, 16))
+    P([mm(pU, r("I5"), r("CKU"), True, False)], "U0")
+    for k, o, e in cuts([32, 32]):
+        P(sums(pU, "ZU", "f" + h, o, e, e == 64), "U" + k)
+    P([mm(pK, r("mI"), r("CK1"), True, False), mm(pK, r("I5"), r("C8k"), False, False)], "Kc")
+    P([mm(E, r("nI"), r("C2k"), True, False)], "E0")
+    abs_sums(E, "Z1", "N1", h, "f", "e", "E")
+    (cp if OPT.get("pv") == "V" else S)(r(pv, A_, c(1, 17)), E, "pv")
+    if OPT["cb"] == "V2":
+        tt(r(cb, A_, c(1, 15)), r(pv, A_, c(1, 15)), r(pE, A_, c(2, 16)), Op.is_lt, "cb")
+        tt(r(cb, A_, c(0, 16, 15)), r(pv, A_, c(16, 14, -1)), r(pv, A_, c(2, 0, -1)), Op.is_lt, "cw")
+    elif OPT["cb"] == "P":
+        S(r(pv, A_, c(0, 18, 17)), r(pE, A_, c(15, None, -15)), "pw")
+        tt(r(cb), r(pv, A_, c(0, 16)), r(pv, A_, c(2, 18)), Op.is_lt, "cb")
+    else:
+        P([mm(r(pE, A_, c(16, 32)), r("mI"), r("C8k"), True, False), mm(r(pE, A_, c(16, 31)), r("mI"), r(pv, A_, c(2, 17)), False, False),
+           mm(r(pE, A_, 31), r("mI"), r(pv, A_, 1), False, False), mm(r(pE, A_, c(17, 32)), r("nI"), r(pv, A_, c(1, 16)), False, False),
+           mm(r(pE, A_, 16), r("nI"), r(pv, A_, 16), False, True)], "D")
+        if OPT["cb"] == "S":
+            S(r(cb), r(pE, A_, c(16, 32)), "cb", AF.Sign, bias=-8192.5)
+        else:
+            ts(r(cb), r(pE, A_, c(16, 32)), 8192.0, Op.is_gt, tag="cb")
+    P([mm(pK, r("I2k"), r(pv, A_, c(1, 17)), False, False)], "Ka")
+    P([mm(pK, r("nB"), r(cb), False, True)], "Kb")
+    scan(r("MU" + h, c(0, 64)), r("SMa"), pK, Op.add, Op.max, "max")
+    tt(r("ne" + h), r("MU" + h, c(0, 64)), pK, Op.not_equal, "ne")
+    scan(r("MU" + h, c(64, 128)), r("ne" + h), pU, Op.mult, Op.max, "sel")
+    for k, tag in (((c4, "k"), (c8, "u")) if OPT["sp"] else ((c(0, 8), ""),)):
+        ts(r("cc", hh, k), r("MU" + h, c(15 + 16 * k.start, 16 * k.stop, 16)), 1023, AND, tag="cc" + tag)
+        cp(r("cu" + h, k), r("cc", hh, k), "cu" + tag)
+    P([mm(r(pW, c(0, 128)), r("mI"), r("CA"), True, False)], "Wc")
+    for k, tag in ((0, "pb"), (64, "pa")):
+        if OPT["pr"] == "S":
+            S(r("mk" + h, c(k, k + 64)), r("tab", c(k, k + 64), ind=("cu" + h, c4)), tag)
+        else:
+            tt(r("pr" + h, c(k, k + 64)), r("tab", c(k, k + 64), ind=("cu" + h, c4)), al, Op.mult, tag)
+    if OPT["pr"] == "S":
+        tt(r("pr" + h), r("mk" + h), r(pA, c(384, 512)), Op.mult, "pr")
+    P([mm(r(pW, c(0, 128)), r("BO"), r("pr" + h), False, True)], "W")
+    P([mm(r(pE, 0, c(64, 128)), r("BO3"), r("pr" + h, c(0, 64))), mm(r(pE, 1, c(64, 128)), r("BO2"), r("pr" + h, c(64, 128)))], "L")
+    if OPT.get("B") == "V":
+        ts(r("B" + h), r("stock", c(512, 1536), ind=("cu" + h, c8)), -2048.0, Op.add, tag="B")
+    else:
+        S(r("B" + h), r("stock", c(512, 1536), ind=("cu" + h, c8)), "B", bias=-2048.0)
+    if OPT.get("dl") == "V":
+        S(r("M" + h), r(pA, c(192, 256)), "dW")
+    tt(r("X" + h, c(0, 64)), r("B" + h), r(pW, c(0, 64)), Op.mult, "Xy")
+    tt(r("X" + h, c(64, 128)), r("B" + h), r(pW, c(64, 128)), Op.mult, "Xz")
+    tt(r("Xi" + h), r("X" + h), r(pE, c(0, 2), c(64, 128)), Op.add, "Xl")
+    offsets(t, h, "3")
+    gathers(h, "y", "d", win)
+
+
+def back(t, hh):
+    h = AT["half"] = str(hh)
+    end = t + 1 == NV
+    al = r(LAND[t] + h)
+    pA, pW, pE = "pA" + h, "pW" + h, "pE" + h
+    k2, R, ng = r(pW, c(448, 512)), r(pE, A_, c(32, 48)), c(4 * hh, 4 * hh + 4)
+    P([mm(k2, r("mI"), r("CK2"), True, False)], "F0")
+    abs_sums(k2, "Z2", "N2", h, "y", "d", "F")
+    scan(r("m2" + h), r("SMi"), k2, Op.add, Op.min, "min")
+    tt(r("ng", ng), r("m2" + h, LAST), r("MU" + h, LAST), Op.is_ge, "ng")
+    ts(r("FI", hh, c4), r("m2" + h, LAST), 1023, AND, tag="J")
+    tt(r("FI", hh, c12), r("cc", hh, c4), r("ng", ng), Op.add, "co")
+    if h in OPT.get("fu", ""):
+        cp(r("FU" + h, c(0, 8)), r("FI", hh, c(0, 8)), "FU")
+        cp(r("FU" + h, c12), r("FI", hh, c12), "FV")
+    else:
+        cp(r("FU" + h, c(0, 12)), r("FI", hh), "FU")
+    if not end:
+        P([mm(r("pC", c(0, 1)), r("onh"), r("ng", c(k, k + 1)), False, k == 7) for k in range(4 * hh, 4 * hh + 4)], "A")
+    if OPT.get("dl") != "V":
+        S(r("mx" + h), r("tab", c(192, 256), ind=("FU" + h, c12)), "mx")
+    S(r("gp" + h), r("tab", c(128, 192), ind=("FU" + h, c12)), "gp")
+    tt(r("bj" + h), r("ohJ", ind=("FU" + h, c4)), r("B" + h), Op.mult, "bj")
+    P([mm(r(pW, c(256, 320)), r("nI"), al, True, False)], "Ba")
+    P([mm(r(pW, c(256, 320)), r("BO"), r("bj" + h), False, True)], "Bb")
+    if OPT.get("dl") == "V":
+        tt(r("dl" + h), r("tab", c(192, 256), ind=("FU" + h, c12)), r("M" + h), Op.mult, "dl")
+    else:
+        tt(r("dl" + h), r("mx" + h), r(pA, c(192, 256)), Op.mult, "dl")
+    P([mm(R, r("mI"), al, True, False)] + [mm(R, r("mI"), r("C2k"), False, False)] * end, "Ra")
+    P([mm(R, r("ISh"), r("dl" + h), False, True)], "Rb")
+    tt(r("Y" + h), r("gp" + h), r(pW, c(256, 320)), Op.mult, "Y")
+    new = r(("nw" if end else "snd") + h)
+    tt(new, r("Y" + h), R, Op.add, "new")
+    sn = add("G", [("remote_dma", dict(to=LAND[t + 1] + h, in_=new))], "send", kind="send", dur=300)
+    add("R", [], "recv", kind="recv", dur=0, pre=[sn], extra=[(LAND[t + 1] + h, cols(LAND[t + 1] + h, ()), True)])
+    if not end:
+        S(r("Rs" + h), R, "Rs", bias=2048.0)
+    w = r("rec2", ind=("FU" + h, c8)) if end and hh == 0 else r("rec", c(2048 * hh, 2048 * hh + 2048), ind=("FU" + h, c8))
+    if OPT["nr"] == "S":
+        S(r("hq" + h), r("d" + h, ind=("FU" + h, c4)), "hq", scale=0.5, bias=1535.75)
+        S(r("yj" + h), r("y" + h, ind=("FU" + h, c4)), "yj")
+        S(r("hb" + h), r("hq" + h), "hb", bias=-1536.0)
+        tt(w, r("yj" + h), r("hb" + h), Op.add, "sr")
+    else:
+        if h in OPT.get("hd", ""):
+            ts(r("hd" + h), r("d" + h, ind=("FU" + h, c4)), 0.5, Op.mult, -0.25, Op.add, "hd")
+        else:
+            S(r("hd" + h), r("d" + h, ind=("FU" + h, c4)), "hd", scale=0.5, bias=-0.25)
+        tt(r("nr" + h), r("y" + h, ind=("FU" + h, c4)), r("hd" + h), Op.add, "nr")
+        cp(w, r("nr" + h), "sr")
+    if hh == 0 and not end:
+        S(r("rec", c(4096, 4128)), r("rec", c(0, 32)), "rep")
+
+
+def stock(t, hs):
+    end = t + 1 == NV
+    k = c(4 * hs[0], 4 * hs[-1] + 4)
+    AT["half"] = str(hs[-1])
+    pS = r("pC", c(8 + k.start, 8 + k.stop))
+    P([mm(pS, r("mI"), r("RS", k), True, False)] + [
+        mm(r("pC", c(8 + 4 * hh, 12 + 4 * hh)), r("I5" if hh else "nI5"), r("ng", c(4 * hh, 4 * hh + 4)), False, hh == hs[-1]) for hh in hs], "Sl")
+    tt(r("SI", k), r("r7", k), pS, Op.add, "SI")
+    cp(r("SU", k), r("SI", k), "SU")
+    for hh in hs:
+        h = AT["half"] = str(hh)
+        w = r("stock", c(1024 * hh, 1024 * hh + 1024), ind=("SU", c(4 * hh, 4 * hh + 4)))
+        if end:
+            cp(w, r("nw" + h), "ss")
+        else:
+            tt(w, r("Y" + h), r("Rs" + h), Op.add, "ss")
+
+
+def build():
+    setup()
     for t in range(NV):
         end = t + 1 == NV
-        win = c(0, 4096 + 32 * (t > 0))
-
-        def offsets(h, tag):
-            ts(r("Xs" + h), r("Xi" + h), 5, SAR, 4095, AND, tag)
-            if t == 0:
-                cp(r("lu" + h), r("Xs" + h), tag + "u")
-            else:
-                ts(r("lu" + h), r("Xs" + h), r("Acol"), Op.add, tag=tag + "u")
-
+        AT["visit"], AT["half"] = t, ""
         if end:
-            HALF[0] = ""
             dma("Y", r("rec2"), r("rec", c(0, 2048)), 3000, "rec2")
         for hh in range(H):
-            h = HALF[0] = str(hh)
-            al = r(LAND[t] + h)
-            pA, pW, pE = "pA" + h, "pW" + h, "pE" + h
-            P([mm(r(pA, c(64 * k, 64 * k + 64)), r(m), al) for k, m in enumerate(("mS", "mF", "mG"))], "lists")
-            tt(r("M" + h), al, r(pA, c(0, 64)), Op.mult, "l")
-            tt(r("Xi" + h, c(0, 64)), r("M" + h), r(pA, c(64, 128)), Op.add, "l")
-            tt(r("Xi" + h, c(64, 128)), r("M" + h), r(pA, c(128, 192)), Op.add, "l")
-            offsets(h, "l2")
-            P([mm(r(pA, c(192, 256)), r("SmI"), al)], "keep")
-            gathers(h, "f", "e", win, 1)
-            pK, pU, E = r(pA, c(256, 320)), r(pA, c(320, 384)), r(pE, A_, c(0, 16))
-            P([mm(pU, r("I5"), r("CKU"), True, False)] + sums(pU, "ZU", "f" + h, range(16), False, True), "u")
-            P(sums(E, "Z1", "ab" + h, range(EARLY), True, False), "key1e")
-            P(sums(E, "Z1", "ab" + h, range(EARLY, 16), False, True), "key1")
-            S(r("pv" + h), E, "ring")
-            P([mm(pK, r("mI"), r("CK1"), True, False), mm(pK, r("I32"), r("pv" + h), False, False)], "k1")
-            tt(r("cb" + h, A_, c(1, 15)), r("pv" + h, A_, c(0, 14)), r(pE, A_, c(2, 16)), Op.is_lt, "a")
-            tt(r("cb" + h, A_, c(0, 16, 15)), r("pv" + h, A_, c(15, 13, -1)), r("pv" + h, A_, c(1, None, -1)), Op.is_lt, "a")
-            P([mm(pK, r("n2I"), r("cb" + h), False, True)], "k2")
-            scan(r("MU" + h, c(0, 64)), r("SMa"), pK, Op.add, Op.max, "a2")
-            tt(r("ne" + h), r("MU" + h, c(0, 64)), pK, Op.not_equal, "a2")
-            scan(r("MU" + h, c(64, 128)), r("ne" + h), pU, Op.mult, Op.max, "a2")
-            ts(r("cc", hh), r("MU" + h, c(15, 128, 16)), 1023, AND, tag="a2")
-            cp(r("cu" + h, c(0, 8)), r("cc", hh), "a2")
-            P([mm(r(pW, c(0, 256)), r("mI"), r("CA"), True, False)], "wc")
-            for k in (0, 64):
-                tt(r("pr" + h, c(k, k + 64)), r("tab", c(k, k + 64), ind=("cu" + h, c4)), al, Op.mult, "a3")
-            P([mm(r(pW, c(0, 128)), r("BO"), r("pr" + h), False, False),
-               mm(r(pW, c(128, 192)), r("BO3"), r("pr" + h, c(0, 64)), False, False),
-               mm(r(pW, c(192, 256)), r("BO2"), r("pr" + h, c(64, 128)), False, True)], "wl")
-            S(r("B" + h), r("stock", c(512, 1536), ind=("cu" + h, c8)), "B", bias=-2048.0)
-            tt(r("X" + h, c(0, 64)), r("B" + h), r(pW, c(0, 64)), Op.mult, "m")
-            tt(r("X" + h, c(64, 128)), r("B" + h), r(pW, c(64, 128)), Op.mult, "m")
-            tt(r("Xi" + h), r("X" + h), r(pW, c(128, 256)), Op.add, "m")
-            offsets(h, "m")
-            gathers(h, "y", "d", win, 3)
-        HALF[0] = ""
-        ts(r("r31"), r("cc", A_, c8), 31, AND, tag="pre")
-        tt(r("FI", A_, c8), r("r31"), r("RC"), Op.add, "pre")
-        ts(r("r7"), r("cc", A_, c8), 7, AND, tag="pre")
+            front(t, hh)
+        AT["half"] = ""
+        ts(r("r31"), r("cc", A_, c8), 31, AND, tag="r31")
+        tt(r("FI", A_, c8), r("r31"), r("RC"), Op.add, "rl")
+        ts(r("r7"), r("cc", A_, c8), 7, AND, tag="r7")
         if not end:
-            P([mm(r("pC", c(0, 1)), r("onh"), r("c48", c(0, 1)), True, False)], "A0")
+            P([mm(r("pC", c(0, 1)), r("onh"), r("c48", c(0, 1)), True, False)], "Ac")
         for hh in range(H):
-            h = HALF[0] = str(hh)
-            al = r(LAND[t] + h)
-            pA, pW, pE = "pA" + h, "pW" + h, "pE" + h
-            k2, R, ng = r(pW, c(448, 512)), r(pE, A_, c(32, 48)), c(4 * hh, 4 * hh + 4)
-            P([mm(k2, r("mI"), r("CK2"), True, False)] + sums(k2, "Z2", "ab" + h, range(EARLY), False, False), "key2e")
-            P(sums(k2, "Z2", "ab" + h, range(EARLY, 16), False, True), "key2")
-            scan(r("m2" + h), r("SMi"), k2, Op.add, Op.min, "b")
-            tt(r("ng", ng), r("m2" + h, last), r("MU" + h, last), Op.is_ge, "b")
-            ts(r("FI", hh, c4), r("m2" + h, last), 1023, AND, tag="b")
-            tt(r("FI", hh, c12), r("cc", hh, c4), r("ng", ng), Op.add, "b")
-            cp(r("FU" + h, c(0, 12)), r("FI", hh), "b2")
-            if not end:
-                P([mm(r("pC", c(0, 1)), r("onh"), r("ng", c(k, k + 1)), False, k == 7) for k in range(4 * hh, 4 * hh + 4)], "A")
-            S(r("mx" + h), r("tab", c(192, 256), ind=("FU" + h, c12)), "mx")
-            S(r("gp" + h), r("tab", c(128, 192), ind=("FU" + h, c12)), "gp")
-            tt(r("bj" + h), r("ohJ", ind=("FU" + h, c4)), r("B" + h), Op.mult, "w")
-            P([mm(r(pW, c(256, 320)), r("nI"), al, True, False), mm(r(pW, c(256, 320)), r("BO"), r("bj" + h), False, True)], "bj")
-            tt(r("dl" + h), r("mx" + h), r(pA, c(192, 256)), Op.mult, "w")
-            P([mm(R, r("mI"), al, True, False)] + [mm(R, r("mI"), r("C2k"), False, False)] * end + [mm(R, r("ISh"), r("dl" + h), False, True)], "R")
-            tt(r("Y" + h), r("gp" + h), r(pW, c(256, 320)), Op.mult, "w")
-            new = r(("nw" if end else "snd") + h)
-            tt(new, r("Y" + h), R, Op.add, "w")
-            sn = add("G", [("remote_dma", dict(to=LAND[t + 1] + h, in_=new))], kind="send", tag="%d%d" % (t, hh), dur=300)
-            add("R", [], kind="recv", tag="%d%d" % (t, hh), dur=0, pre=[sn], extra=[(LAND[t + 1] + h, 0, 64, True)])
-            if not end:
-                S(r("Rs" + h), R, "Rs", bias=2048.0)
-            S(r("hd" + h), r("d" + h, ind=("FU" + h, c4)), "hd", scale=0.5, bias=-0.25)
-            tt(r("nr" + h), r("y" + h, ind=("FU" + h, c4)), r("hd" + h), Op.add, "nr")
-            w = r("rec2", ind=("FU" + h, c8)) if end and hh == 0 else r("rec", c(2048 * hh, 2048 * hh + 2048), ind=("FU" + h, c8))
-            cp(w, r("nr" + h), "sr")
-            if hh == 0 and not end:
-                S(r("rec", c(4096, 4128)), r("rec", c(0, 32)), "mirror")
-        HALF[0] = ""
+            back(t, hh)
+        AT["half"] = ""
         if not end:
             S(r("nq"), r("pC", c(0, 1)), "nq", scale=-1.0, bias=15.75)
-            S(r("Acol"), r("pC", c(0, 1)), "nq", AF.Identity, bias=r("nq"))
+            S(r("Acol"), r("pC", c(0, 1)), "Acol", AF.Identity, bias=r("nq"))
         for hs in ([[0], [1]] if end else [[0, 1]]):
-            k = c(4 * hs[0], 4 * hs[-1] + 4)
-            HALF[0] = str(hs[0]) if end else ""
-            P([mm(r("pS", k), r("mI"), r("RS", k), True, False)] + [
-                mm(r("pS", c(4 * hh, 4 * hh + 4)), r("I5" if hh else "nI5"), r("ng", c(4 * hh, 4 * hh + 4)), False, hh == hs[-1]) for hh in hs], "sl")
-            tt(r("SI", k), r("r7", k), r("pS", k), Op.add, "sl")
-            cp(r("SU", k), r("SI", k), "sl")
-            for hh in hs:
-                h = HALF[0] = str(hh)
-                w = r("stock", c(1024 * hh, 1024 * hh + 1024), ind=("SU", c(4 * hh, 4 * hh + 4)))
-                if end:
-                    cp(w, r("nw" + h), "ss")
-                else:
-                    tt(w, r("Y" + h), r("Rs" + h), Op.add, "ss")
+            stock(t, hs)
     for hh in range(H):
-        h = HALF[0] = str(hh)
-        dma("Y", r("yx", c(2048 * hh, 2048 * hh + 2048)), r("rec", c(2048, 4096)) if hh else r("rec2"), 3000, "store")
-        dma("Y", r("yp", c(512 * hh, 512 * hh + 512)), r("stock", c(512 + 512 * hh, 1024 + 512 * hh)), 2500, "store")
-        dma("Y", r("yw", c(64 * hh, 64 * hh + 64)), r("le" + h), 2000, "store")
-
-
-def ways():
-    n = len(NODES)
-    succ = [[] for _ in range(n)]
-    for i, x in enumerate(NODES):
-        for p in x["preds"] + x["after"]:
-            succ[p].append(i)
-    way = [0.0] * n
-    for i in range(n - 1, -1, -1):
-        way[i] = NODES[i]["dur"][0] + max([way[j] + 100.0 for j in succ[i]], default=0.0)
-    return succ, way
+        h = AT["half"] = str(hh)
+        dma("Y", r("yx", c(2048 * hh, 2048 * hh + 2048)), r("rec", c(2048, 4096)) if hh else r("rec2"), 3000, "yx")
+        dma("Y", r("yp", c(512 * hh, 512 * hh + 512)), r("stock", c(512 + 512 * hh, 1024 + 512 * hh)), 2500, "yp")
+        dma("Y", r("yw", c(64 * hh, 64 * hh + 64)), r("le" + h), 2000, "yw")
 
 
 def busy(x, d):
     return 100.0 if x["kind"] == "dma" else 0.0 if x["kind"] == "recv" else d
 
 
-def schedule(bonus, sw):
-    succ, way = sw
+def schedule():
     n = len(NODES)
-    w1, w2 = MODELS[0][6:]
-    prio = [way[i] + bonus.get(NODES[i]["key"], 0) for i in range(n)]
-    look = {q: bonus.get("look" + q, 0) for q in "VSPGYR"}
+    by = {(x["visit"], x["key"]): i for i, x in enumerate(NODES)}
+    for names in ORDER.values():
+        line = [by.get((t + (k[0] == "+"), k.lstrip("+"))) for t in range(-1, NV) for k in names.split()]
+        line = [i for i in line if i is not None]
+        for a, b in zip(line, line[1:]):
+            NODES[b]["after"].append(a)
+    succ = [[] for _ in range(n)]
+    for i, x in enumerate(NODES):
+        for p in x["preds"] + x["after"]:
+            succ[p].append(i)
     left = [len(x["preds"]) + len(x["after"]) for x in NODES]
+    top, cnt = [i for i in range(n) if left[i] == 0], list(left)
+    for i in top:
+        for j in succ[i]:
+            cnt[j] -= 1
+            if cnt[j] == 0:
+                top.append(j)
+    way = [0.0] * n
+    for i in reversed(top):
+        way[i] = NODES[i]["dur"][0] + max([way[j] + 50.0 for j in succ[i]], default=0.0)
+    w1, w2 = MODELS[0][6:]
     rt = [0.0] * n
-    ready = {}
+    ready, free, order = {}, {}, []
     for i in range(n):
         if left[i] == 0:
             ready.setdefault(NODES[i]["eng"], []).append(i)
-    free = {}
-    order = []
-    end = 0.0
     while len(order) < n:
         s, e = min((max(free.get(q, 0.0), min(rt[i] for i in L)), q) for q, L in ready.items() if L)
-        i = max((i for i in ready[e] if rt[i] <= s + look[e]), key=lambda k: (prio[k] - 10 * max(rt[k] - s, 0), -k))
+        i = max((i for i in ready[e] if rt[i] <= s + 60), key=lambda k: (way[k], -k))
         s = max(s, rt[i])
         ready[e].remove(i)
         x = NODES[i]
         free[e] = s + busy(x, x["dur"][0])
         x["t0"], x["t1"] = s, s + x["dur"][0]
-        end = max(end, x["t1"])
         order.append(i)
         for j in succ[i]:
             left[j] -= 1
-            rt[j] = max(rt[j], x["t1"] + (0.0 if i in NODES[j]["after"] else w1 if NODES[j]["eng"] == e else w2))
+            rt[j] = max(rt[j], x["t1"] + (0.0 if i not in NODES[j]["preds"] else w1 if NODES[j]["eng"] == e else w2))
             if left[j] == 0:
                 ready.setdefault(NODES[j]["eng"], []).append(j)
-    return order, end
-
-
-def replay(order, k):
-    w1, w2 = MODELS[k][6:]
-    free, t1 = {}, [0.0] * len(NODES)
-    for i in order:
-        x = NODES[i]
-        e, d = x["eng"], x["dur"][k]
-        s = free.get(e, 0.0)
-        for p in x["preds"]:
-            s = max(s, t1[p] + (w1 if NODES[p]["eng"] == e else w2))
-        t1[i] = s + d
-        free[e] = s + busy(x, d)
-    return max(t1)
-
-
-def search(tries, seed):
-    rnd = np.random.RandomState(seed)
-    sw = ways()
-    keys = sorted({x["key"] for x in NODES})
-
-    def value(C):
-        o, v = schedule(C, sw)
-        return v + sum(replay(o, k) for k in range(1, len(MODELS)))
-
-    B = {q: 1500 for q in keys if q.endswith("0") and q[0] != "s"}
-    B.update({"ss0": -5000, "ss1": -5000, "set": -3000, "lookS": 50, "lookV": 100})
-    end = value(B)
-    steps = (-8000, -4000, -2000, -1000, -500, 500, 1000, 2000, 4000, 8000)
-    for _ in range(tries):
-        C = dict(B)
-        for _ in range((1, 1, 2, 3, 6)[rnd.randint(5)]):
-            k = rnd.randint(len(keys) + 6)
-            if k >= len(keys):
-                C["look" + "VSP"[k % 3]] = (0, 50, 100, 200, 300, 500)[rnd.randint(6)]
-            else:
-                C[keys[k]] = steps[rnd.randint(10)] + (C.get(keys[k], 0) if rnd.randint(2) else 0)
-        v = value(C)
-        if v <= end:
-            end, B = v, C
-    return schedule(B, sw)[0]
+    return order
 
 
 def plan(order):
@@ -560,7 +623,7 @@ def plan(order):
         elif kind == "dma":
             sm, v = "d%d" % i, 16
         else:
-            sm, v = ("l" if kind == "send" else "r") + x["tag"], 8
+            sm, v = "%s%d" % (x["key"], x["visit"]), 8
         clk[sm] = v
         x["tok"], x["clk"] = (sm, v), clk
         final[sm] = v
@@ -569,7 +632,7 @@ def plan(order):
 
 
 build()
-PLAN, FINAL, KNOWG = plan(search(TRIES, SEED))
+PLAN, FINAL, KNOWG = plan(schedule())
 SEMAPHORES = list(FINAL)
 
 
@@ -587,12 +650,13 @@ def rank_program(g, core, T, topo):
         for sm, v in waits:
             q.wait_ge(T.sem[sm], v)
         if x["kind"] == "send":
-            t = int(x["tag"][0])
+            t = x["visit"]
             dst = T.cores[(rank + (STEP if t + 1 < NV else -STEP * (NV - 1))) % n]
             kw = x["calls"][0][1]
             rid, pid = topo.addr(dst)[:2]
-            g.remote_dma(out_ap=T[kw["to"]][:], in_ap=ap(T, kw["in_"]), remote_sem=T.sem["r" + x["tag"]], local_sem=T.sem["l" + x["tag"]],
-                         pid=pid, routing_id=rid, dma_engine_mask=sum(1 << e for e in topo.engines(core, dst)[:8]))
+            g.remote_dma(out_ap=T[kw["to"]][:], in_ap=ap(T, kw["in_"]), remote_sem=T.sem[x["tok"][0].replace("send", "recv")],
+                         local_sem=T.sem[x["tok"][0]], pid=pid, routing_id=rid,
+                         dma_engine_mask=sum(1 << e for e in topo.engines(core, dst)[:8]))
             continue
         for m, kw in x["calls"]:
             kw = {a: (ap(T, b) if isref(b) else b) for a, b in kw.items()}

@@ -7,7 +7,7 @@ NV, STEP, H = 4, 3, 2
 CH = {q: ([16, 16, 16, 16], [16, 16, 16, 8, 8], [16, 16, 16, 8, 8]) for q in ("f0", "f1", "y0", "y1")}
 OWN = []
 SOLO = []
-SEL = dict(cb="V2", pr="S", nr="V", sp=1, own=["fa1", "ya0"], dl="V", fu="01", ch={q: ([12, 20, 20, 12],) * 3 for q in CH})
+SEL = dict(cb="V2", pr="V", nr="V", sp=1, own=["fa1", "ya0"], solo=["eb1", "db0"], dl="V", fu="01", ch={q: ([12, 20, 20, 12],) * 3 for q in CH})
 RELU = []
 OPT = {"cb": "V2", "pr": "V", "nr": "V", "sp": 0}
 ORDER = {
@@ -19,6 +19,11 @@ ORDER = {
     "V": "ea0 eb0 ec0 ed0 M1 Xf1 Xg1 s11 u11 fa1 cb0 cw0 ea1 max0 eb1 ne0 cck0 sel0 cuk0 ec1 ccu0 pr0 cuu0 ed1 Xz0 Xy0 Xl0 s30 u30 cb1 ya0 cw1 da0 max1 db0 ne1 cck1 sel1 cuk1 ccu1 dc0 cuu1 pr1 dd0 r31 Xy1 Xz1 r7 Xl1 s31 u31 min0 rl ng0 J0 co0 FU0 FV0 bj0 dl0 da1 Y0 new0 db1 dc1 dd1 nr0 sr0 min1 ng1 J1 co1 FU1 FV1 bj1 dl1 SI0 nr1 Y1 new1 sr1 SU0 +M0 SI1 +Xg0 +Xf0 +s10 +u10 SU1 ss0 ss1",
     "S": "fd0 |ea0 |eb0 |ec0 |ed0 pv0 fb1 fc1 |ea1 fd1 |eb1 pb0 pa0 |ec1 B0 |ed1 pv1 dW0 yb0 yd0 |da0 yc0 |db0 pa1 pb1 B1 |dc0 |dd0 ya1 yb1 gp0 yc1 hd0 |da1 yd1 |db1 |dc1 |dd1 dW1 hd1 gp1 nq Acol Rs0 rep0 Rs1 +fa0 +fb0 +fc0",
     "P": "E00 lists1 Ea0 E01 Eb0 Ec0 Ed0 Ub0 Kc0 Ka0 keep1 Kb0 U01 Ua1 Wc0 Ea1 Ub1 Kc1 W0 L0 Eb1 Ec1 Ed1 Ra0 Ka1 F00 Kb1 W1 L1 Fa0 Fb0 Fc0 Fd0 Sl0 F01 Ra1 Ba0 Bb0 Rb0 Fa1 A0 Fb1 Fc1 Fd1 Ba1 A1 Bb1 Rb1 +lists0 Sl1 +keep0 +Ac +Wc1 +U00 +Ua0",
+}
+ORDER = {
+    "V": "ed0 M1 Xg1 Xf1 s11 u11 cb0 cw0 fa1 max0 ea1 ne0 cck0 sel0 cuk0 ccu0 pa0 cuu0 pb0 ec1 ed1 Xz0 Xy0 Xl0 s30 u30 ya0 cw1 cb1 da0 max1 ne1 cck1 sel1 cuk1 ccu1 pa1 cuu1 pb1 dc0 dd0 Xy1 Xz1 Xl1 r31 s31 u31 rl r7 min0 ng0 J0 co0 FU0 FV0 bj0 dl0 da1 Y0 new0 db1 dc1 dd1 nr0 sr0 min1 ng1 J1 co1 FU1 FV1 bj1 dl1 nr1 +M0 Y1 +Xg0 +Xf0 new1 SI0 +s10 sr1 +u10 SU0 SI1 SU1 ss0 ss1 +ea0 +eb0 +ec0",
+    "S": "|eb0 |ec0 |ed0 pv0 eb1 fb1 fc1 |ea1 fd1 B0 |eb1 |ec1 |ed1 dW0 pv1 db0 yc0 yb0 yd0 |da0 B1 |db0 |dc0 |dd0 ya1 yb1 gp0 yc1 yd1 |da1 |db1 hd0 |dc1 |dd1 dW1 rep0 hd1 gp1 nq Rs0 Acol Rs1 +fa0 +fb0 +fc0 +|ea0 +fd0",
+    "P": "Ed0 Ub0 Kc0 Ka0 keep1 Kb0 U01 Wc0 Deb1 Ua1 Ea1 L0 W0 Ub1 Kc1 Eb1 Ec1 Ed1 Ka1 Kb1 F00 Ddb0 Ra0 W1 L1 Fa0 Fb0 Fc0 Fd0 F01 Ra1 Ba0 Sl0 Bb0 Rb0 A0 Fa1 Fb1 Fc1 Fd1 Ba1 A1 +lists0 Bb1 Rb1 +E00 Sl1 +keep0 +U00 +Wc1 +Ac +E01 +Ua0 +lists1 +Ea0 +Eb0 +Ec0",
 }
 OPT.update(SEL)
 OWN, RELU, SOLO = (SEL.get(k, []) for k in ("own", "relu", "solo"))
@@ -91,7 +96,7 @@ bufs("sbuf", "float16", [128, 4, 16], "cb", halves=True)
 bufs("psum", "float32", [128, 512], "pA pW", halves=True)
 bufs("psum", "float32", [128, 4, 128], "pE", halves=True)
 bufs("psum", "float32", [128, 512], "pC pD")
-bufs("sbuf", "bfloat16", [128, 128], "bI nbI", "PB")
+bufs("sbuf", "bfloat16", [128, 128], "bI nbI n2I", "PB")
 A_ = slice(None)
 
 
@@ -269,7 +274,8 @@ def cuts(w):
 def gathers(h, a, b, win):
     one, two, three = CH[a + h]
     for k, o, e in cuts(one):
-        (cp if a + k + h in OWN else S)(piece(a + h, o, e), r("rec", win, ind=("lu" + h, c(o, e))), a + k)
+        half = {"scale": 0.5} if a == "y" and b + k + h in SOLO else {}
+        (cp if a + k + h in OWN else S)(piece(a + h, o, e), r("rec", win, ind=("lu" + h, c(o, e))), a + k, **half)
     for k, o, e in cuts(two):
         if b + k + h in SOLO:
             S(piece(b + h, o, e), r("rec", win, ind=("lu" + h, c(64 + o, 64 + e))), b + k)
@@ -278,7 +284,7 @@ def gathers(h, a, b, win):
     for k, o, e in cuts(three):
         if b + k + h in SOLO:
             D = r("pD", c(0, 16 * (e - o)))
-            P([mm(D, r("bI"), piece(b + h, o, e), True, False), mm(D, r("nbI"), piece(a + h, o, e), False, True)], "D" + k)
+            P([mm(D, r("bI"), piece(b + h, o, e), True, False), mm(D, r("nbI" if a == "f" else "n2I"), piece(a + h, o, e), False, True)], "D" + b + k)
             S(piece("ab" + h, o, e), D, "|" + b + k, AF.Abs)
         elif b + k + h in RELU:
             ts(piece("ab" + h, o, e), piece(b + h, o, e), 0.0, Op.max, 2.0, Op.mult, "|" + b + k)
@@ -315,7 +321,7 @@ def setup():
     tt(r("mS"), r("tA"), r("BO"), Op.mult)
     for o, i, k in (("I3", "mI", 3232.0), ("I2", "mI", 2080.0), ("nI", "mI", -1.0),
                     ("BO3", "BO", 3232.0), ("BO2", "BO", 2080.0), ("nB", "mI", -1.0 if OPT["cb"] == "S" else -2.0),
-                    ("I5", "mI", 512.0), ("nI5", "mI", -512.0), ("I2k", "mI", 2048.0)) + (("bI", "mI", 1.0), ("nbI", "mI", -1.0)) * bool(SOLO):
+                    ("I5", "mI", 512.0), ("nI5", "mI", -512.0), ("I2k", "mI", 2048.0)) + (("bI", "mI", 1.0), ("nbI", "mI", -1.0), ("n2I", "mI", -2.0)) * bool(SOLO):
         S(r(o), r(i), "set", scale=k)
     for k, (o, a, b, a2, b2) in enumerate((("mF", "I3", "mI", "I2", "mS"), ("mG", "I2", "mI", "I3", "mS"),
                                            ("SmI", "nI", "mI", "mI", "mS"), ("ISh", "mI", "mI", "mS", "nI"))):
@@ -441,7 +447,6 @@ def front(t, hh):
     tt(r("X" + h, c(64, 128)), r("B" + h), r(pW, c(64, 128)), Op.mult, "Xz")
     tt(r("Xi" + h), r("X" + h), r(pE, c(0, 2), c(64, 128)), Op.add, "Xl")
     offsets(t, h, "3")
-    gathers(h, "y", "d", win)
 
 
 def back(t, hh):
@@ -526,6 +531,9 @@ def build():
             dma("Y", r("rec2"), r("rec", c(0, 2048)), 3000, "rec2")
         for hh in range(H):
             front(t, hh)
+        for h in "01":
+            AT["half"] = h
+            gathers(h, "y", "d", c(0, 4096 + 32 * (t > 0)))
         AT["half"] = ""
         ts(r("r31"), r("cc", A_, c8), 31, AND, tag="r31")
         tt(r("FI", A_, c8), r("r31"), r("RC"), Op.add, "rl")

@@ -7,7 +7,7 @@ NV, STEP, H = 4, 3, 2
 CH = {q: ([16, 16, 16, 16], [16, 16, 16, 8, 8], [16, 16, 16, 8, 8]) for q in ("f0", "f1", "y0", "y1")}
 OWN = []
 SOLO = []
-SEL = dict(cb="V2", pr="V", nr="V", sp=1, own=["fa1", "ya0"], solo=["eb1", "db0"], dl="V", fu="01", ch={q: ([12, 20, 20, 12],) * 3 for q in CH})
+SEL = dict(cb="V2", pr="V", nr="V", nc=1, xs=1, own=["fa0", "fa1", "ya0"], solo=["eb1", "db0"], ch={q: ([16, 20, 16, 12],) * 3 if q in ("f1", "y0") else ([12, 20, 20, 12],) * 2 + ([32, 20, 12],) for q in CH})
 RELU = []
 OPT = {"cb": "V2", "pr": "V", "nr": "V", "sp": 0}
 ORDER = {
@@ -24,6 +24,46 @@ ORDER = {
     "V": "ed0 M1 Xg1 Xf1 s11 u11 cb0 cw0 fa1 max0 ea1 ne0 cck0 sel0 cuk0 ccu0 pa0 cuu0 pb0 ec1 ed1 Xz0 Xy0 Xl0 s30 u30 ya0 cw1 cb1 da0 max1 ne1 cck1 sel1 cuk1 ccu1 pa1 cuu1 pb1 dc0 dd0 Xy1 Xz1 Xl1 r31 s31 u31 rl r7 min0 ng0 J0 co0 FU0 FV0 bj0 dl0 da1 Y0 new0 db1 dc1 dd1 nr0 sr0 min1 ng1 J1 co1 FU1 FV1 bj1 dl1 nr1 +M0 Y1 +Xg0 +Xf0 new1 SI0 +s10 sr1 +u10 SU0 SI1 SU1 ss0 ss1 +ea0 +eb0 +ec0",
     "S": "|eb0 |ec0 |ed0 pv0 eb1 fb1 fc1 |ea1 fd1 B0 |eb1 |ec1 |ed1 dW0 pv1 db0 yc0 yb0 yd0 |da0 B1 |db0 |dc0 |dd0 ya1 yb1 gp0 yc1 yd1 |da1 |db1 hd0 |dc1 |dd1 dW1 rep0 hd1 gp1 nq Rs0 Acol Rs1 +fa0 +fb0 +fc0 +|ea0 +fd0",
     "P": "Ed0 Ub0 Kc0 Ka0 keep1 Kb0 U01 Wc0 Deb1 Ua1 Ea1 L0 W0 Ub1 Kc1 Eb1 Ec1 Ed1 Ka1 Kb1 F00 Ddb0 Ra0 W1 L1 Fa0 Fb0 Fc0 Fd0 F01 Ra1 Ba0 Sl0 Bb0 Rb0 A0 Fa1 Fb1 Fc1 Fd1 Ba1 A1 +lists0 Bb1 Rb1 +E00 Sl1 +keep0 +U00 +Wc1 +Ac +E01 +Ua0 +lists1 +Ea0 +Eb0 +Ec0",
+}
+ORDER = {
+    "V": "Xg1 s11 u11 fa1 cb0 cw0 ea1 max0 ne0 cck0 sel0 cuk0 ccu0 pa0 cuu0 pb0 ec1 Xy0 Xz0 ed1 Xl0 s30 u30 ya0 cw1 cb1 da0 max1 ne1 cck1 sel1 cuk1 ccu1 pb1 cuu1 pa1 dc0 dd0 Xz1 Xy1 Xl1 r31 s31 u31 rl min0 r7 ng0 J0 co0 FU0 FV0 bj0 dl0 da1 SI0 Y0 new0 db1 dc1 dd1 nr0 SU0 sr0 re0 se0 min1 ng1 J1 co1 FU1 FV1 bj1 dl1 +M0 Y1 +Xg0 +Xf0 new1 +s10 sr1 +u10 SI1 SU1 ss1 ss0 re1 +ea0 se1 +eb0 +ec0 +ed0 +M1 +Xf1",
+    "S": "fa0 fb0 fc0 fd0 |ea0 |eb0 |ec0 |ed0 pv0 fb1 eb1 fc1 dW0 fd1 B0 |eb1 |ea1 |ec1 |ed1 pv1 db0 yc0 yb0 yd0 |da0 B1 |db0 |dc0 |dd0 ya1 yb1 gp0 yc1 yd1 |da1 |db1 hd0 |dc1 |dd1 Rs0 dW1 rep0 gp1 nq yj1 hq1 Acol hb1 Rs1",
+    "P": "Ac lists1 lin1 Ea0 Eb0 Ec0 Ed0 Ua0 Ub0 Kc0 Ka0 keep1 Kb0 U01 Wc0 Deb1 Ua1 W0 L0 E01 Ub1 Kc1 Eb1 Ea1 Ec1 Ed1 F00 Ka1 Ra0 Kb1 Ddb0 W1 Fa0 L1 Fb0 F01 Fc0 Fd0 Ba0 Sl0 A0 Bb0 Rb0 Fa1 Fb1 Fc1 Fd1 Ba1 Ra1 A1 +lists0 Bb1 +lin0 Rb1 +E00 +keep0 +U00 Sl1 +Wc1",
+}
+ORDER = {
+    "V": "Xf1 Xg1 s11 u11 fa1 cw0 cb0 ea1 max0 ne0 cck0 sel0 cuk0 ccu0 pa0 cuu0 pb0 ec1 Xy0 Xz0 ed1 Xl0 s30 u30 ya0 cw1 cb1 da0 max1 ne1 cck1 sel1 cuk1 ccu1 pb1 pa1 cuu1 dc0 dd0 Xy1 Xz1 Xl1 s31 r31 u31 rl r7 min0 ng0 J0 co0 FU0 FV0 bj0 dl0 da1 Y0 SI0 new0 db1 dc1 dd1 SU0 nr0 re0 se0 sr0 min1 ng1 J1 co1 FU1 FV1 bj1 dl1 +M0 +Xf0 +Xg0 Y1 +s10 new1 sr1 +u10 re1 SI1 SU1 ss1 se1 ss0 +ea0 +eb0 +ec0 +ed0 +M1",
+    "S": "fb0 fc0 fd0 |ea0 |eb0 |ec0 pv0 fb1 eb1 fc1 fd1 B0 |eb1 |ea1 |ec1 |ed1 dW0 pv1 db0 yb0 yc0 yd0 |da0 B1 |db0 |dc0 |dd0 ya1 yb1 gp0 yc1 yd1 hd0 |da1 |db1 |dc1 Rs0 rep0 dW1 gp1 hq1 yj1 hb1 nq Acol Rs1 +fa0",
+    "P": "U00 Ac lists1 lin1 Ea0 Eb0 Ec0 Ua0 Ub0 Kc0 Ka0 Kb0 keep1 E01 U01 Wc0 Ua1 Deb1 W0 L0 Ub1 Kc1 Eb1 F00 Ea1 Ec1 Ed1 Ka1 Kb1 Ddb0 Ra0 W1 L1 Fa0 Fb0 Fc0 Fd0 Ra1 F01 Ba0 Sl0 A0 Bb0 Rb0 Fa1 Fb1 Fc1 Ba1 A1 +lists0 +lin0 Bb1 Rb1 +E00 +keep0 +Wc1 Sl1",
+}
+ORDER = {
+    "V": "eb0 ec0 ed0 M1 Xg1 Xf1 s11 u11 fa1 cw0 cb0 ea1 max0 ne0 cck0 sel0 cuk0 ccu0 pa0 cuu0 pb0 Bi0 ec1 Xy0 Xz0 ed1 Xl0 s30 u30 ya0 cw1 cb1 da0 max1 ne1 cck1 sel1 cuk1 ccu1 pa1 cuu1 pb1 Bi1 dc0 dd0 Xz1 Xy1 Xl1 s31 u31 r7 r31 min0 rl ng0 J0 co0 FU0 FV0 bj0 dl0 da1 SI0 Y0 nr0 new0 re0 SU0 db1 se0 dc1 dd1 sr0 min1 ng1 J1 co1 FU1 FV1 bj1 dl1 +M0 re1 +Xf0 +Xg0 Y1 +s10 new1 sr1 +u10 SI1 SU1 ss1 ss0 +ea0 se1",
+    "S": "pv0 fb1 eb1 fc1 fd1 B0 |eb1 |ea1 |ec1 |ed1 dW0 pv1 db0 yb0 yc0 yd0 B1 |da0 |db0 |dc0 |dd0 dW1 ya1 yb1 gp0 hd0 yc1 yd1 |da1 |db1 |dc1 rep0 Rs0 hq1 gp1 nq yj1 hb1 Acol Rs1 +fa0 +fb0 +fc0 +fd0 +|ea0 +|eb0 +|ec0",
+    "P": "E00 Ua0 lists1 lin1 Ea0 Eb0 Ec0 Wc0 keep1 Ub0 Kc0 Ka0 U01 Kb0 Deb1 E01 Ua1 W0 L0 Ub1 Eb1 F00 Ea1 Ec1 Ed1 Kc1 Ka1 Kb1 Ra0 Ddb0 L1 W1 Fa0 Fb0 Fc0 Fd0 Sl0 Ra1 Ba0 F01 A0 Bb0 Rb0 Fa1 Fb1 Fc1 Ba1 A1 +lists0 +lin0 Bb1 Rb1 Sl1 +keep0 +U00 +Wc1 +Ac",
+}
+ORDER = {
+    "V": "M1 Xf1 Xg1 s11 u11 fa1 cw0 cb0 ea1 max0 ne0 cck0 sel0 cuk0 ccu0 pa0 cuu0 pb0 ec1 Xy0 Xz0 ed1 Xl0 s30 u30 ya0 cw1 cb1 da0 max1 ne1 cck1 sel1 cuk1 ccu1 pb1 cuu1 pa1 dc0 Xz1 Xy1 dd0 Xl1 r7 s31 r31 u31 rl min0 ng0 J0 co0 FU0 FV0 bj0 dl0 da1 Y0 SI0 new0 db1 dc1 dd1 nr0 SU0 re0 se0 sr0 min1 ng1 J1 co1 FU1 FV1 bj1 dl1 Y1 +M0 new1 +Xg0 +Xf0 sr1 +s10 +u10 re1 SI1 SU1 ss0 ss1 +ea0 se1 +eb0 +ec0 +ed0",
+    "S": "|eb1 |ec1 |ed1 dW0 pv1 yb0 db0 yc0 yd0 B1 |da0 |db0 |dc0 |dd0 ya1 yb1 gp0 yc1 hd0 yd1 |da1 |db1 |dc1 Rs0 rep0 dW1 nq gp1 hq1 hb1 yj1 Rs1 Acol +fa0 +fb0 +fc0 +fd0 +|ea0 +|eb0 +|ec0 +pv0 +fb1 +eb1 +fc1 +fd1 +B0 +|ea1",
+    "P": "E00 Ac keep0 Wc1 U00 Ua0 lists1 lin1 Ea0 Eb0 Ec0 Ub0 Kc0 Ka0 Kb0 keep1 U01 Wc0 E01 Ua1 Deb1 W0 L0 Ub1 Ea1 Eb1 Ec1 Ed1 Kc1 Ka1 Kb1 F00 Ddb0 W1 L1 Fa0 Fb0 Fc0 Fd0 Ra0 A0 F01 Ra1 Sl0 Ba0 Bb0 Rb0 Fa1 Fb1 Fc1 A1 Ba1 Bb1 +lists0 Rb1 +lin0 Sl1",
+}
+ORDER = {
+    "V": "s11 u11 fa1 pv0 cb0 cw0 ea1 max0 ne0 cck0 sel0 cuk0 ccu0 pa0 cuu0 pb0 ec1 ed1 Xy0 Xz0 Xl0 s30 |ed1 u30 ya0 pv1 cb1 cw1 da0 max1 ne1 cck1 sel1 cuk1 ccu1 pa1 cuu1 pb1 dc0 dd0 Xz1 Xy1 |dd0 Xl1 r31 s31 u31 rl r7 min0 ng0 J0 co0 FU0 FV0 bj0 dl0 da1 Y0 new0 db1 dc1 SI0 hd0 SU0 dd1 nr0 |dc1 re0 se0 sr0 min1 ng1 J1 co1 FU1 FV1 bj1 dl1 +M0 hd1 +Xf0 nr1 Y1 +Xg0 new1 +s10 sr1 +u10 SI1 SU1 ss0 re1 se1 ss1 +ea0 +eb0 +ec0 +ed0 +M1 +Xf1 +Xg1 +|ec0",
+    "S": "fa0 fb0 fc0 fd0 |ea0 |eb0 fb1 eb1 fc1 fd1 |ea1 B0 |eb1 |ec1 dW0 db0 yb0 yc0 yd0 |da0 B1 |db0 |dc0 ya1 yb1 gp0 yc1 yd1 |da1 |db1 Rs0 rep0 dW1 gp1 nq Acol Rs1",
+    "P": "Ac lists1 lin1 Ua0 Wc0 Enc0 Ea0 Eb0 Ec0 Ub0 Kc0 Ka0 keep1 Kb0 E01 U01 Deb1 Ua1 W0 L0 Ub1 Kc1 Eb1 End1 F00 Ea1 Ec1 Ed1 Ka1 Kb1 Ddb0 Ra0 W1 L1 Fa0 Fnd0 Fb0 Fc0 Fd0 F01 Ba0 A0 Sl0 Ra1 Bb0 Rb0 Fa1 Fnc1 Fb1 Fc1 +lists0 +lin0 Ba1 A1 Bb1 Rb1 +E00 +keep0 +Wc1 +U00 Sl1",
+}
+ORDER = {
+    "V": "eb0 ec0 M1 ed0 Xg1 Xf1 s11 u11 fa1 cb0 cw0 ea1 max0 ne0 sel0 cc0 cu0 ec1 pa0 pb0 ed1 Xy0 Xz0 Xl0 s30 u30 ya0 cw1 cb1 da0 max1 ne1 sel1 cc1 dc0 cu1 pb1 pa1 dd0 Xz1 Xy1 Xl1 s31 u31 r31 min0 rl ng0 J0 co0 FU0 r7 dl0 bj0 SI0 da1 Y0 new0 db1 dc1 dd1 nr0 SU0 sr0 re0 se0 min1 ng1 J1 co1 FU1 bj1 +M0 dl1 +Xg0 +Xf0 Y1 +s10 new1 sr1 +u10 re1 SI1 SU1 ss0 ss1 se1 +ea0",
+    "S": "fa0 fb0 fc0 fd0 |ea0 |eb0 |ec0 pv0 fb1 fc1 eb1 fd1 B0 |eb1 |ec1 |ea1 |ed1 dW0 pv1 yd0 yc0 yb0 db0 |da0 B1 |dc0 |db0 |dd0 ya1 yb1 gp0 yc1 yd1 hd0 |da1 |db1 |dc1 dW1 rep0 Rs0 gp1 hq1 yj1 hb1 nq Acol Rs1",
+    "P": "Ua0 lists1 lin1 Ub0 Ea0 Eb0 Ec0 keep1 U01 E01 Kc0 Wc0 Ka0 Kb0 Ua1 Deb1 Ub1 W0 L0 Eb1 Kc1 Ec1 Ea1 Ed1 F00 Ka1 Kb1 Ddb0 W1 Fa0 L1 Fb0 Fc0 Fd0 A0 Ba0 F01 Sl0 Ra0 Ra1 Bb0 Rb0 Fa1 Fb1 Fc1 A1 +lists0 +lin0 Ba1 Bb1 Rb1 +keep0 Sl1 +Wc1 +Ac +E00 +U00",
+}
+ORDER = {
+    "V": "Xf1 Xg1 s11 u11 pv0 pw0 max0 cb0 cw0 ne0 fa1 sel0 code0 ccu0 cuk0 ec1 cuu0 pb0 pa0 ea1 ed1 Xl0 s30 u30 pv1 max1 ya0 pw1 ne1 cb1 cw1 sel1 da0 ccu1 code1 cuu1 cuk1 dc0 pb1 pa1 dd0 r7 dk0 r31 Xl1 dk1 s31 rl min0 u31 ng0 J0 FV0 FU0 dl0 bj0 gp0 db1 Y0 SI0 new0 da1 dc1 dd1 SU0 nr0 sr0 se0 re0 min1 ng1 J1 FV1 FU1 dl1 bj1 +M0 gp1 +Xg0 +Xf0 nr1 Y1 new1 +s10 sr1 SI1 +u10 SU1 re1 se1 ss1 ss0 +ea0 +eb0 +ec0 +ed0 +M1",
+    "S": "fc0 fd0 |ea0 |eb0 |ec0 fc1 fb1 eb1 fd1 C0 B0 |eb1 |ea1 |ec1 |ed1 yb0 db0 yc0 dW0 yd0 |da0 |db0 C1 B1 |dc0 dW1 |dd0 mp0 yb1 ya1 mp1 yc1 hd0 yd1 |da1 |db1 |dc1 rep0 hd1 nq Acol Rs0 Rs1 +fa0 +fb0",
+    "P": "Ac lists1 lin1 Kc0 Ea0 Eb0 Ec0 keep1 U01 Ub0 Kb0 E01 Ua1 Deb1 Wc0 W0 Eb1 Ea1 Ec1 Ed1 Kc1 Ub1 Kb1 F00 Ddb0 Wc1 Fa0 W1 Fb0 Fc0 Fd0 F01 Ba0 Sl0 A0 Rb0 Bb0 Fa1 Fb1 Fc1 Ba1 +lists0 +lin0 A1 Rb1 Bb1 +keep0 Sl1 +U00 +Ua0 +E00",
+}
+ORDER = {
+    "V": "u11 pv0 pw0 max0 cb0 cw0 ne0 fa1 sel0 code0 ec1 ccu0 cuk0 cuu0 pa0 pb0 ea1 ed1 Xl0 s30 u30 pv1 max1 pw1 ya0 ne1 cb1 cw1 sel1 da0 ccu1 code1 cuu1 cuk1 dc0 pa1 pb1 dd0 dk0 r31 r7 Xl1 rl s31 dk1 min0 u31 ng0 J0 FV0 FU0 dl0 bj0 SI0 gp0 db1 Y0 new0 da1 dc1 dd1 nr0 sr0 SU0 se0 re0 min1 ng1 J1 FV1 FU1 dl1 bj1 +M0 gp1 +Xf0 +Xg0 nr1 Y1 new1 +s10 sr1 SI1 +u10 re1 SU1 +fa0 se1 ss1 +ea0 +eb0 +ec0 +ed0 +M1 +Xf1 +Xg1 ss0 +s11",
+    "S": "fc0 fd0 |ea0 |eb0 |ec0 fc1 fb1 eb1 fd1 |ec1 C0 B0 |eb1 |ea1 dW0 |ed1 yc0 yb0 db0 |da0 yd0 B1 C1 |db0 |dc0 |dd0 dW1 mp0 yb1 ya1 yc1 yd1 hd0 |da1 |db1 |dc1 mp1 rep0 hd1 nq Acol Rs0 Rs1 +fb0",
+    "P": "lists1 lin1 Ea0 Eb0 Ec0 Kc0 keep1 U01 Ub0 Kb0 E01 Ua1 Deb1 Wc0 W0 Ec1 Eb1 Ea1 Ed1 Ub1 Kc1 F00 Kb1 Ddb0 Fa0 Wc1 W1 Fb0 Fc0 Fd0 F01 Ba0 Sl0 A0 Rb0 Bb0 Fa1 Fb1 Fc1 Ba1 A1 +lists0 +lin0 Rb1 Bb1 +keep0 Sl1 +U00 +Ua0 +Ac +E00",
 }
 OPT.update(SEL)
 OWN, RELU, SOLO = (SEL.get(k, []) for k in ("own", "relu", "solo"))
@@ -73,25 +113,27 @@ bufs("sbuf", "bfloat16", [128, 1], "nq", "PB")
 bufs("sbuf", "float32", [128, 128], "ISh", "PF")
 bufs("sbuf", "float32", [128, 64], "SMa SMi", "PF")
 bufs("sbuf", "float16", [128, 128], "BO mI nI mS tA I3 I2 mF mG SmI BO3 BO2 onh nB I5 nI5 I2k", "PH")
-bufs("sbuf", "float16", [128, 128], "CA", "PH")
-bufs("sbuf", "float16", [128, 64], "C2k", "PH")
+bufs("sbuf", "float16", [128, 256], "CA CN", "PH")
+bufs("sbuf", "bfloat16", [128, 32], "yes", "PB")
 bufs("sbuf", "float16", [128, 8], "RS ng c48", "PH")
-bufs("sbuf", "float16", [128, 64], "la lb lc ld snd", halves=True)
+bufs("sbuf", "float16", [128, 128], "la lb lc ld snd", halves=True)
 bufs("sbuf", "float32", [128, 64], "le nw", halves=True)
 bufs("sbuf", "float16", [128, 64], "bj hq", "PH", True)
 bufs("sbuf", "float16", [128, 128], "pr", "PH", True)
-bufs("sbuf", "float32", [128, 64], "M B dl Y Rs hd ne", "PF", True)
+bufs("sbuf", "float32", [128, 64], "M dl dk Y hd ne", "PF", True)
 bufs("sbuf", "float32", [128, 128], "X", "PF", True)
+bufs("sbuf", "float32", [128, 256], "B", "PF", True)
+bufs("sbuf", "int32", [128, 256], "X2", "PI", True)
 bufs("sbuf", "int32", [128, 128], "Xi Xs MU", "PI", True)
-bufs("sbuf", "int32", [128, 64], "nr m2", "PI", True)
+bufs("sbuf", "int32", [128, 64], "nr m2 cd", "PI", True)
 bufs("sbuf", "int32", [128, 2, 8], "cc")
 bufs("sbuf", "int32", [128, 2, 12], "FI")
 bufs("sbuf", "uint16", [128, 128], "lu", "PU", True)
 bufs("sbuf", "uint16", [128, 16], "cu FU", "PU", True)
-bufs("sbuf", "bfloat16", [128, 64], "mx gp hb yj", "PB", True)
-bufs("sbuf", "bfloat16", [128, 128], "mk", "PB", True)
+bufs("sbuf", "bfloat16", [128, 64], "mx hb yj", "PB", True)
+bufs("sbuf", "bfloat16", [128, 128], "gp", "PB", True)
 bufs("sbuf", "bfloat16", [128, 1024], "ab f e y d", halves=True)
-bufs("sbuf", "float16", [128, 4, 18], "pv", halves=True)
+bufs("sbuf", "float32", [128, 4, 16], "pv pw", halves=True)
 bufs("sbuf", "float16", [128, 4, 16], "cb", halves=True)
 bufs("psum", "float32", [128, 512], "pA pW", halves=True)
 bufs("psum", "float32", [128, 4, 128], "pE", halves=True)
@@ -146,7 +188,7 @@ NODES = []
 ACC = {}
 BANK = {}
 AT = {"visit": -1, "half": ""}
-MODELS = [(1.04, 1.56, 3.8, 25, 0.55, 2300, 60, 110)]
+MODELS = [(0.86, 1.5, 3.7, 0, 0.42, 1200, 222, 222, 0, 222, 10, 600, 1.5, 222, 65, 0.5)]
 
 
 def cost(eng, calls, model):
@@ -163,14 +205,14 @@ def cost(eng, calls, model):
         elif kw["out"][3] is not None:
             t += 50 + sc * cy * n
         elif any(v[3] is not None for v in refs):
-            t += (50 if eng == "V" else 65) + gam * cy * n
+            t += (50 if eng == "V" else model[14]) + (model[12] if m == "tensor_tensor" else gam) * cy * n
         else:
             if m == "tensor_tensor" and SCRATCH[kw["in0"][1]][0] == SCRATCH[kw["in1"][1]][0]:
                 n *= 2
             elif eng == "V" and m != "tensor_tensor" and all(d in ("bfloat16", "float16", "uint16") for d in dts):
-                n /= 2
-            t += fix + cy * max(n, 64)
-    return t + (40 if eng == "P" else 0)
+                n *= model[15]
+            t += (fix if eng == "V" else model[8]) + cy * max(n, 64)
+    return t + (model[10] if eng == "P" else 0)
 
 
 def add(eng, calls, tag, kind="comp", dur=None, extra=(), pre=()):
@@ -186,8 +228,11 @@ def add(eng, calls, tag, kind="comp", dur=None, extra=(), pre=()):
     for name, x, w in touch:
         psum = name in SCRATCH and SCRATCH[name][0] == "psum"
         if psum and eng == "P":
-            after.add(BANK.get(name, n))
-            BANK[name] = n
+            B = BANK.setdefault(name, [n])
+            if n not in B:
+                mid = not any(kw["start"] or kw["stop"] for m, kw in calls)
+                after.update(B[:1] if mid else B)
+                BANK[name] = B + [n] if mid else [n]
         keep = []
         for q in ACC.setdefault(name, []):
             m, me, a, mw = q
@@ -203,7 +248,7 @@ def add(eng, calls, tag, kind="comp", dur=None, extra=(), pre=()):
             keep.append(q)
         keep.append((n, eng, x, w))
         ACC[name] = keep[-40:] if psum else keep
-    durs = [cost(eng, calls, M) if dur is None else M[5] if kind == "recv" else dur for M in MODELS]
+    durs = [cost(eng, calls, M) if dur is None else M[5] if kind == "recv" else M[11] if kind == "send" else dur for M in MODELS]
     NODES.append({"eng": eng, "dur": durs, "calls": calls, "kind": kind, "preds": sorted(preds), "after": sorted(after - preds - {n}),
                   "key": tag + AT["half"], "visit": AT["visit"]})
     return n
@@ -255,8 +300,8 @@ def scan(out, data0, data1, op0, op1, tag):
     return V("tensor_tensor_scan", tag, out=out, data0=data0, data1=data1, initial=0.0, op0=op0, op1=op1)
 
 
-def dma(q, out, in_, dur, tag):
-    return add(q, [("dma_start", dict(out=out, in_=in_))], tag, kind="dma", dur=dur)
+def dma(q, out, in_, dur, tag, pre=()):
+    return add(q, [("dma_start", dict(out=out, in_=in_))], tag, kind="dma", dur=dur, pre=pre)
 
 
 def sums(out, Z, src, o, e, stop):
@@ -306,7 +351,7 @@ LAST = c(15, 64, 16)
 
 
 def setup():
-    dma("Y", r("wdi"), r("wd"), 2000, "load")
+    x0 = dma("Y", r("wdi"), r("wd"), 2000, "load")
     dma("S", r("wti"), r("wt"), 2000, "load")
     dma("Y", r("rec", c(0, 2048)), r("xt", c(0, 2048)), 4300, "load")
     dma("S", r("rec", c(2048, 4096)), r("xt", c(2048, 4096)), 4300, "load")
@@ -321,7 +366,7 @@ def setup():
     tt(r("mS"), r("tA"), r("BO"), Op.mult)
     for o, i, k in (("I3", "mI", 3232.0), ("I2", "mI", 2080.0), ("nI", "mI", -1.0),
                     ("BO3", "BO", 3232.0), ("BO2", "BO", 2080.0), ("nB", "mI", -1.0 if OPT["cb"] == "S" else -2.0),
-                    ("I5", "mI", 512.0), ("nI5", "mI", -512.0), ("I2k", "mI", 2048.0)) + (("bI", "mI", 1.0), ("nbI", "mI", -1.0), ("n2I", "mI", -2.0)) * bool(SOLO):
+                    ("I5", "mI", 512.0), ("nI5", "mI", -512.0)) + (("bI", "mI", 1.0), ("nbI", "mI", -1.0), ("n2I", "mI", -2.0)) * bool(SOLO):
         S(r(o), r(i), "set", scale=k)
     for k, (o, a, b, a2, b2) in enumerate((("mF", "I3", "mI", "I2", "mS"), ("mG", "I2", "mI", "I3", "mS"),
                                            ("SmI", "nI", "mI", "mI", "mS"), ("ISh", "mI", "mI", "mS", "nI"))):
@@ -329,19 +374,21 @@ def setup():
         P([mm(x, r(a), r(b), True, False), mm(x, r(a2), r(b2), False, True)], "set")
         S(r(o), x, "set")
     for h in "01":
-        ts(r("la" + h), r("wdi", c(64 * int(h), 64 * int(h) + 64)), -2048.0, Op.add)
+        ts(words(0, h), r("wdi", c(64 * int(h), 64 * int(h) + 64)), -2048.0, Op.add)
     ms(r("Z1"), 0.0)
-    cp(r("Z1", c(15, 143, 16)), r("BO", c(0, 128, 16)))
-    for o, k in (("Z2", 4096.0),) + (("N1", -1.0), ("N2", -4096.0)) * bool(RELU):
+    ts(r("Z1", c(15, 143, 16)), r("BO", c(0, 128, 16)), 2048.0, Op.mult)
+    for o, k in (("Z2", 2.0),) + (("N1", -1.0), ("N2", -2.0)) * bool(RELU):
         S(r(o), r("Z1"), "set", scale=k)
-    cp(r("wcol"), r("wti"))
+    ts(r("wcol"), r("wti"), 1.0 / 2048, Op.mult)
     S(r("ZU"), r("Z1"), "set", scale=r("wcol"))
     ms(r("onh"), 1.0)
     ms(r("c48"), 48.0)
-    ms(r("C2k"), 2048.0)
-    ms(r("C8k"), 8192.0)
-    ms(r("CA", c(0, 64)), 2080.0)
-    ms(r("CA", c(64, 128)), 3232.0)
+    for o in ("CA", "CN", "yes", "B0", "B1", "gp0", "gp1"):
+        ms(r(o), 0.0)
+    ms(r("CN", c(129, 256, 2)), 2048.0)
+    ms(r("yes", c(1, 17, 15)), 1.0)
+    ms(r("CA", c(0, 128, 2)), 2080.0)
+    ms(r("CA", c(128, 256, 2)), 3232.0)
     I(r("CKi"), [[16, 4], [1, 16]], 0, 64)
     for o, pat, base in (("PD", [[64, 2], [4, 4]], 0), ("CKa", [[0, 4], [-4, 16]], 61 if OPT["cb"] == "S" else 62),
                          ("CKb", [[0, 4], [-2048, 16]], 15 * 2048), ("RD", [[0, 2], [512, 4]], 0)):
@@ -364,7 +411,7 @@ def setup():
         ms(r(o), 0.0)
         ms(r(o, c(0, 64, 16)), v)
     for q, (pat, base) in enumerate((([[1, 16], [1, 2], [0, 2]], 1), ([[1, 16], [1, 2], [0, 2]], 15), ([[1, 16], [1, 2], [256, 2]], 0),
-                                     ([[1, 16], [0, 2], [-256, 2]], 257))):
+                                     ([[1, 16], [0, 2], [0, 2]], 1) if OPT.get("nc") else ([[1, 16], [0, 2], [-256, 2]], 257))):
         I(r("tabi", c(64 * q, 64 * q + 64)), pat, base, 1)
     ts(r("tabj"), r("tabi"), 0x10F, AND)
     ts(r("tab"), r("tabj"), 0, Op.is_equal)
@@ -377,8 +424,12 @@ def setup():
         gcopy(r("ohJ", c(k, 2 * k)), r("ohJ", c(0, k)), k)
 
 
-def offsets(t, h, tag):
-    ts(r("Xs" + h), r("Xi" + h), 5, SAR, 4095, AND, "s" + tag)
+def words(t, h):
+    return r(LAND[t] + h, c(1, 128, 2))
+
+
+def offsets(t, h, tag, X):
+    ts(r("Xs" + h), X, 5, SAR, 4095, AND, "s" + tag)
     if t == 0:
         cp(r("lu" + h), r("Xs" + h, ind=("PERM", A_)), "u" + tag)
     else:
@@ -388,118 +439,120 @@ def offsets(t, h, tag):
 def front(t, hh):
     h = AT["half"] = str(hh)
     win = c(0, 4096 + 32 * (t > 0))
-    al = r(LAND[t] + h)
+    al = words(t, h)
     pA, pW, pE, pv, cb = "pA" + h, "pW" + h, "pE" + h, "pv" + h, "cb" + h
-    P([mm(r(pA, c(64 * k, 64 * k + 64)), r(m), al) for k, m in enumerate(("mS", "mF", "mG"))], "lists")
-    tt(r("M" + h), al, r(pA, c(0, 64)), Op.mult, "M")
+    Wn = r(pE, 2, c(64, 128))
+    AT["visit"] = t or -1
+    P([mm(Wn, r("mS"), al)], "lists")
+    P([mm(r(pA, c(64, 128)), r("mF"), al), mm(r(pA, c(128, 192)), r("mG"), al)], "lin")
+    tt(r("M" + h), al, Wn, Op.mult, "M")
     tt(r("Xi" + h, c(0, 64)), r("M" + h), r(pA, c(64, 128)), Op.add, "Xf")
     tt(r("Xi" + h, c(64, 128)), r("M" + h), r(pA, c(128, 192)), Op.add, "Xg")
-    offsets(t, h, "1")
-    P([mm(r(pA, c(192, 256)), r("SmI"), al)] + [mm(r(pA, c(k, k + 64)), r("mI"), al) for k in (384, 448) if OPT["pr"] == "S"], "keep")
+    offsets(t, h, "1", r("Xi" + h))
+    AT["visit"] = t
+    P([mm(r(pA, c(192, 256)), r("SmI"), al)], "keep")
     gathers(h, "f", "e", win)
-    pK, pU, E = r(pA, c(256, 320)), r(pA, c(320, 384)), r(pE, A_, c(0, 16))
+    pU, E = r(pA, c(320, 384)), r(pE, 0, c(0, 64))
     P([mm(pU, r("I5"), r("CKU"), True, False)], "U0")
     for k, o, e in cuts([32, 32]):
         P(sums(pU, "ZU", "f" + h, o, e, e == 64), "U" + k)
-    P([mm(pK, r("mI"), r("CK1"), True, False), mm(pK, r("I5"), r("C8k"), False, False)], "Kc")
-    P([mm(E, r("nI"), r("C2k"), True, False)], "E0")
+    P([mm(E, r("mI"), r("CK1"), True, False)], "E0")
     abs_sums(E, "Z1", "N1", h, "f", "e", "E")
-    (cp if OPT.get("pv") == "V" else S)(r(pv, A_, c(1, 17)), E, "pv")
-    if OPT["cb"] == "V2":
-        tt(r(cb, A_, c(1, 15)), r(pv, A_, c(1, 15)), r(pE, A_, c(2, 16)), Op.is_lt, "cb")
-        tt(r(cb, A_, c(0, 16, 15)), r(pv, A_, c(16, 14, -1)), r(pv, A_, c(2, 0, -1)), Op.is_lt, "cw")
-    elif OPT["cb"] == "P":
-        S(r(pv, A_, c(0, 18, 17)), r(pE, A_, c(15, None, -15)), "pw")
-        tt(r(cb), r(pv, A_, c(0, 16)), r(pv, A_, c(2, 18)), Op.is_lt, "cb")
-    else:
-        P([mm(r(pE, A_, c(16, 32)), r("mI"), r("C8k"), True, False), mm(r(pE, A_, c(16, 31)), r("mI"), r(pv, A_, c(2, 17)), False, False),
-           mm(r(pE, A_, 31), r("mI"), r(pv, A_, 1), False, False), mm(r(pE, A_, c(17, 32)), r("nI"), r(pv, A_, c(1, 16)), False, False),
-           mm(r(pE, A_, 16), r("nI"), r(pv, A_, 16), False, True)], "D")
-        if OPT["cb"] == "S":
-            S(r(cb), r(pE, A_, c(16, 32)), "cb", AF.Sign, bias=-8192.5)
-        else:
-            ts(r(cb), r(pE, A_, c(16, 32)), 8192.0, Op.is_gt, tag="cb")
-    P([mm(pK, r("I2k"), r(pv, A_, c(1, 17)), False, False)], "Ka")
+    pK = r(pW, c(384, 448))
+    scan(r("MU" + h, c(0, 64)), r("SMa"), E, Op.add, Op.max, "max")
+    cp(r(pv), E, "pv")
+    ts(r("pw" + h), E, 100.0, Op.add, tag="pw")
+    tt(r("ne" + h), r("MU" + h, c(0, 64)), E, Op.not_equal, "ne")
+    P([mm(pK, r("mI"), r("CK1"), True, False)], "Kc")
+    tt(r(cb, A_, c(1, 15)), r(pv, A_, c(0, 14)), r(pv, A_, c(2, 16)), Op.is_lt, "cb")
+    tt(r(cb, A_, c(0, 16, 15)), r("pw" + h, A_, c(15, 13, -1)), r(pv, A_, c(1, None, -1)), Op.is_lt, "cw")
     P([mm(pK, r("nB"), r(cb), False, True)], "Kb")
-    scan(r("MU" + h, c(0, 64)), r("SMa"), pK, Op.add, Op.max, "max")
-    tt(r("ne" + h), r("MU" + h, c(0, 64)), pK, Op.not_equal, "ne")
     scan(r("MU" + h, c(64, 128)), r("ne" + h), pU, Op.mult, Op.max, "sel")
-    for k, tag in (((c4, "k"), (c8, "u")) if OPT["sp"] else ((c(0, 8), ""),)):
-        ts(r("cc", hh, k), r("MU" + h, c(15 + 16 * k.start, 16 * k.stop, 16)), 1023, AND, tag="cc" + tag)
-        cp(r("cu" + h, k), r("cc", hh, k), "cu" + tag)
-    P([mm(r(pW, c(0, 128)), r("mI"), r("CA"), True, False)], "Wc")
+    ts(r("cc", hh, c8), r("MU" + h, c(79, 128, 16)), 1023, AND, tag="ccu")
+    cp(r("cu" + h, c8), r("cc", hh, c8), "cuu")
+    scan(r("cd" + h), r("ne" + h), pK, Op.mult, Op.max, "code")
+    cp(r("cu" + h, c4), r("cd" + h, LAST), "cuk")
     for k, tag in ((0, "pb"), (64, "pa")):
-        if OPT["pr"] == "S":
-            S(r("mk" + h, c(k, k + 64)), r("tab", c(k, k + 64), ind=("cu" + h, c4)), tag)
-        else:
-            tt(r("pr" + h, c(k, k + 64)), r("tab", c(k, k + 64), ind=("cu" + h, c4)), al, Op.mult, tag)
-    if OPT["pr"] == "S":
-        tt(r("pr" + h), r("mk" + h), r(pA, c(384, 512)), Op.mult, "pr")
+        tt(r("pr" + h, c(k, k + 64)), r("tab", c(k, k + 64), ind=("cu" + h, c4)), al, Op.mult, tag)
+    S(r("M" + h), r(pA, c(192, 256)), "dW")
+    if OPT.get("nc"):
+        tt(r("dk" + h), r("tab", c(192, 256), ind=("cu" + h, c4)), r("M" + h), Op.mult, "dk")
+        S(r("mx" + h), r("tab", c(128, 192), ind=("cu" + h, c4)), "mp")
+    if OPT.get("xs"):
+        P([mm(r(pW, c(0, 256)), r("mI"), r("CA"), True, False)], "Wc")
+        P([mm(r(pW, c(0, 256, 2)), r("BO"), r("pr" + h), False, False), mm(r(pW, c(1, 128, 2)), r("BO3"), r("pr" + h, c(0, 64)), False, False),
+           mm(r(pW, c(129, 256, 2)), r("BO2"), r("pr" + h, c(64, 128)), False, True)], "W")
+        for k, tag in ((1, "B"), (129, "C")):
+            S(r("B" + h, c(k, k + 127, 2)), r("stock", c(512, 1536), ind=("cu" + h, c8)), tag, bias=-2048.0)
+        scan(r("X2" + h), r("B" + h), r(pW, c(0, 256)), Op.mult, Op.add, "Xl")
+        offsets(t, h, "3", r("X2" + h, c(1, 256, 2)))
+        return
+    P([mm(r(pW, c(0, 128)), r("mI"), r("CA", c(0, 256, 2)), True, False)], "Wc")
     P([mm(r(pW, c(0, 128)), r("BO"), r("pr" + h), False, True)], "W")
     P([mm(r(pE, 0, c(64, 128)), r("BO3"), r("pr" + h, c(0, 64))), mm(r(pE, 1, c(64, 128)), r("BO2"), r("pr" + h, c(64, 128)))], "L")
-    if OPT.get("B") == "V":
-        ts(r("B" + h), r("stock", c(512, 1536), ind=("cu" + h, c8)), -2048.0, Op.add, tag="B")
-    else:
-        S(r("B" + h), r("stock", c(512, 1536), ind=("cu" + h, c8)), "B", bias=-2048.0)
-    if OPT.get("dl") == "V":
-        S(r("M" + h), r(pA, c(192, 256)), "dW")
-    tt(r("X" + h, c(0, 64)), r("B" + h), r(pW, c(0, 64)), Op.mult, "Xy")
-    tt(r("X" + h, c(64, 128)), r("B" + h), r(pW, c(64, 128)), Op.mult, "Xz")
+    B = r("B" + h, c(1, 128, 2))
+    S(B, r("stock", c(512, 1536), ind=("cu" + h, c8)), "B", bias=-2048.0)
+    tt(r("X" + h, c(0, 64)), B, r(pW, c(0, 64)), Op.mult, "Xy")
+    tt(r("X" + h, c(64, 128)), B, r(pW, c(64, 128)), Op.mult, "Xz")
     tt(r("Xi" + h), r("X" + h), r(pE, c(0, 2), c(64, 128)), Op.add, "Xl")
-    offsets(t, h, "3")
+    offsets(t, h, "3", r("Xi" + h))
 
 
 def back(t, hh):
     h = AT["half"] = str(hh)
     end = t + 1 == NV
-    al = r(LAND[t] + h)
-    pA, pW, pE = "pA" + h, "pW" + h, "pE" + h
-    k2, R, ng = r(pW, c(448, 512)), r(pE, A_, c(32, 48)), c(4 * hh, 4 * hh + 4)
+    al = words(t, h)
+    pW = "pW" + h
+    k2, ng = r(pW, c(448, 512)), c(4 * hh, 4 * hh + 4)
     P([mm(k2, r("mI"), r("CK2"), True, False)], "F0")
     abs_sums(k2, "Z2", "N2", h, "y", "d", "F")
     scan(r("m2" + h), r("SMi"), k2, Op.add, Op.min, "min")
     tt(r("ng", ng), r("m2" + h, LAST), r("MU" + h, LAST), Op.is_ge, "ng")
     ts(r("FI", hh, c4), r("m2" + h, LAST), 1023, AND, tag="J")
-    tt(r("FI", hh, c12), r("cc", hh, c4), r("ng", ng), Op.add, "co")
-    if h in OPT.get("fu", ""):
-        cp(r("FU" + h, c(0, 8)), r("FI", hh, c(0, 8)), "FU")
-        cp(r("FU" + h, c12), r("FI", hh, c12), "FV")
+    cp(r("FU" + h, c(0, 8)), r("FI", hh, c(0, 8)), "FU")
+    gp = r("gp" + h, c(1, 128, 2))
+    if OPT.get("nc"):
+        cp(r("FU" + h, c12), r("ng", ng), "FV")
+        tt(r("dl" + h), r("yes", c(0, 16), ind=("FU" + h, c12)), r("dk" + h), Op.mult, "dl")
+        tt(gp, r("yes", c(16, 32), ind=("FU" + h, c12)), r("mx" + h), Op.mult, "gp")
     else:
-        cp(r("FU" + h, c(0, 12)), r("FI", hh), "FU")
+        tt(r("FI", hh, c12), r("cd" + h, LAST), r("ng", ng), Op.add, "co")
+        cp(r("FU" + h, c12), r("FI", hh, c12), "FV")
+        tt(r("dl" + h), r("tab", c(192, 256), ind=("FU" + h, c12)), r("M" + h), Op.mult, "dl")
+        S(gp, r("tab", c(128, 192), ind=("FU" + h, c12)), "gp")
     if not end:
         P([mm(r("pC", c(0, 1)), r("onh"), r("ng", c(k, k + 1)), False, k == 7) for k in range(4 * hh, 4 * hh + 4)], "A")
-    if OPT.get("dl") != "V":
-        S(r("mx" + h), r("tab", c(192, 256), ind=("FU" + h, c12)), "mx")
-    S(r("gp" + h), r("tab", c(128, 192), ind=("FU" + h, c12)), "gp")
-    tt(r("bj" + h), r("ohJ", ind=("FU" + h, c4)), r("B" + h), Op.mult, "bj")
-    P([mm(r(pW, c(256, 320)), r("nI"), al, True, False)], "Ba")
-    P([mm(r(pW, c(256, 320)), r("BO"), r("bj" + h), False, True)], "Bb")
-    if OPT.get("dl") == "V":
-        tt(r("dl" + h), r("tab", c(192, 256), ind=("FU" + h, c12)), r("M" + h), Op.mult, "dl")
+    tt(r("bj" + h), r("ohJ", ind=("FU" + h, c4)), r("B" + h, c(1, 128, 2)), Op.mult, "bj")
+    Q = "pE" + h
+    P1, R = r(Q, 3, c(0, 128, 2)), r(Q, 3, c(1, 128, 2))
+    P([mm(r(Q, 3), r("mI"), r("CN", c(128 * end, 128 * end + 128)), True, False), mm(P1, r("nI"), al, False, False),
+       mm(R, r("mI"), al, False, False)], "Ba")
+    P([mm(R, r("ISh"), r("dl" + h), False, False)], "Rb")
+    P([mm(P1, r("BO"), r("bj" + h), False, True)], "Bb")
+    if end:
+        new = r("nw" + h)
+        tt(r("Y" + h), gp, P1, Op.mult, "Y")
+        tt(new, r("Y" + h), R, Op.add, "new")
     else:
-        tt(r("dl" + h), r("mx" + h), r(pA, c(192, 256)), Op.mult, "dl")
-    P([mm(R, r("mI"), al, True, False)] + [mm(R, r("mI"), r("C2k"), False, False)] * end, "Ra")
-    P([mm(R, r("ISh"), r("dl" + h), False, True)], "Rb")
-    tt(r("Y" + h), r("gp" + h), r(pW, c(256, 320)), Op.mult, "Y")
-    new = r(("nw" if end else "snd") + h)
-    tt(new, r("Y" + h), R, Op.add, "new")
+        new = r("snd" + h)
+        scan(new, r("gp" + h), r(Q, 3), Op.mult, Op.add, "new")
     sn = add("G", [("remote_dma", dict(to=LAND[t + 1] + h, in_=new))], "send", kind="send", dur=300)
     add("R", [], "recv", kind="recv", dur=0, pre=[sn], extra=[(LAND[t + 1] + h, cols(LAND[t + 1] + h, ()), True)])
     if not end:
-        S(r("Rs" + h), R, "Rs", bias=2048.0)
+        S(r("nw" + h), r("snd" + h, c(1, 128, 2)), "Rs", bias=2048.0)
     w = r("rec2", ind=("FU" + h, c8)) if end and hh == 0 else r("rec", c(2048 * hh, 2048 * hh + 2048), ind=("FU" + h, c8))
-    if OPT["nr"] == "S":
+    if h in OPT["nr"]:
         S(r("hq" + h), r("d" + h, ind=("FU" + h, c4)), "hq", scale=0.5, bias=1535.75)
         S(r("yj" + h), r("y" + h, ind=("FU" + h, c4)), "yj")
         S(r("hb" + h), r("hq" + h), "hb", bias=-1536.0)
-        tt(w, r("yj" + h), r("hb" + h), Op.add, "sr")
+        tt(w, r("yj" + h), r("hb" + h), Op.add, "re" if end else "sr")
     else:
         if h in OPT.get("hd", ""):
             ts(r("hd" + h), r("d" + h, ind=("FU" + h, c4)), 0.5, Op.mult, -0.25, Op.add, "hd")
         else:
             S(r("hd" + h), r("d" + h, ind=("FU" + h, c4)), "hd", scale=0.5, bias=-0.25)
         tt(r("nr" + h), r("y" + h, ind=("FU" + h, c4)), r("hd" + h), Op.add, "nr")
-        cp(w, r("nr" + h), "sr")
+        cp(w, r("nr" + h), "re" if end else "sr")
     if hh == 0 and not end:
         S(r("rec", c(4096, 4128)), r("rec", c(0, 32)), "rep")
 
@@ -516,10 +569,7 @@ def stock(t, hs):
     for hh in hs:
         h = AT["half"] = str(hh)
         w = r("stock", c(1024 * hh, 1024 * hh + 1024), ind=("SU", c(4 * hh, 4 * hh + 4)))
-        if end:
-            cp(w, r("nw" + h), "ss")
-        else:
-            tt(w, r("Y" + h), r("Rs" + h), Op.add, "ss")
+        cp(w, r("nw" + h), "se" if end else "ss")
 
 
 def build():
@@ -528,7 +578,7 @@ def build():
         end = t + 1 == NV
         AT["visit"], AT["half"] = t, ""
         if end:
-            dma("Y", r("rec2"), r("rec", c(0, 2048)), 3000, "rec2")
+            dma("Y", r("rec2"), r("rec", c(0, 2048)), 3500, "rec2")
         for hh in range(H):
             front(t, hh)
         for h in "01":
@@ -543,16 +593,19 @@ def build():
         for hh in range(H):
             back(t, hh)
         AT["half"] = ""
-        if not end:
+        if not end and OPT.get("Av"):
+            ts(r("nq"), r("pC", c(0, 1)), -1.0, Op.mult, 15.75, Op.add, "nq")
+            tt(r("Acol"), r("pC", c(0, 1)), r("nq"), Op.add, "Acol")
+        elif not end:
             S(r("nq"), r("pC", c(0, 1)), "nq", scale=-1.0, bias=15.75)
             S(r("Acol"), r("pC", c(0, 1)), "Acol", AF.Identity, bias=r("nq"))
         for hs in ([[0], [1]] if end else [[0, 1]]):
             stock(t, hs)
     for hh in range(H):
         h = AT["half"] = str(hh)
-        dma("Y", r("yx", c(2048 * hh, 2048 * hh + 2048)), r("rec", c(2048, 4096)) if hh else r("rec2"), 3000, "yx")
-        dma("Y", r("yp", c(512 * hh, 512 * hh + 512)), r("stock", c(512 + 512 * hh, 1024 + 512 * hh)), 2500, "yp")
-        dma("Y", r("yw", c(64 * hh, 64 * hh + 64)), r("le" + h), 2000, "yw")
+        dma("Y", r("yx", c(2048 * hh, 2048 * hh + 2048)), r("rec", c(2048, 4096)) if hh else r("rec2"), 2800, "yx")
+        dma("Y", r("yp", c(512 * hh, 512 * hh + 512)), r("stock", c(512 + 512 * hh, 1024 + 512 * hh)), 2250, "yp")
+        dma("Y", r("yw", c(64 * hh, 64 * hh + 64)), r("le" + h), 1200, "yw")
 
 
 def busy(x, d):
@@ -561,7 +614,7 @@ def busy(x, d):
 
 def schedule():
     n = len(NODES)
-    by = {(x["visit"], x["key"]): i for i, x in enumerate(NODES)}
+    by = {(x["visit"], x["key"]): i for i, x in enumerate(NODES) if x["visit"] >= 0}
     for names in ORDER.values():
         line = [by.get((t + (k[0] == "+"), k.lstrip("+"))) for t in range(-1, NV) for k in names.split()]
         line = [i for i in line if i is not None]
@@ -581,7 +634,7 @@ def schedule():
     way = [0.0] * n
     for i in reversed(top):
         way[i] = NODES[i]["dur"][0] + max([way[j] + 50.0 for j in succ[i]], default=0.0)
-    w1, w2 = MODELS[0][6:]
+    w1, w2 = MODELS[0][6], {e: MODELS[0][{"P": 9, "S": 13}.get(e, 7)] for e in "VSPGYR"}
     rt = [0.0] * n
     ready, free, order = {}, {}, []
     for i in range(n):
@@ -598,7 +651,7 @@ def schedule():
         order.append(i)
         for j in succ[i]:
             left[j] -= 1
-            rt[j] = max(rt[j], x["t1"] + (0.0 if i not in NODES[j]["preds"] else w1 if NODES[j]["eng"] == e else w2))
+            rt[j] = max(rt[j], x["t1"] + (0.0 if i not in NODES[j]["preds"] else w1 if NODES[j]["eng"] == e else w2[e]))
             if left[j] == 0:
                 ready.setdefault(NODES[j]["eng"], []).append(j)
     return order

import numpy as np
from concourse.mybir import AluOpType, ActivationFunctionType

Op = AluOpType
AF = ActivationFunctionType
NV, STEP, H = 4, 3, 2
CH = {q: ([16, 16, 16, 16], [16, 16, 16, 8, 8], [16, 16, 16, 8, 8]) for q in ("f0", "f1", "y0", "y1")}
OWN = []
SOLO = []
SEL = dict(cb="V2", pr="V", nr="V", nc=1, xs=1, own=["fa0", "fa1", "ya0"], solo=["eb1", "db0"], ch={q: ([16, 20, 16, 12],) * 3 if q in ("f1", "y0") else ([12, 20, 20, 12],) * 2 + ([32, 20, 12],) for q in CH})
RELU = []
OPT = {"cb": "V2", "pr": "V", "nr": "V", "sp": 0}
ORDER = {
    "V": "ee0 ed0 ea0 eb0 ec0 M1 Xg1 Xf1 s11 u11 fa1 ea1 eb1 ec1 max0 cck0 ne0 cuk0 sel0 ccu0 ed1 cuu0 pr0 ee1 Xy0 Xz0 Xl0 s30 u30 ya0 da0 max1 cck1 ne1 cuk1 sel1 dc0 db0 ccu1 pr1 cuu1 dd0 de0 Xy1 Xz1 Xl1 s31 r31 u31 r7 rl min0 ng0 J0 co0 FU0 bj0 da1 dl0 Y0 db1 new0 dc1 dd1 de1 nr0 SI0 sr0 min1 ng1 J1 co1 FU1 bj1 dl1 nr1 Y1 +M0 new1 SU0 +Xg0 +Xf0 sr1 +s10 SI1 +u10 SU1 ss0 ss1",
    "S": "fb0 fc0 |ed0 |eb0 |ea0 |ec0 |ee0 fb1 pv0 fc1 cb0 fd1 |ea1 |eb1 pb0 pa0 |ec1 B0 |ed1 |ee1 pv1 yd0 cb1 yc0 yb0 pa1 pb1 |da0 |dc0 |db0 B1 |dd0 |de0 ya1 yb1 mx0 gp0 yc1 yd1 |db1 |da1 |dc1 |dd1 |de1 hd0 rep0 Rs0 mx1 hd1 gp1 nq Acol Rs1 +fd0 +fa0",
    "P": "lists1 U0 Ea0 Eb0 Ec1 Kc0 D0 keep1 Ra0 Ka0 Kb0 U1 W0 Kc1 Ea1 Eb1 Fc0 D1 Ka1 Kb1 W1 Fa0 Fb0 Sl0 Ba0 Bb0 A0 Fc1 Rb0 Fa1 Fb1 Ba1 A1 Ra1 Bb1 +lists0 Rb1 +Wc0 Sl1 +Ac +Wc1 +keep0 +Ec0",
}
ORDER = {
    "V": "ea0 eb0 ec0 ed0 M1 Xf1 Xg1 s11 u11 fa1 cb0 cw0 ea1 max0 eb1 ne0 cck0 sel0 cuk0 ec1 ccu0 pr0 cuu0 ed1 Xz0 Xy0 Xl0 s30 u30 cb1 ya0 cw1 da0 max1 db0 ne1 cck1 sel1 cuk1 ccu1 dc0 cuu1 pr1 dd0 r31 Xy1 Xz1 r7 Xl1 s31 u31 min0 rl ng0 J0 co0 FU0 FV0 bj0 dl0 da1 Y0 new0 db1 dc1 dd1 nr0 sr0 min1 ng1 J1 co1 FU1 FV1 bj1 dl1 SI0 nr1 Y1 new1 sr1 SU0 +M0 SI1 +Xg0 +Xf0 +s10 +u10 SU1 ss0 ss1",
    "S": "fd0 |ea0 |eb0 |ec0 |ed0 pv0 fb1 fc1 |ea1 fd1 |eb1 pb0 pa0 |ec1 B0 |ed1 pv1 dW0 yb0 yd0 |da0 yc0 |db0 pa1 pb1 B1 |dc0 |dd0 ya1 yb1 gp0 yc1 hd0 |da1 yd1 |db1 |dc1 |dd1 dW1 hd1 gp1 nq Acol Rs0 rep0 Rs1 +fa0 +fb0 +fc0",
    "P": "E00 lists1 Ea0 E01 Eb0 Ec0 Ed0 Ub0 Kc0 Ka0 keep1 Kb0 U01 Ua1 Wc0 Ea1 Ub1 Kc1 W0 L0 Eb1 Ec1 Ed1 Ra0 Ka1 F00 Kb1 W1 L1 Fa0 Fb0 Fc0 Fd0 Sl0 F01 Ra1 Ba0 Bb0 Rb0 Fa1 A0 Fb1 Fc1 Fd1 Ba1 A1 Bb1 Rb1 +lists0 Sl1 +keep0 +Ac +Wc1 +U00 +Ua0",
}
ORDER = {
    "V": "ed0 M1 Xg1 Xf1 s11 u11 cb0 cw0 fa1 max0 ea1 ne0 cck0 sel0 cuk0 ccu0 pa0 cuu0 pb0 ec1 ed1 Xz0 Xy0 Xl0 s30 u30 ya0 cw1 cb1 da0 max1 ne1 cck1 sel1 cuk1 ccu1 pa1 cuu1 pb1 dc0 dd0 Xy1 Xz1 Xl1 r31 s31 u31 rl r7 min0 ng0 J0 co0 FU0 FV0 bj0 dl0 da1 Y0 new0 db1 dc1 dd1 nr0 sr0 min1 ng1 J1 co1 FU1 FV1 bj1 dl1 nr1 +M0 Y1 +Xg0 +Xf0 new1 SI0 +s10 sr1 +u10 SU0 SI1 SU1 ss0 ss1 +ea0 +eb0 +ec0",
    "S": "|eb0 |ec0 |ed0 pv0 eb1 fb1 fc1 |ea1 fd1 B0 |eb1 |ec1 |ed1 dW0 pv1 db0 yc0 yb0 yd0 |da0 B1 |db0 |dc0 |dd0 ya1 yb1 gp0 yc1 yd1 |da1 |db1 hd0 |dc1 |dd1 dW1 rep0 hd1 gp1 nq Rs0 Acol Rs1 +fa0 +fb0 +fc0 +|ea0 +fd0",
    "P": "Ed0 Ub0 Kc0 Ka0 keep1 Kb0 U01 Wc0 Deb1 Ua1 Ea1 L0 W0 Ub1 Kc1 Eb1 Ec1 Ed1 Ka1 Kb1 F00 Ddb0 Ra0 W1 L1 Fa0 Fb0 Fc0 Fd0 F01 Ra1 Ba0 Sl0 Bb0 Rb0 A0 Fa1 Fb1 Fc1 Fd1 Ba1 A1 +lists0 Bb1 Rb1 +E00 Sl1 +keep0 +U00 +Wc1 +Ac +E01 +Ua0 +lists1 +Ea0 +Eb0 +Ec0",
}
ORDER = {
    "V": "Xg1 s11 u11 fa1 cb0 cw0 ea1 max0 ne0 cck0 sel0 cuk0 ccu0 pa0 cuu0 pb0 ec1 Xy0 Xz0 ed1 Xl0 s30 u30 ya0 cw1 cb1 da0 max1 ne1 cck1 sel1 cuk1 ccu1 pb1 cuu1 pa1 dc0 dd0 Xz1 Xy1 Xl1 r31 s31 u31 rl min0 r7 ng0 J0 co0 FU0 FV0 bj0 dl0 da1 SI0 Y0 new0 db1 dc1 dd1 nr0 SU0 sr0 re0 se0 min1 ng1 J1 co1 FU1 FV1 bj1 dl1 +M0 Y1 +Xg0 +Xf0 new1 +s10 sr1 +u10 SI1 SU1 ss1 ss0 re1 +ea0 se1 +eb0 +ec0 +ed0 +M1 +Xf1",
    "S": "fa0 fb0 fc0 fd0 |ea0 |eb0 |ec0 |ed0 pv0 fb1 eb1 fc1 dW0 fd1 B0 |eb1 |ea1 |ec1 |ed1 pv1 db0 yc0 yb0 yd0 |da0 B1 |db0 |dc0 |dd0 ya1 yb1 gp0 yc1 yd1 |da1 |db1 hd0 |dc1 |dd1 Rs0 dW1 rep0 gp1 nq yj1 hq1 Acol hb1 Rs1",
    "P": "Ac lists1 lin1 Ea0 Eb0 Ec0 Ed0 Ua0 Ub0 Kc0 Ka0 keep1 Kb0 U01 Wc0 Deb1 Ua1 W0 L0 E01 Ub1 Kc1 Eb1 Ea1 Ec1 Ed1 F00 Ka1 Ra0 Kb1 Ddb0 W1 Fa0 L1 Fb0 F01 Fc0 Fd0 Ba0 Sl0 A0 Bb0 Rb0 Fa1 Fb1 Fc1 Fd1 Ba1 Ra1 A1 +lists0 Bb1 +lin0 Rb1 +E00 +keep0 +U00 Sl1 +Wc1",
}
ORDER = {
    "V": "Xf1 Xg1 s11 u11 fa1 cw0 cb0 ea1 max0 ne0 cck0 sel0 cuk0 ccu0 pa0 cuu0 pb0 ec1 Xy0 Xz0 ed1 Xl0 s30 u30 ya0 cw1 cb1 da0 max1 ne1 cck1 sel1 cuk1 ccu1 pb1 pa1 cuu1 dc0 dd0 Xy1 Xz1 Xl1 s31 r31 u31 rl r7 min0 ng0 J0 co0 FU0 FV0 bj0 dl0 da1 Y0 SI0 new0 db1 dc1 dd1 SU0 nr0 re0 se0 sr0 min1 ng1 J1 co1 FU1 FV1 bj1 dl1 +M0 +Xf0 +Xg0 Y1 +s10 new1 sr1 +u10 re1 SI1 SU1 ss1 se1 ss0 +ea0 +eb0 +ec0 +ed0 +M1",
    "S": "fb0 fc0 fd0 |ea0 |eb0 |ec0 pv0 fb1 eb1 fc1 fd1 B0 |eb1 |ea1 |ec1 |ed1 dW0 pv1 db0 yb0 yc0 yd0 |da0 B1 |db0 |dc0 |dd0 ya1 yb1 gp0 yc1 yd1 hd0 |da1 |db1 |dc1 Rs0 rep0 dW1 gp1 hq1 yj1 hb1 nq Acol Rs1 +fa0",
    "P": "U00 Ac lists1 lin1 Ea0 Eb0 Ec0 Ua0 Ub0 Kc0 Ka0 Kb0 keep1 E01 U01 Wc0 Ua1 Deb1 W0 L0 Ub1 Kc1 Eb1 F00 Ea1 Ec1 Ed1 Ka1 Kb1 Ddb0 Ra0 W1 L1 Fa0 Fb0 Fc0 Fd0 Ra1 F01 Ba0 Sl0 A0 Bb0 Rb0 Fa1 Fb1 Fc1 Ba1 A1 +lists0 +lin0 Bb1 Rb1 +E00 +keep0 +Wc1 Sl1",
}
ORDER = {
    "V": "eb0 ec0 ed0 M1 Xg1 Xf1 s11 u11 fa1 cw0 cb0 ea1 max0 ne0 cck0 sel0 cuk0 ccu0 pa0 cuu0 pb0 Bi0 ec1 Xy0 Xz0 ed1 Xl0 s30 u30 ya0 cw1 cb1 da0 max1 ne1 cck1 sel1 cuk1 ccu1 pa1 cuu1 pb1 Bi1 dc0 dd0 Xz1 Xy1 Xl1 s31 u31 r7 r31 min0 rl ng0 J0 co0 FU0 FV0 bj0 dl0 da1 SI0 Y0 nr0 new0 re0 SU0 db1 se0 dc1 dd1 sr0 min1 ng1 J1 co1 FU1 FV1 bj1 dl1 +M0 re1 +Xf0 +Xg0 Y1 +s10 new1 sr1 +u10 SI1 SU1 ss1 ss0 +ea0 se1",
    "S": "pv0 fb1 eb1 fc1 fd1 B0 |eb1 |ea1 |ec1 |ed1 dW0 pv1 db0 yb0 yc0 yd0 B1 |da0 |db0 |dc0 |dd0 dW1 ya1 yb1 gp0 hd0 yc1 yd1 |da1 |db1 |dc1 rep0 Rs0 hq1 gp1 nq yj1 hb1 Acol Rs1 +fa0 +fb0 +fc0 +fd0 +|ea0 +|eb0 +|ec0",
    "P": "E00 Ua0 lists1 lin1 Ea0 Eb0 Ec0 Wc0 keep1 Ub0 Kc0 Ka0 U01 Kb0 Deb1 E01 Ua1 W0 L0 Ub1 Eb1 F00 Ea1 Ec1 Ed1 Kc1 Ka1 Kb1 Ra0 Ddb0 L1 W1 Fa0 Fb0 Fc0 Fd0 Sl0 Ra1 Ba0 F01 A0 Bb0 Rb0 Fa1 Fb1 Fc1 Ba1 A1 +lists0 +lin0 Bb1 Rb1 Sl1 +keep0 +U00 +Wc1 +Ac",
}
ORDER = {
    "V": "M1 Xf1 Xg1 s11 u11 fa1 cw0 cb0 ea1 max0 ne0 cck0 sel0 cuk0 ccu0 pa0 cuu0 pb0 ec1 Xy0 Xz0 ed1 Xl0 s30 u30 ya0 cw1 cb1 da0 max1 ne1 cck1 sel1 cuk1 ccu1 pb1 cuu1 pa1 dc0 Xz1 Xy1 dd0 Xl1 r7 s31 r31 u31 rl min0 ng0 J0 co0 FU0 FV0 bj0 dl0 da1 Y0 SI0 new0 db1 dc1 dd1 nr0 SU0 re0 se0 sr0 min1 ng1 J1 co1 FU1 FV1 bj1 dl1 Y1 +M0 new1 +Xg0 +Xf0 sr1 +s10 +u10 re1 SI1 SU1 ss0 ss1 +ea0 se1 +eb0 +ec0 +ed0",
    "S": "|eb1 |ec1 |ed1 dW0 pv1 yb0 db0 yc0 yd0 B1 |da0 |db0 |dc0 |dd0 ya1 yb1 gp0 yc1 hd0 yd1 |da1 |db1 |dc1 Rs0 rep0 dW1 nq gp1 hq1 hb1 yj1 Rs1 Acol +fa0 +fb0 +fc0 +fd0 +|ea0 +|eb0 +|ec0 +pv0 +fb1 +eb1 +fc1 +fd1 +B0 +|ea1",
    "P": "E00 Ac keep0 Wc1 U00 Ua0 lists1 lin1 Ea0 Eb0 Ec0 Ub0 Kc0 Ka0 Kb0 keep1 U01 Wc0 E01 Ua1 Deb1 W0 L0 Ub1 Ea1 Eb1 Ec1 Ed1 Kc1 Ka1 Kb1 F00 Ddb0 W1 L1 Fa0 Fb0 Fc0 Fd0 Ra0 A0 F01 Ra1 Sl0 Ba0 Bb0 Rb0 Fa1 Fb1 Fc1 A1 Ba1 Bb1 +lists0 Rb1 +lin0 Sl1",
}
ORDER = {
    "V": "s11 u11 fa1 pv0 cb0 cw0 ea1 max0 ne0 cck0 sel0 cuk0 ccu0 pa0 cuu0 pb0 ec1 ed1 Xy0 Xz0 Xl0 s30 |ed1 u30 ya0 pv1 cb1 cw1 da0 max1 ne1 cck1 sel1 cuk1 ccu1 pa1 cuu1 pb1 dc0 dd0 Xz1 Xy1 |dd0 Xl1 r31 s31 u31 rl r7 min0 ng0 J0 co0 FU0 FV0 bj0 dl0 da1 Y0 new0 db1 dc1 SI0 hd0 SU0 dd1 nr0 |dc1 re0 se0 sr0 min1 ng1 J1 co1 FU1 FV1 bj1 dl1 +M0 hd1 +Xf0 nr1 Y1 +Xg0 new1 +s10 sr1 +u10 SI1 SU1 ss0 re1 se1 ss1 +ea0 +eb0 +ec0 +ed0 +M1 +Xf1 +Xg1 +|ec0",
    "S": "fa0 fb0 fc0 fd0 |ea0 |eb0 fb1 eb1 fc1 fd1 |ea1 B0 |eb1 |ec1 dW0 db0 yb0 yc0 yd0 |da0 B1 |db0 |dc0 ya1 yb1 gp0 yc1 yd1 |da1 |db1 Rs0 rep0 dW1 gp1 nq Acol Rs1",
    "P": "Ac lists1 lin1 Ua0 Wc0 Enc0 Ea0 Eb0 Ec0 Ub0 Kc0 Ka0 keep1 Kb0 E01 U01 Deb1 Ua1 W0 L0 Ub1 Kc1 Eb1 End1 F00 Ea1 Ec1 Ed1 Ka1 Kb1 Ddb0 Ra0 W1 L1 Fa0 Fnd0 Fb0 Fc0 Fd0 F01 Ba0 A0 Sl0 Ra1 Bb0 Rb0 Fa1 Fnc1 Fb1 Fc1 +lists0 +lin0 Ba1 A1 Bb1 Rb1 +E00 +keep0 +Wc1 +U00 Sl1",
}
ORDER = {
    "V": "eb0 ec0 M1 ed0 Xg1 Xf1 s11 u11 fa1 cb0 cw0 ea1 max0 ne0 sel0 cc0 cu0 ec1 pa0 pb0 ed1 Xy0 Xz0 Xl0 s30 u30 ya0 cw1 cb1 da0 max1 ne1 sel1 cc1 dc0 cu1 pb1 pa1 dd0 Xz1 Xy1 Xl1 s31 u31 r31 min0 rl ng0 J0 co0 FU0 r7 dl0 bj0 SI0 da1 Y0 new0 db1 dc1 dd1 nr0 SU0 sr0 re0 se0 min1 ng1 J1 co1 FU1 bj1 +M0 dl1 +Xg0 +Xf0 Y1 +s10 new1 sr1 +u10 re1 SI1 SU1 ss0 ss1 se1 +ea0",
    "S": "fa0 fb0 fc0 fd0 |ea0 |eb0 |ec0 pv0 fb1 fc1 eb1 fd1 B0 |eb1 |ec1 |ea1 |ed1 dW0 pv1 yd0 yc0 yb0 db0 |da0 B1 |dc0 |db0 |dd0 ya1 yb1 gp0 yc1 yd1 hd0 |da1 |db1 |dc1 dW1 rep0 Rs0 gp1 hq1 yj1 hb1 nq Acol Rs1",
    "P": "Ua0 lists1 lin1 Ub0 Ea0 Eb0 Ec0 keep1 U01 E01 Kc0 Wc0 Ka0 Kb0 Ua1 Deb1 Ub1 W0 L0 Eb1 Kc1 Ec1 Ea1 Ed1 F00 Ka1 Kb1 Ddb0 W1 Fa0 L1 Fb0 Fc0 Fd0 A0 Ba0 F01 Sl0 Ra0 Ra1 Bb0 Rb0 Fa1 Fb1 Fc1 A1 +lists0 +lin0 Ba1 Bb1 Rb1 +keep0 Sl1 +Wc1 +Ac +E00 +U00",
}
ORDER = {
    "V": "Xf1 Xg1 s11 u11 pv0 pw0 max0 cb0 cw0 ne0 fa1 sel0 code0 ccu0 cuk0 ec1 cuu0 pb0 pa0 ea1 ed1 Xl0 s30 u30 pv1 max1 ya0 pw1 ne1 cb1 cw1 sel1 da0 ccu1 code1 cuu1 cuk1 dc0 pb1 pa1 dd0 r7 dk0 r31 Xl1 dk1 s31 rl min0 u31 ng0 J0 FV0 FU0 dl0 bj0 gp0 db1 Y0 SI0 new0 da1 dc1 dd1 SU0 nr0 sr0 se0 re0 min1 ng1 J1 FV1 FU1 dl1 bj1 +M0 gp1 +Xg0 +Xf0 nr1 Y1 new1 +s10 sr1 SI1 +u10 SU1 re1 se1 ss1 ss0 +ea0 +eb0 +ec0 +ed0 +M1",
    "S": "fc0 fd0 |ea0 |eb0 |ec0 fc1 fb1 eb1 fd1 C0 B0 |eb1 |ea1 |ec1 |ed1 yb0 db0 yc0 dW0 yd0 |da0 |db0 C1 B1 |dc0 dW1 |dd0 mp0 yb1 ya1 mp1 yc1 hd0 yd1 |da1 |db1 |dc1 rep0 hd1 nq Acol Rs0 Rs1 +fa0 +fb0",
    "P": "Ac lists1 lin1 Kc0 Ea0 Eb0 Ec0 keep1 U01 Ub0 Kb0 E01 Ua1 Deb1 Wc0 W0 Eb1 Ea1 Ec1 Ed1 Kc1 Ub1 Kb1 F00 Ddb0 Wc1 Fa0 W1 Fb0 Fc0 Fd0 F01 Ba0 Sl0 A0 Rb0 Bb0 Fa1 Fb1 Fc1 Ba1 +lists0 +lin0 A1 Rb1 Bb1 +keep0 Sl1 +U00 +Ua0 +E00",
}
ORDER = {
    "V": "u11 pv0 pw0 max0 cb0 cw0 ne0 fa1 sel0 code0 ec1 ccu0 cuk0 cuu0 pa0 pb0 ea1 ed1 Xl0 s30 u30 pv1 max1 pw1 ya0 ne1 cb1 cw1 sel1 da0 ccu1 code1 cuu1 cuk1 dc0 pa1 pb1 dd0 dk0 r31 r7 Xl1 rl s31 dk1 min0 u31 ng0 J0 FV0 FU0 dl0 bj0 SI0 gp0 db1 Y0 new0 da1 dc1 dd1 nr0 sr0 SU0 se0 re0 min1 ng1 J1 FV1 FU1 dl1 bj1 +M0 gp1 +Xf0 +Xg0 nr1 Y1 new1 +s10 sr1 SI1 +u10 re1 SU1 +fa0 se1 ss1 +ea0 +eb0 +ec0 +ed0 +M1 +Xf1 +Xg1 ss0 +s11",
    "S": "fc0 fd0 |ea0 |eb0 |ec0 fc1 fb1 eb1 fd1 |ec1 C0 B0 |eb1 |ea1 dW0 |ed1 yc0 yb0 db0 |da0 yd0 B1 C1 |db0 |dc0 |dd0 dW1 mp0 yb1 ya1 yc1 yd1 hd0 |da1 |db1 |dc1 mp1 rep0 hd1 nq Acol Rs0 Rs1 +fb0",
    "P": "lists1 lin1 Ea0 Eb0 Ec0 Kc0 keep1 U01 Ub0 Kb0 E01 Ua1 Deb1 Wc0 W0 Ec1 Eb1 Ea1 Ed1 Ub1 Kc1 F00 Kb1 Ddb0 Fa0 Wc1 W1 Fb0 Fc0 Fd0 F01 Ba0 Sl0 A0 Rb0 Bb0 Fa1 Fb1 Fc1 Ba1 A1 +lists0 +lin0 Rb1 Bb1 +keep0 Sl1 +U00 +Ua0 +Ac +E00",
}
OPT.update(SEL)
OWN, RELU, SOLO = (SEL.get(k, []) for k in ("own", "relu", "solo"))
CH.update(SEL.get("ch", {}))
BIG = float(2 ** 24)
LAND = "la lb lc ld le".split()
EXT = {"xt": [128, 4096], "wd": [128, 128], "pd": [128, 1024], "wt": [128, 1],
       "yw": [128, 128], "yp": [128, 1024], "yx": [128, 4096]}
SCRATCH = {}
PK = {}


def bufs(where, dtype, shape, names, pack=None, halves=False):
    for n in names.split():
        for m in ([n + "0", n + "1"] if halves else [n]):
            if pack is None:
                SCRATCH[m] = (where, shape, dtype)
            else:
                o = SCRATCH[pack][1][1] if pack in SCRATCH else 0
                PK[m] = (pack, o, shape[1])
                SCRATCH[pack] = (where, [128, o + (shape[1] + 15) // 16 * 16], dtype)


bufs("sbuf", "bfloat16", [128, 4096 + 32], "rec")
bufs("sbuf", "bfloat16", [128, 2048], "rec2")
bufs("sbuf", "float32", [128, 2048], "stock")
bufs("sbuf", "int32", [128, 1024], "pdi")
bufs("sbuf", "int32", [128, 128], "wdi")
bufs("sbuf", "int32", [128, 1], "wti")
bufs("sbuf", "bfloat16", [128, 144], "Z1 Z2 ZU N1 N2", "PB")
bufs("sbuf", "bfloat16", [128, 1024], "ohJ")
bufs("sbuf", "bfloat16", [128, 256], "tab")
bufs("sbuf", "float16", [128, 4, 16], "CK1 CK2 CKU C8k")
bufs("sbuf", "float32", [128, 4, 16], "CKa CKb")
bufs("sbuf", "int32", [128, 4, 16], "CKi CKj")
bufs("sbuf", "int32", [128, 128], "cD cM cT1 cT3", "PI")
bufs("sbuf", "int32", [128, 256], "tabi tabj", "PI")
bufs("sbuf", "int32", [128, 16], "oji ojk", "PI")
bufs("sbuf", "int32", [128, 8], "r31 r7 SI", "PI")
bufs("sbuf", "float32", [128, 8], "RC RD PD", "PF")
bufs("sbuf", "int32", [128, 1], "q0 q1", "PI")
bufs("sbuf", "float32", [128, 1], "g0 g1 f2", "PF")
bufs("sbuf", "uint16", [128, 8], "PERM", "PU")
bufs("sbuf", "uint16", [128, 8], "SU", "PU")
bufs("sbuf", "float32", [128, 1], "wcol Acol", "PF")
bufs("sbuf", "bfloat16", [128, 1], "nq", "PB")
bufs("sbuf", "float32", [128, 128], "ISh", "PF")
bufs("sbuf", "float32", [128, 64], "SMa SMi", "PF")
bufs("sbuf", "float16", [128, 128], "BO mI nI mS tA I3 I2 mF mG SmI BO3 BO2 onh nB I5 nI5 I2k", "PH")
bufs("sbuf", "float16", [128, 256], "CA CN", "PH")
bufs("sbuf", "bfloat16", [128, 32], "yes", "PB")
bufs("sbuf", "float16", [128, 8], "RS ng c48", "PH")
bufs("sbuf", "float16", [128, 128], "la lb lc ld snd", halves=True)
bufs("sbuf", "float32", [128, 64], "le nw", halves=True)
bufs("sbuf", "float16", [128, 64], "bj hq", "PH", True)
bufs("sbuf", "float16", [128, 128], "pr", "PH", True)
bufs("sbuf", "float32", [128, 64], "M dl dk Y hd ne", "PF", True)
bufs("sbuf", "float32", [128, 128], "X", "PF", True)
bufs("sbuf", "float32", [128, 256], "B", "PF", True)
bufs("sbuf", "int32", [128, 256], "X2", "PI", True)
bufs("sbuf", "int32", [128, 128], "Xi Xs MU", "PI", True)
bufs("sbuf", "int32", [128, 64], "nr m2 cd", "PI", True)
bufs("sbuf", "int32", [128, 2, 8], "cc")
bufs("sbuf", "int32", [128, 2, 12], "FI")
bufs("sbuf", "uint16", [128, 128], "lu", "PU", True)
bufs("sbuf", "uint16", [128, 16], "cu FU", "PU", True)
bufs("sbuf", "bfloat16", [128, 64], "mx hb yj", "PB", True)
bufs("sbuf", "bfloat16", [128, 128], "gp", "PB", True)
bufs("sbuf", "bfloat16", [128, 1024], "ab f e y d", halves=True)
bufs("sbuf", "float32", [128, 4, 16], "pv pw", halves=True)
bufs("sbuf", "float16", [128, 4, 16], "cb", halves=True)
bufs("psum", "float32", [128, 512], "pA pW", halves=True)
bufs("psum", "float32", [128, 4, 128], "pE", halves=True)
bufs("psum", "float32", [128, 512], "pC pD")
bufs("sbuf", "bfloat16", [128, 128], "bI nbI n2I", "PB")
A_ = slice(None)


def c(a, b, st=1):
    return slice(a, b, st)


def shift(name, s):
    o, w = PK[name][1:]
    a, b, st = s.indices(w)
    return slice(o + a, o + b, st)


def r(name, *ix, ind=None):
    if ind is not None:
        ind = (PK[ind[0]][0], shift(ind[0], ind[1]))
    if name in PK:
        return ("ref", PK[name][0], (shift(name, ix[0] if ix else A_),), ind)
    return ("ref", name, ix, ind)


def isref(x):
    return isinstance(x, tuple) and len(x) == 4 and x[0] == "ref"


def cols(name, ix):
    shape = (SCRATCH[name][1] if name in SCRATCH else EXT[name])[1:]
    x, stride = 1, 1
    for k in range(len(shape) - 1, -1, -1):
        s = ix[k] if k < len(ix) else A_
        q = [s] if isinstance(s, int) else range(*s.indices(shape[k]))
        x = (((1 << len(q)) - 1) << q[0]) if stride == 1 and len(q) > 1 and q[1] == q[0] + 1 else sum(x << (j * stride) for j in q)
        stride *= shape[k]
    return x


def size(ref):
    return bin(cols(ref[1], ref[2])).count("1")


def ap(T, ref):
    x = T[ref[1]][(A_,) + tuple(ref[2])]
    return x if ref[3] is None else x.indirect(T[ref[3][0]][:, ref[3][1]])


NODES = []
ACC = {}
BANK = {}
AT = {"visit": -1, "half": ""}
MODELS = [(0.86, 1.5, 3.7, 0, 0.42, 1200, 222, 222, 0, 222, 10, 600, 1.5, 222, 65, 0.5)]


def cost(eng, calls, model):
    cy, gam, sc, fix, pe = model[:5]
    t = 0.0
    for m, kw in calls:
        refs = [v for v in kw.values() if isref(v)]
        n = max(size(v) for v in refs if v[3] is None)
        dts = [SCRATCH[v[1]][2] for v in refs if size(v) > 1]
        if m == "matmul":
            t += max(64, size(kw["rhs"])) * pe * (4 if SCRATCH[kw["rhs"][1]][2] == "float32" else 1)
        elif eng == "G":
            t += 150 + 2 * cy * n
        elif kw["out"][3] is not None:
            t += 50 + sc * cy * n
        elif any(v[3] is not None for v in refs):
            t += (50 if eng == "V" else model[14]) + (model[12] if m == "tensor_tensor" else gam) * cy * n
        else:
            if m == "tensor_tensor" and SCRATCH[kw["in0"][1]][0] == SCRATCH[kw["in1"][1]][0]:
                n *= 2
            elif eng == "V" and m != "tensor_tensor" and all(d in ("bfloat16", "float16", "uint16") for d in dts):
                n *= model[15]
            t += (fix if eng == "V" else model[8]) + cy * max(n, 64)
    return t + (model[10] if eng == "P" else 0)


def add(eng, calls, tag, kind="comp", dur=None, extra=(), pre=()):
    n = len(NODES)
    preds, after = set(pre), set()
    touch = list(extra)
    for m, kw in calls:
        for k, v in kw.items():
            if isref(v):
                touch.append((v[1], cols(v[1], v[2]), k == "out"))
                if v[3] is not None:
                    touch.append((v[3][0], cols(v[3][0], (v[3][1],)), False))
    for name, x, w in touch:
        psum = name in SCRATCH and SCRATCH[name][0] == "psum"
        if psum and eng == "P":
            B = BANK.setdefault(name, [n])
            if n not in B:
                mid = not any(kw["start"] or kw["stop"] for m, kw in calls)
                after.update(B[:1] if mid else B)
                BANK[name] = B + [n] if mid else [n]
        keep = []
        for q in ACC.setdefault(name, []):
            m, me, a, mw = q
            if m != n and psum and (me != eng or eng == "P"):
                if me != eng:
                    preds.add(m)
                keep.append(q)
                continue
            if m != n and a & x and (w or mw):
                preds.add(m)
                if w and a & x == a:
                    continue
            keep.append(q)
        keep.append((n, eng, x, w))
        ACC[name] = keep[-40:] if psum else keep
    durs = [cost(eng, calls, M) if dur is None else M[5] if kind == "recv" else M[11] if kind == "send" else dur for M in MODELS]
    NODES.append({"eng": eng, "dur": durs, "calls": calls, "kind": kind, "preds": sorted(preds), "after": sorted(after - preds - {n}),
                  "key": tag + AT["half"], "visit": AT["visit"]})
    return n


def V(meth, tag, **kw):
    return add("V", [(meth, kw)], tag)


def S(out, in_, tag, func=AF.Copy, **kw):
    return add("S", [("activation", dict(out=out, in_=in_, func=func, **kw))], tag)


def P(calls, tag):
    return add("P", [("matmul", kw) for kw in calls], tag)


def I(out, pattern, base, cm, **kw):
    return add("G", [("iota", dict(out=out, pattern=pattern, base=base, channel_multiplier=cm, **kw))], "set")


def gcopy(out, in_, n):
    return add("G", [("affine_select", dict(out=out, in_=in_, pattern=[[0, n]], compare_op=Op.is_gt, fill=0.0, base=1,
                                            channel_multiplier=0))], "set")


def mm(out, lhsT, rhs, start=True, stop=True):
    return dict(out=out, lhsT=lhsT, rhs=rhs, start=start, stop=stop)


def ts(out, in0, s1, op0, s2=None, op1=None, tag="set"):
    kw = {} if op1 is None else {"op1": op1}
    return V("tensor_scalar", tag, out=out, in0=in0, scalar1=s1, scalar2=s2, op0=op0, **kw)


def tt(out, a, b, op, tag="set"):
    return V("tensor_tensor", tag, out=out, in0=a, in1=b, op=op)


def cp(out, in_, tag="set"):
    return V("tensor_copy", tag, out=out, in_=in_)


def ms(out, v):
    return V("memset", "set", out=out, value=v)


def scan(out, data0, data1, op0, op1, tag):
    return V("tensor_tensor_scan", tag, out=out, data0=data0, data1=data1, initial=0.0, op0=op0, op1=op1)


def dma(q, out, in_, dur, tag, pre=()):
    return add(q, [("dma_start", dict(out=out, in_=in_))], tag, kind="dma", dur=dur, pre=pre)


def sums(out, Z, src, o, e, stop):
    return [mm(out, r(Z, c(15 - k, 143 - k)), r(src, c(64 * k, 64 * k + 64)), False, stop and k == 15) for k in range(o // 4, e // 4)]


def piece(name, o, e):
    return r(name, c(16 * o, 16 * e))


def cuts(w):
    return [("abcdefgh"[k], sum(w[:k]), sum(w[:k + 1])) for k in range(len(w))]


def gathers(h, a, b, win):
    one, two, three = CH[a + h]
    for k, o, e in cuts(one):
        half = {"scale": 0.5} if a == "y" and b + k + h in SOLO else {}
        (cp if a + k + h in OWN else S)(piece(a + h, o, e), r("rec", win, ind=("lu" + h, c(o, e))), a + k, **half)
    for k, o, e in cuts(two):
        if b + k + h in SOLO:
            S(piece(b + h, o, e), r("rec", win, ind=("lu" + h, c(64 + o, 64 + e))), b + k)
        else:
            tt(piece(b + h, o, e), r("rec", win, ind=("lu" + h, c(64 + o, 64 + e))), piece(a + h, o, e), Op.subtract, b + k)
    for k, o, e in cuts(three):
        if b + k + h in SOLO:
            D = r("pD", c(0, 16 * (e - o)))
            P([mm(D, r("bI"), piece(b + h, o, e), True, False), mm(D, r("nbI" if a == "f" else "n2I"), piece(a + h, o, e), False, True)], "D" + b + k)
            S(piece("ab" + h, o, e), D, "|" + b + k, AF.Abs)
        elif b + k + h in RELU:
            ts(piece("ab" + h, o, e), piece(b + h, o, e), 0.0, Op.max, 2.0, Op.mult, "|" + b + k)
        else:
            S(piece("ab" + h, o, e), piece(b + h, o, e), "|" + b + k, AF.Abs)


def abs_sums(out, Z, N, h, a, b, tag):
    for k, o, e in cuts(CH[a + h][2]):
        if b + k + h in RELU:
            P(sums(out, N, b + h, o, e, False), tag + "n" + k)
    for k, o, e in cuts(CH[a + h][2]):
        P(sums(out, Z, "ab" + h, o, e, e == 64), tag + k)


AND, SAR, SLR = Op.bitwise_and, Op.arith_shift_right, Op.logical_shift_right
c4, c8, c12 = c(0, 4), c(4, 8), c(8, 12)
LAST = c(15, 64, 16)


def setup():
    x0 = dma("Y", r("wdi"), r("wd"), 2000, "load")
    dma("S", r("wti"), r("wt"), 2000, "load")
    dma("Y", r("rec", c(0, 2048)), r("xt", c(0, 2048)), 4300, "load")
    dma("S", r("rec", c(2048, 4096)), r("xt", c(2048, 4096)), 4300, "load")
    dma("Y", r("pdi"), r("pd"), 5800, "load")
    I(r("cD"), [[1, 128]], 0, -1)
    I(r("cM"), [[-16, 8], [0, 16]], 0, 1)
    ts(r("cT3"), r("cD"), 15, AND)
    ts(r("cT1"), r("cM"), 4, SLR)
    ts(r("BO"), r("cT1"), 0, Op.is_equal)
    ts(r("mI"), r("cD"), 0, Op.is_equal)
    ts(r("tA"), r("cT3"), 15, Op.is_equal)
    tt(r("mS"), r("tA"), r("BO"), Op.mult)
    for o, i, k in (("I3", "mI", 3232.0), ("I2", "mI", 2080.0), ("nI", "mI", -1.0),
                    ("BO3", "BO", 3232.0), ("BO2", "BO", 2080.0), ("nB", "mI", -1.0 if OPT["cb"] == "S" else -2.0),
                    ("I5", "mI", 512.0), ("nI5", "mI", -512.0)) + (("bI", "mI", 1.0), ("nbI", "mI", -1.0), ("n2I", "mI", -2.0)) * bool(SOLO):
        S(r(o), r(i), "set", scale=k)
    for k, (o, a, b, a2, b2) in enumerate((("mF", "I3", "mI", "I2", "mS"), ("mG", "I2", "mI", "I3", "mS"),
                                           ("SmI", "nI", "mI", "mI", "mS"), ("ISh", "mI", "mI", "mS", "nI"))):
        x = r(("pW0", "pW1")[k % 2], c(k // 2 * 128, k // 2 * 128 + 128))
        P([mm(x, r(a), r(b), True, False), mm(x, r(a2), r(b2), False, True)], "set")
        S(r(o), x, "set")
    for h in "01":
        ts(words(0, h), r("wdi", c(64 * int(h), 64 * int(h) + 64)), -2048.0, Op.add)
    ms(r("Z1"), 0.0)
    ts(r("Z1", c(15, 143, 16)), r("BO", c(0, 128, 16)), 2048.0, Op.mult)
    for o, k in (("Z2", 2.0),) + (("N1", -1.0), ("N2", -2.0)) * bool(RELU):
        S(r(o), r("Z1"), "set", scale=k)
    ts(r("wcol"), r("wti"), 1.0 / 2048, Op.mult)
    S(r("ZU"), r("Z1"), "set", scale=r("wcol"))
    ms(r("onh"), 1.0)
    ms(r("c48"), 48.0)
    for o in ("CA", "CN", "yes", "B0", "B1", "gp0", "gp1"):
        ms(r(o), 0.0)
    ms(r("CN", c(129, 256, 2)), 2048.0)
    ms(r("yes", c(1, 17, 15)), 1.0)
    ms(r("CA", c(0, 128, 2)), 2080.0)
    ms(r("CA", c(128, 256, 2)), 3232.0)
    I(r("CKi"), [[16, 4], [1, 16]], 0, 64)
    for o, pat, base in (("PD", [[64, 2], [4, 4]], 0), ("CKa", [[0, 4], [-4, 16]], 61 if OPT["cb"] == "S" else 62),
                         ("CKb", [[0, 4], [-2048, 16]], 15 * 2048), ("RD", [[0, 2], [512, 4]], 0)):
        I(r(o), pat, base, 0, allow_small_or_imprecise_dtypes=True)
    p64 = r("CKi", 0, c(0, 1))
    ts(r("q0"), p64, 192, AND)
    ts(r("q1"), p64, 8, SAR, 3, AND)
    ts(r("g0"), r("q0"), 0.25, Op.mult)
    cp(r("g1"), r("q1"))
    ts(r("PERM"), r("PD"), r("g0"), Op.add, r("g1"), Op.add)
    ts(r("CKj"), r("CKi"), 1023, AND)
    ts(r("CK2"), r("CKj"), 1024.0, Op.add)
    ts(r("f2"), r("CKj", 0, c(0, 1)), 0.5, Op.mult)
    S(r("CK1"), r("CKa"), "set")
    S(r("CKU"), r("CKb"), "set")
    S(r("RC"), r("RD"), "set", AF.Identity, bias=r("f2"))
    for hh in range(H):
        S(r("RS", c(4 * hh, 4 * hh + 4)), r("RC", c4), "set", scale=0.25, bias=512.0 - 512.0 * hh)
    for o, v in (("SMa", -BIG), ("SMi", BIG)):
        ms(r(o), 0.0)
        ms(r(o, c(0, 64, 16)), v)
    for q, (pat, base) in enumerate((([[1, 16], [1, 2], [0, 2]], 1), ([[1, 16], [1, 2], [0, 2]], 15), ([[1, 16], [1, 2], [256, 2]], 0),
                                     ([[1, 16], [0, 2], [0, 2]], 1) if OPT.get("nc") else ([[1, 16], [0, 2], [-256, 2]], 257))):
        I(r("tabi", c(64 * q, 64 * q + 64)), pat, base, 1)
    ts(r("tabj"), r("tabi"), 0x10F, AND)
    ts(r("tab"), r("tabj"), 0, Op.is_equal)
    I(r("oji"), [[1, 16]], 0, -1)
    ts(r("ojk"), r("oji"), 15, AND)
    ts(r("ohJ", c(0, 16)), r("ojk"), 0, Op.is_equal)
    for h in (0, 1):
        gcopy(r("stock", c(512 + 512 * h, 1024 + 512 * h)), r("pdi", c(512 * h, 512 * h + 512)), 512)
    for k in (16, 32, 64, 128, 256, 512):
        gcopy(r("ohJ", c(k, 2 * k)), r("ohJ", c(0, k)), k)


def words(t, h):
    return r(LAND[t] + h, c(1, 128, 2))


def offsets(t, h, tag, X):
    ts(r("Xs" + h), X, 5, SAR, 4095, AND, "s" + tag)
    if t == 0:
        cp(r("lu" + h), r("Xs" + h, ind=("PERM", A_)), "u" + tag)
    else:
        ts(r("lu" + h), r("Xs" + h, ind=("PERM", A_)), r("Acol"), Op.add, tag="u" + tag)


def front(t, hh):
    h = AT["half"] = str(hh)
    win = c(0, 4096 + 32 * (t > 0))
    al = words(t, h)
    pA, pW, pE, pv, cb = "pA" + h, "pW" + h, "pE" + h, "pv" + h, "cb" + h
    Wn = r(pE, 2, c(64, 128))
    AT["visit"] = t or -1
    P([mm(Wn, r("mS"), al)], "lists")
    P([mm(r(pA, c(64, 128)), r("mF"), al), mm(r(pA, c(128, 192)), r("mG"), al)], "lin")
    tt(r("M" + h), al, Wn, Op.mult, "M")
    tt(r("Xi" + h, c(0, 64)), r("M" + h), r(pA, c(64, 128)), Op.add, "Xf")
    tt(r("Xi" + h, c(64, 128)), r("M" + h), r(pA, c(128, 192)), Op.add, "Xg")
    offsets(t, h, "1", r("Xi" + h))
    AT["visit"] = t
    P([mm(r(pA, c(192, 256)), r("SmI"), al)], "keep")
    gathers(h, "f", "e", win)
    pU, E = r(pA, c(320, 384)), r(pE, 0, c(0, 64))
    P([mm(pU, r("I5"), r("CKU"), True, False)], "U0")
    for k, o, e in cuts([32, 32]):
        P(sums(pU, "ZU", "f" + h, o, e, e == 64), "U" + k)
    P([mm(E, r("mI"), r("CK1"), True, False)], "E0")
    abs_sums(E, "Z1", "N1", h, "f", "e", "E")
    pK = r(pW, c(384, 448))
    scan(r("MU" + h, c(0, 64)), r("SMa"), E, Op.add, Op.max, "max")
    cp(r(pv), E, "pv")
    ts(r("pw" + h), E, 100.0, Op.add, tag="pw")
    tt(r("ne" + h), r("MU" + h, c(0, 64)), E, Op.not_equal, "ne")
    P([mm(pK, r("mI"), r("CK1"), True, False)], "Kc")
    tt(r(cb, A_, c(1, 15)), r(pv, A_, c(0, 14)), r(pv, A_, c(2, 16)), Op.is_lt, "cb")
    tt(r(cb, A_, c(0, 16, 15)), r("pw" + h, A_, c(15, 13, -1)), r(pv, A_, c(1, None, -1)), Op.is_lt, "cw")
    P([mm(pK, r("nB"), r(cb), False, True)], "Kb")
    scan(r("MU" + h, c(64, 128)), r("ne" + h), pU, Op.mult, Op.max, "sel")
    ts(r("cc", hh, c8), r("MU" + h, c(79, 128, 16)), 1023, AND, tag="ccu")
    cp(r("cu" + h, c8), r("cc", hh, c8), "cuu")
    scan(r("cd" + h), r("ne" + h), pK, Op.mult, Op.max, "code")
    cp(r("cu" + h, c4), r("cd" + h, LAST), "cuk")
    for k, tag in ((0, "pb"), (64, "pa")):
        tt(r("pr" + h, c(k, k + 64)), r("tab", c(k, k + 64), ind=("cu" + h, c4)), al, Op.mult, tag)
    S(r("M" + h), r(pA, c(192, 256)), "dW")
    if OPT.get("nc"):
        tt(r("dk" + h), r("tab", c(192, 256), ind=("cu" + h, c4)), r("M" + h), Op.mult, "dk")
        S(r("mx" + h), r("tab", c(128, 192), ind=("cu" + h, c4)), "mp")
    if OPT.get("xs"):
        P([mm(r(pW, c(0, 256)), r("mI"), r("CA"), True, False)], "Wc")
        P([mm(r(pW, c(0, 256, 2)), r("BO"), r("pr" + h), False, False), mm(r(pW, c(1, 128, 2)), r("BO3"), r("pr" + h, c(0, 64)), False, False),
           mm(r(pW, c(129, 256, 2)), r("BO2"), r("pr" + h, c(64, 128)), False, True)], "W")
        for k, tag in ((1, "B"), (129, "C")):
            S(r("B" + h, c(k, k + 127, 2)), r("stock", c(512, 1536), ind=("cu" + h, c8)), tag, bias=-2048.0)
        scan(r("X2" + h), r("B" + h), r(pW, c(0, 256)), Op.mult, Op.add, "Xl")
        offsets(t, h, "3", r("X2" + h, c(1, 256, 2)))
        return
    P([mm(r(pW, c(0, 128)), r("mI"), r("CA", c(0, 256, 2)), True, False)], "Wc")
    P([mm(r(pW, c(0, 128)), r("BO"), r("pr" + h), False, True)], "W")
    P([mm(r(pE, 0, c(64, 128)), r("BO3"), r("pr" + h, c(0, 64))), mm(r(pE, 1, c(64, 128)), r("BO2"), r("pr" + h, c(64, 128)))], "L")
    B = r("B" + h, c(1, 128, 2))
    S(B, r("stock", c(512, 1536), ind=("cu" + h, c8)), "B", bias=-2048.0)
    tt(r("X" + h, c(0, 64)), B, r(pW, c(0, 64)), Op.mult, "Xy")
    tt(r("X" + h, c(64, 128)), B, r(pW, c(64, 128)), Op.mult, "Xz")
    tt(r("Xi" + h), r("X" + h), r(pE, c(0, 2), c(64, 128)), Op.add, "Xl")
    offsets(t, h, "3", r("Xi" + h))


def back(t, hh):
    h = AT["half"] = str(hh)
    end = t + 1 == NV
    al = words(t, h)
    pW = "pW" + h
    k2, ng = r(pW, c(448, 512)), c(4 * hh, 4 * hh + 4)
    P([mm(k2, r("mI"), r("CK2"), True, False)], "F0")
    abs_sums(k2, "Z2", "N2", h, "y", "d", "F")
    scan(r("m2" + h), r("SMi"), k2, Op.add, Op.min, "min")
    tt(r("ng", ng), r("m2" + h, LAST), r("MU" + h, LAST), Op.is_ge, "ng")
    ts(r("FI", hh, c4), r("m2" + h, LAST), 1023, AND, tag="J")
    cp(r("FU" + h, c(0, 8)), r("FI", hh, c(0, 8)), "FU")
    gp = r("gp" + h, c(1, 128, 2))
    if OPT.get("nc"):
        cp(r("FU" + h, c12), r("ng", ng), "FV")
        tt(r("dl" + h), r("yes", c(0, 16), ind=("FU" + h, c12)), r("dk" + h), Op.mult, "dl")
        tt(gp, r("yes", c(16, 32), ind=("FU" + h, c12)), r("mx" + h), Op.mult, "gp")
    else:
        tt(r("FI", hh, c12), r("cd" + h, LAST), r("ng", ng), Op.add, "co")
        cp(r("FU" + h, c12), r("FI", hh, c12), "FV")
        tt(r("dl" + h), r("tab", c(192, 256), ind=("FU" + h, c12)), r("M" + h), Op.mult, "dl")
        S(gp, r("tab", c(128, 192), ind=("FU" + h, c12)), "gp")
    if not end:
        P([mm(r("pC", c(0, 1)), r("onh"), r("ng", c(k, k + 1)), False, k == 7) for k in range(4 * hh, 4 * hh + 4)], "A")
    tt(r("bj" + h), r("ohJ", ind=("FU" + h, c4)), r("B" + h, c(1, 128, 2)), Op.mult, "bj")
    Q = "pE" + h
    P1, R = r(Q, 3, c(0, 128, 2)), r(Q, 3, c(1, 128, 2))
    P([mm(r(Q, 3), r("mI"), r("CN", c(128 * end, 128 * end + 128)), True, False), mm(P1, r("nI"), al, False, False),
       mm(R, r("mI"), al, False, False)], "Ba")
    P([mm(R, r("ISh"), r("dl" + h), False, False)], "Rb")
    P([mm(P1, r("BO"), r("bj" + h), False, True)], "Bb")
    if end:
        new = r("nw" + h)
        tt(r("Y" + h), gp, P1, Op.mult, "Y")
        tt(new, r("Y" + h), R, Op.add, "new")
    else:
        new = r("snd" + h)
        scan(new, r("gp" + h), r(Q, 3), Op.mult, Op.add, "new")
    sn = add("G", [("remote_dma", dict(to=LAND[t + 1] + h, in_=new))], "send", kind="send", dur=300)
    add("R", [], "recv", kind="recv", dur=0, pre=[sn], extra=[(LAND[t + 1] + h, cols(LAND[t + 1] + h, ()), True)])
    if not end:
        S(r("nw" + h), r("snd" + h, c(1, 128, 2)), "Rs", bias=2048.0)
    w = r("rec2", ind=("FU" + h, c8)) if end and hh == 0 else r("rec", c(2048 * hh, 2048 * hh + 2048), ind=("FU" + h, c8))
    if h in OPT["nr"]:
        S(r("hq" + h), r("d" + h, ind=("FU" + h, c4)), "hq", scale=0.5, bias=1535.75)
        S(r("yj" + h), r("y" + h, ind=("FU" + h, c4)), "yj")
        S(r("hb" + h), r("hq" + h), "hb", bias=-1536.0)
        tt(w, r("yj" + h), r("hb" + h), Op.add, "re" if end else "sr")
    else:
        if h in OPT.get("hd", ""):
            ts(r("hd" + h), r("d" + h, ind=("FU" + h, c4)), 0.5, Op.mult, -0.25, Op.add, "hd")
        else:
            S(r("hd" + h), r("d" + h, ind=("FU" + h, c4)), "hd", scale=0.5, bias=-0.25)
        tt(r("nr" + h), r("y" + h, ind=("FU" + h, c4)), r("hd" + h), Op.add, "nr")
        cp(w, r("nr" + h), "re" if end else "sr")
    if hh == 0 and not end:
        S(r("rec", c(4096, 4128)), r("rec", c(0, 32)), "rep")


def stock(t, hs):
    end = t + 1 == NV
    k = c(4 * hs[0], 4 * hs[-1] + 4)
    AT["half"] = str(hs[-1])
    pS = r("pC", c(8 + k.start, 8 + k.stop))
    P([mm(pS, r("mI"), r("RS", k), True, False)] + [
        mm(r("pC", c(8 + 4 * hh, 12 + 4 * hh)), r("I5" if hh else "nI5"), r("ng", c(4 * hh, 4 * hh + 4)), False, hh == hs[-1]) for hh in hs], "Sl")
    tt(r("SI", k), r("r7", k), pS, Op.add, "SI")
    cp(r("SU", k), r("SI", k), "SU")
    for hh in hs:
        h = AT["half"] = str(hh)
        w = r("stock", c(1024 * hh, 1024 * hh + 1024), ind=("SU", c(4 * hh, 4 * hh + 4)))
        cp(w, r("nw" + h), "se" if end else "ss")


def build():
    setup()
    for t in range(NV):
        end = t + 1 == NV
        AT["visit"], AT["half"] = t, ""
        if end:
            dma("Y", r("rec2"), r("rec", c(0, 2048)), 3500, "rec2")
        for hh in range(H):
            front(t, hh)
        for h in "01":
            AT["half"] = h
            gathers(h, "y", "d", c(0, 4096 + 32 * (t > 0)))
        AT["half"] = ""
        ts(r("r31"), r("cc", A_, c8), 31, AND, tag="r31")
        tt(r("FI", A_, c8), r("r31"), r("RC"), Op.add, "rl")
        ts(r("r7"), r("cc", A_, c8), 7, AND, tag="r7")
        if not end:
            P([mm(r("pC", c(0, 1)), r("onh"), r("c48", c(0, 1)), True, False)], "Ac")
        for hh in range(H):
            back(t, hh)
        AT["half"] = ""
        if not end and OPT.get("Av"):
            ts(r("nq"), r("pC", c(0, 1)), -1.0, Op.mult, 15.75, Op.add, "nq")
            tt(r("Acol"), r("pC", c(0, 1)), r("nq"), Op.add, "Acol")
        elif not end:
            S(r("nq"), r("pC", c(0, 1)), "nq", scale=-1.0, bias=15.75)
            S(r("Acol"), r("pC", c(0, 1)), "Acol", AF.Identity, bias=r("nq"))
        for hs in ([[0], [1]] if end else [[0, 1]]):
            stock(t, hs)
    for hh in range(H):
        h = AT["half"] = str(hh)
        dma("Y", r("yx", c(2048 * hh, 2048 * hh + 2048)), r("rec", c(2048, 4096)) if hh else r("rec2"), 2800, "yx")
        dma("Y", r("yp", c(512 * hh, 512 * hh + 512)), r("stock", c(512 + 512 * hh, 1024 + 512 * hh)), 2250, "yp")
        dma("Y", r("yw", c(64 * hh, 64 * hh + 64)), r("le" + h), 1200, "yw")


def busy(x, d):
    return 100.0 if x["kind"] == "dma" else 0.0 if x["kind"] == "recv" else d


def schedule():
    n = len(NODES)
    by = {(x["visit"], x["key"]): i for i, x in enumerate(NODES) if x["visit"] >= 0}
    for names in ORDER.values():
        line = [by.get((t + (k[0] == "+"), k.lstrip("+"))) for t in range(-1, NV) for k in names.split()]
        line = [i for i in line if i is not None]
        for a, b in zip(line, line[1:]):
            NODES[b]["after"].append(a)
    succ = [[] for _ in range(n)]
    for i, x in enumerate(NODES):
        for p in x["preds"] + x["after"]:
            succ[p].append(i)
    left = [len(x["preds"]) + len(x["after"]) for x in NODES]
    top, cnt = [i for i in range(n) if left[i] == 0], list(left)
    for i in top:
        for j in succ[i]:
            cnt[j] -= 1
            if cnt[j] == 0:
                top.append(j)
    way = [0.0] * n
    for i in reversed(top):
        way[i] = NODES[i]["dur"][0] + max([way[j] + 50.0 for j in succ[i]], default=0.0)
    w1, w2 = MODELS[0][6], {e: MODELS[0][{"P": 9, "S": 13}.get(e, 7)] for e in "VSPGYR"}
    rt = [0.0] * n
    ready, free, order = {}, {}, []
    for i in range(n):
        if left[i] == 0:
            ready.setdefault(NODES[i]["eng"], []).append(i)
    while len(order) < n:
        s, e = min((max(free.get(q, 0.0), min(rt[i] for i in L)), q) for q, L in ready.items() if L)
        i = max((i for i in ready[e] if rt[i] <= s + 60), key=lambda k: (way[k], -k))
        s = max(s, rt[i])
        ready[e].remove(i)
        x = NODES[i]
        free[e] = s + busy(x, x["dur"][0])
        x["t0"], x["t1"] = s, s + x["dur"][0]
        order.append(i)
        for j in succ[i]:
            left[j] -= 1
            rt[j] = max(rt[j], x["t1"] + (0.0 if i not in NODES[j]["preds"] else w1 if NODES[j]["eng"] == e else w2[e]))
            if left[j] == 0:
                ready.setdefault(NODES[j]["eng"], []).append(j)
    return order


def plan(order):
    cnt, know, comp, out, final = {}, {}, {}, [], {}
    for i in order:
        x = NODES[i]
        e, kind = x["eng"], x["kind"]
        K = know.setdefault(e, {})
        waits = []
        need = {}
        for p in (x["preds"] if kind != "recv" else []):
            sm, v = NODES[p]["tok"]
            if need.get(sm, (0, 0))[0] < v:
                need[sm] = (v, p)
        for sm, (v, p) in sorted(need.items(), key=lambda z: -NODES[z[1][1]]["t1"]):
            if K.get(sm, 0) < v:
                waits.append((sm, v))
                for a, b in NODES[p]["clk"].items():
                    K[a] = max(K.get(a, 0), b)
        clk = dict(K) if kind != "recv" else {}
        if kind == "comp":
            sm = "s" + e
            v = cnt[sm] = cnt.get(sm, 0) + 1
            for a, b in comp.get(e, {}).items():
                clk[a] = max(clk.get(a, 0), b)
            comp[e] = clk
        elif kind == "dma":
            sm, v = "d%d" % i, 16
        else:
            sm, v = "%s%d" % (x["key"], x["visit"]), 8
        clk[sm] = v
        x["tok"], x["clk"] = (sm, v), clk
        final[sm] = v
        out.append((i, waits))
    return out, final, know["G"]


build()
PLAN, FINAL, KNOWG = plan(schedule())
SEMAPHORES = list(FINAL)


def rank_program(g, core, T, topo):
    rank = T.rank_of(core)
    if rank is None:
        return
    n = len(T.cores)
    Q = {"V": g.vector, "S": g.scalar, "P": g.tensor, "G": g, "Y": g.sync}
    for i, waits in PLAN:
        x = NODES[i]
        if x["kind"] == "recv":
            continue
        q = Q[x["eng"]]
        for sm, v in waits:
            q.wait_ge(T.sem[sm], v)
        if x["kind"] == "send":
            t = x["visit"]
            dst = T.cores[(rank + (STEP if t + 1 < NV else -STEP * (NV - 1))) % n]
            kw = x["calls"][0][1]
            rid, pid = topo.addr(dst)[:2]
            g.remote_dma(out_ap=T[kw["to"]][:], in_ap=ap(T, kw["in_"]), remote_sem=T.sem[x["tok"][0].replace("send", "recv")],
                         local_sem=T.sem[x["tok"][0]], pid=pid, routing_id=rid,
                         dma_engine_mask=sum(1 << e for e in topo.engines(core, dst)[:8]))
            continue
        for m, kw in x["calls"]:
            kw = {a: (ap(T, b) if isref(b) else b) for a, b in kw.items()}
            if m == "memset":
                ins = q.memset(kw["out"], kw["value"])
            elif m == "dma_start":
                ins = q.dma_start(kw["out"], kw["in_"])
            elif m == "matmul":
                ins = q.matmul(kw["out"], kw["lhsT"], kw["rhs"], kw["start"], kw["stop"])
            elif m == "iota":
                ins = q.iota(kw.pop("out"), **kw)
            elif m == "affine_select":
                ins = q.affine_select(**kw)
            elif m == "activation":
                ins = q.activation(**kw)
            else:
                ins = {"tensor_copy": q.tensor_copy, "tensor_tensor": q.tensor_tensor, "tensor_scalar": q.tensor_scalar,
                       "tensor_tensor_scan": q.tensor_tensor_scan}[m](**kw)
        ins.then_inc(T.sem[x["tok"][0]], 16 if x["kind"] == "dma" else 1)
    for sm in SEMAPHORES:
        if KNOWG.get(sm, 0) < FINAL[sm]:
            g.wait_ge(T.sem[sm], FINAL[sm])
